import numpy as np
import ml_dtypes


def mxq(x, axis, fmt="e4m3"):
    dtype, down = {"e4m3": (ml_dtypes.float8_e4m3fn, 7), "e5m2": (ml_dtypes.float8_e5m2, 14)}[fmt]
    v = np.moveaxis(np.asarray(x, np.float32).astype(ml_dtypes.bfloat16).astype(np.float64), axis, -1)
    blocks = v.reshape(v.shape[:-1] + (-1, 32))
    amax = np.abs(blocks).max(-1, keepdims=True)
    byte = np.maximum(np.where(amax > 0, np.frexp(amax)[1] - 1 + 127, 0) - down, 1)
    scale = np.exp2(byte - 127.0)
    codes = (blocks / scale).astype(np.float32).astype(dtype).astype(np.float64)
    return np.moveaxis((codes * scale).reshape(v.shape), -1, axis)


WIDE = False


def mx_kscale(k):
    if not WIDE:
        return np.ones(k)
    levels = np.array([18, -18])
    if k % 512:
        return np.exp2(np.random.permutation(np.resize(levels, k // 32))).repeat(32)
    a = np.empty((k // 512, 16))
    for p in range(k // 512):
        a[p, :8] = np.random.permutation(np.resize(levels, 8))
        for g in range(8):
            far = levels[np.abs(levels - a[p, g]) >= 10]
            a[p, g + 8] = far[np.random.randint(len(far))]
    return np.exp2(a.ravel()).repeat(32)


def f64(x):
    return np.asarray(x).astype(np.float64)


def striped(idx):
    return np.tile(np.asarray(idx).reshape(-1, 16).T, (8, 1)).astype(np.uint16)


def unstriped(offs):
    return offs[:16].T.reshape(-1).astype(np.int64)


E2M1 = np.array([0.0, 0.5, 1.0, 1.5, 2.0, 3.0, 4.0, 6.0, -0.0, -0.5, -1.0, -1.5, -2.0, -3.0, -4.0, -6.0])


def pack_weight(w, fmt):
    k, n = w.shape
    w = f64(np.asarray(w, np.float32).astype(ml_dtypes.bfloat16)).reshape(k // 32, 32, n)
    amax = np.abs(w).max(1)
    if fmt == "e4m3":
        byte = np.frexp(amax)[1] - 1 + 127 - 7
    else:
        mant, ex = np.frexp(amax / 6.0)
        byte = np.where(mant > 0.5, ex, ex - 1) + 127
    byte = np.clip(np.where(amax > 0, byte, 1), 1, 254)
    scaled = (w * np.exp2(127.0 - byte)[:, None, :]).reshape(k, n).astype(np.float32)
    by_word = np.ascontiguousarray(scaled.reshape(k // 512, 128, 4, n).transpose(0, 1, 3, 2))
    if fmt == "e4m3":
        words = by_word.astype(ml_dtypes.float8_e4m3fn).view(np.uint8)
    else:
        c = by_word.astype(ml_dtypes.float4_e2m1fn).view(np.uint8) & 0xF
        words = (c[..., 0::2] | (c[..., 1::2] << 4)).reshape(k // 512, 128, 2 * n)
    return np.ascontiguousarray(words), np.ascontiguousarray(byte.astype(np.uint8).reshape(k // 512, 16, n))


def unpack_weight(words, scales, fmt):
    g, _, n = scales.shape
    words = np.ascontiguousarray(words).reshape(g, 128, n, -1)
    if fmt == "e4m3":
        vals = words.view(ml_dtypes.float8_e4m3fn).astype(np.float64)
    else:
        nib = np.empty((g, 128, n, 4), np.uint8)
        nib[..., 0::2] = words & 0xF
        nib[..., 1::2] = words >> 4
        vals = E2M1[nib]
    vals = vals * np.repeat(np.exp2(scales.astype(np.float64) - 127.0), 8, axis=1)[..., None]
    return vals.transpose(0, 1, 3, 2).reshape(g * 512, n)


B, N, T, D, R = 1, 512, 2048, 1024, 512


def setup_inputs():
    n = np.random.standard_normal
    idx = np.random.permutation(T)[:B * N]
    s = mx_kscale(D)[:, None]
    z = mx_kscale(R)[:, None]
    x = n((B, D, R))
    wp = pack_weight(n((D, T)) * (1.00 / np.sqrt(D)) / s, "e2m1")
    return {
        "xT": (x * s).astype(np.float32),
        "w_words": np.ascontiguousarray(wp[0].reshape(1, 2, 128, T, 2).transpose(0, 2, 3, 1, 4)).reshape(1, 128, T, 4),
        "w_scales": wp[1],
        "y": np.random.randint(0, 2, (B, R, N)).astype(np.float32),
        "wt": (np.random.uniform(0.5, 1.5, (B, R, 1)) * 1.0 / np.sqrt(R) * z).astype(np.float32),
        "xm": (x.transpose(0, 2, 1) / z).astype(np.float32),
        "offs": striped(idx),
    }


def reference(xT, w_words, w_scales, y, wt, xm, offs):
    idx = unstriped(offs)
    w = unpack_weight(w_words.reshape(1, 128, T, 2, 2).transpose(0, 3, 1, 2, 4).reshape(2, 128, 2 * T), w_scales, "e2m1")
    pick = lambda x: x[:, idx].reshape(x.shape[0], B, N).transpose(1, 0, 2)
    a = mxq(f64(xT), 1, "e4m3").transpose(0, 2, 1) @ pick(w)
    g = f64(wt) * (1.0 / (1.0 + np.exp(-a)) - f64(y))
    dw = mxq(f64(xm), 1, "e4m3").transpose(0, 2, 1) @ mxq(g, 1, "e5m2")
    gw = np.zeros((D, T))
    gw[:, idx] = dw.transpose(1, 0, 2).reshape(D, B * N)
    return gw

@@ -1,0 +1,201 @@
+from contextlib import ExitStack
+
+import concourse.mybir as mybir
+
+N, T, D, R = 512, 2048, 1024, 512
+FLOPS = 2 * 2 * N * D * R
+
+F32 = mybir.dt.float32
+BF16 = mybir.dt.bfloat16
+I32 = mybir.dt.int32
+U32 = mybir.dt.uint32
+U16 = mybir.dt.uint16
+U8 = mybir.dt.uint8
+E4M3 = mybir.dt.float8_e4m3fn_x4
+E5M2 = mybir.dt.float8_e5m2_x4
+E2M1 = mybir.dt.float4_e2m1fn_x4
+MULT = mybir.AluOpType.mult
+SUBTRACT = mybir.AluOpType.subtract
+SIGMOID = mybir.ActivationFunctionType.Sigmoid
+
+P = 128
+PACK = 4
+PASSES = D // (P * PACK)
+D_TILES = D // P
+WINDOWS = 3
+G_SCALAR_SHARE = 128
+XM_LOADS = ((0, 2), (2, 4), (4, 8))
+
+
+def tile_attend_gnce_w_kernel(tc, xT, w_words, w_scales, y, wt, xm, offs, out):
+    nc = tc.nc
+    with ExitStack() as ctx:
+        keep = ctx.enter_context(tc.tile_pool(name="keep", bufs=1))
+        ring = ctx.enter_context(tc.tile_pool(name="ring", bufs=3))
+        psum_a = ctx.enter_context(tc.psum_pool(name="psum_a", bufs=1))
+        psum_dw = ctx.enter_context(tc.psum_pool(name="psum_dw", bufs=4))
+
+        offsets = keep.tile([P, N // 16], U16, name="offsets")
+        table_words = keep.tile([P, T], I32, name="table_words", align_bytes=64)
+        table_scales = keep.tile([P, PASSES, T], U8, name="table_scales", align_bytes=64)
+        x_raw = [keep.tile([P, PACK, R], F32, name="x_raw%d" % o, align_bytes=64) for o in range(PASSES)]
+        y_raw = [keep.tile([P, 2, N], F32, name="y_raw%d" % h, align_bytes=64) for h in range(2)]
+        wt_sb = keep.tile([P, PACK], F32, name="wt_sb")
+        xm_raw = [keep.tile([P, PACK, (k1 - k0) * P], F32, name="xm_raw%d" % k0, align_bytes=64) for k0, k1 in XM_LOADS]
+        windows = [keep.tile([P, T], F32, name="window%d" % k, align_bytes=64) for k in range(WINDOWS)]
+
+        nc.vector.memset(table_scales[:].rearrange("p o t -> p (o t)").bitcast(I32), 0)
+        for window in windows:
+            nc.vector.memset(window[:], 0.0)
+
+        nc.sync.dma_start(offsets[:], offs)
+        nc.sync.dma_start(table_words[:], w_words[0].rearrange("p t b -> p (t b)").bitcast(I32))
+        for q in range(4):
+            nc.sync.dma_start(
+                table_scales[32 * q : 32 * q + 4, :, :].bitcast(I32),
+                w_scales[:, 4 * q : 4 * q + 4, :].rearrange("o f t -> f o t").bitcast(I32),
+            )
+        for o in range(PASSES):
+            nc.sync.dma_start(x_raw[o][:], xT[0, 512 * o : 512 * (o + 1), :].rearrange("(p j) r -> p j r", j=PACK))
+        nc.sync.dma_start(wt_sb[:], wt[0].rearrange("(p t) one -> p (t one)", t=PACK))
+        y_rows = y[0].rearrange("(p t) i -> p t i", t=PACK)
+        for h in range(2):
+            nc.sync.dma_start(y_raw[h][:], y_rows[:, 2 * h : 2 * h + 2, :])
+        xm_rows = xm[0].rearrange("(p j) d -> p j d", j=PACK)
+        for raw, (k0, k1) in zip(xm_raw, XM_LOADS):
+            nc.sync.dma_start(raw[:], xm_rows[:, :, k0 * P : k1 * P])
+
+        word_pairs = keep.tile([P, N], U32, name="word_pairs", align_bytes=64)
+        nc.vector.tensor_copy(word_pairs[:], table_words[:].bitcast(U32).indirect(offsets[:]))
+        w_plane = keep.tile([P, PASSES, N], U8, name="w_plane", align_bytes=64)
+        w_codes = keep.tile([P, PASSES, 2 * N], U8, name="w_codes", align_bytes=64)
+        nc.vector.tensor_copy(w_plane[:, 0, :], table_scales[:, 0, :].indirect(offsets[:]))
+        nc.vector.tensor_copy(
+            w_codes[:].bitcast(U16), word_pairs[:].bitcast(U16).rearrange("p (n o) -> p o n", o=PASSES)
+        )
+        nc.vector.tensor_copy(w_plane[:, 1, :], table_scales[:, 1, :].indirect(offsets[:]))
+
+        x_grouped = [keep.tile([P, PACK, P, PACK], BF16, name="x_grouped%d" % o, align_bytes=64) for o in range(PASSES)]
+        x_codes = [keep.tile([P, PACK, P], U32, name="x_codes%d" % o, align_bytes=64) for o in range(PASSES)]
+        x_plane = [keep.tile([P, PACK, P], U8, name="x_plane%d" % o, align_bytes=64) for o in range(PASSES)]
+
+        def round_x(copy, o, t0):
+            copy(
+                x_grouped[o][:, t0 : t0 + 2].rearrange("p t m j -> p m j t"),
+                x_raw[o][:].rearrange("p j (m t) -> p m j t", t=PACK)[:, :, :, t0 : t0 + 2],
+            )
+
+        def quantize_x(o, t0, t1):
+            nc.vector.quantize_mx(
+                out=x_codes[o][:, t0:t1, :].rearrange("p t m -> p (t m)").bitcast(E4M3),
+                scales=x_plane[o][:, t0:t1, :].rearrange("p t m -> p (t m)"),
+                in_=x_grouped[o][:, t0:t1].rearrange("p t m j -> p (t m j)"),
+            )
+
+        round_x(nc.scalar.copy, 0, 0)
+        round_x(nc.scalar.copy, 0, 2)
+        quantize_x(0, 0, 2)
+        round_x(nc.vector.tensor_copy, 1, 0)
+        round_x(nc.scalar.copy, 1, 2)
+        quantize_x(1, 0, 1)
+        quantize_x(1, 1, 2)
+        quantize_x(0, 2, 4)
+        quantize_x(1, 2, 4)
+
+        logits = [psum_a.tile([P, N], F32, name="logits%d" % t) for t in range(PACK)]
+        for o, t in ((0, 0), (0, 1), (1, 0), (1, 1), (0, 2), (1, 2), (0, 3), (1, 3)):
+            nc.tensor.matmul_mx(
+                out=logits[t][:],
+                lhsT=x_codes[o][:, t, :].bitcast(E4M3),
+                lhsT_scale=x_plane[o][:, t, :],
+                rhs=w_codes[:, o, :].bitcast(E2M1),
+                rhs_scale=w_plane[:, o, :],
+                start=(o == 0),
+                stop=(o == PASSES - 1),
+            )
+
+        g_rows = keep.tile([P, PACK, N], BF16, name="g_rows", align_bytes=64)
+        for t in range(PACK):
+            prob = keep.tile([P, N], F32, name="prob%d" % t, tag="prob%d" % t, align_bytes=64)
+            nc.scalar.activation(prob[:], logits[t][:], SIGMOID)
+            wy = keep.tile([P, N], F32, name="wy%d" % t, align_bytes=64)
+            nc.vector.tensor_scalar(wy[:], y_raw[t // 2][:, t % 2, :], wt_sb[:, t : t + 1], None, MULT)
+            nc.vector.scalar_tensor_tensor(g_rows[:, t, :], prob[:], wt_sb[:, t : t + 1], wy[:], MULT, SUBTRACT)
+
+        xm_codes = keep.tile([P, D], U32, name="xm_codes", align_bytes=64)
+        xm_plane = keep.tile([P, D], U8, name="xm_plane", align_bytes=64)
+        xm_grouped = {}
+
+        def grouped_tile(k0, k1, tag):
+            tile = keep.tile([P, (k1 - k0) * P, PACK], BF16, name="xm_grouped%d" % k0, tag=tag, align_bytes=64)
+            for k in range(k0, k1):
+                xm_grouped[k] = (tile, k0)
+
+        def round_xm(k):
+            half = max(h for h, (k0, k1) in enumerate(XM_LOADS) if k0 <= k)
+            d0 = (k - XM_LOADS[half][0]) * P
+            tile, base = xm_grouped[k]
+            nc.scalar.copy(
+                tile[:, (k - base) * P : (k - base + 1) * P, :].rearrange("p (c i) j -> p c j i", i=4),
+                xm_raw[half][:, :, d0 : d0 + P].rearrange("p j (c i) -> p c j i", i=4),
+            )
+
+        def quantize_xm(k0, k1):
+            cols = slice(k0 * P, k1 * P)
+            tile, base = xm_grouped[k0]
+            nc.vector.quantize_mx(
+                out=xm_codes[:, cols].bitcast(E4M3),
+                scales=xm_plane[:, cols],
+                in_=tile[:, (k0 - base) * P : (k1 - base) * P, :].rearrange("p d j -> p (d j)"),
+            )
+
+        grouped_tile(0, 1, "prob2")
+        round_xm(0)
+
+        g_grouped = keep.tile([P, N, PACK], BF16, name="g_grouped", align_bytes=64)
+        dst = g_grouped[:].rearrange("p (c i) t -> p c t i", i=4)
+        src = g_rows[:].rearrange("p t (c i) -> p c t i", i=4)
+        cut = G_SCALAR_SHARE // 4
+        nc.vector.tensor_copy(dst[:, cut:], src[:, cut:])
+        nc.scalar.copy(dst[:, :cut], src[:, :cut])
+        quantize_xm(0, 1)
+        g_codes = keep.tile([P, N], U32, name="g_codes", align_bytes=64)
+        g_plane = keep.tile([P, N], U8, name="g_plane", align_bytes=64)
+        nc.vector.quantize_mx(
+            out=g_codes[:].bitcast(E5M2), scales=g_plane[:], in_=g_grouped[:].rearrange("p i t -> p (i t)")
+        )
+
+        def product(k):
+            dw = psum_dw.tile([P, N], F32, name="dw")
+            nc.tensor.matmul_mx(
+                out=dw[:],
+                lhsT=xm_codes[:, k * P : (k + 1) * P].bitcast(E4M3),
+                lhsT_scale=xm_plane[:, k * P : (k + 1) * P],
+                rhs=g_codes[:].bitcast(E5M2),
+                rhs_scale=g_plane[:],
+                start=True,
+                stop=True,
+            )
+            if k == 0:
+                dw_sb = keep.tile([P, N], F32, name="dw_first", tag="dw_first", align_bytes=64)
+            else:
+                dw_sb = ring.tile([P, N], F32, name="dw_sb", align_bytes=64)
+            nc.scalar.copy(dw_sb[:], dw[:])
+            window = windows[k % WINDOWS]
+            nc.vector.tensor_copy(window[:].indirect(offsets[:]), dw_sb[:])
+            nc.sync.dma_start(out[k * P : (k + 1) * P, :], window[:])
+
+        grouped_tile(1, 4, "prob3")
+        round_xm(1)
+        quantize_xm(1, 2)
+        product(0)
+        round_xm(2)
+        round_xm(3)
+        quantize_xm(2, 4)
+        product(1)
+        grouped_tile(4, D_TILES, "dw_first")
+        for k in range(4, D_TILES):
+            round_xm(k)
+        quantize_xm(4, D_TILES)
+        for k in range(2, D_TILES):
+            product(k)

@@ -16,6 +16,7 @@ E5M2 = mybir.dt.float8_e5m2_x4
 E2M1 = mybir.dt.float4_e2m1fn_x4
 MULT = mybir.AluOpType.mult
 SUBTRACT = mybir.AluOpType.subtract
+COPY = mybir.ActivationFunctionType.Copy
 SIGMOID = mybir.ActivationFunctionType.Sigmoid
 
 P = 128
@@ -23,8 +24,8 @@ PACK = 4
 PASSES = D // (P * PACK)
 D_TILES = D // P
 WINDOWS = 3
-G_SCALAR_SHARE = 128
-XM_LOADS = ((0, 2), (2, 4), (4, 8))
+G_SCALAR_SHARE = 160
+XM_LOADS = ((0, 1), (1, 4), (4, 8))
 
 
 def tile_attend_gnce_w_kernel(tc, xT, w_words, w_scales, y, wt, xm, offs, out):
@@ -39,17 +40,22 @@ def tile_attend_gnce_w_kernel(tc, xT, w_words, w_scales, y, wt, xm, offs, out):
         table_words = keep.tile([P, T], I32, name="table_words", align_bytes=64)
         table_scales = keep.tile([P, PASSES, T], U8, name="table_scales", align_bytes=64)
         x_raw = [keep.tile([P, PACK, R], F32, name="x_raw%d" % o, align_bytes=64) for o in range(PASSES)]
-        y_raw = [keep.tile([P, 2, N], F32, name="y_raw%d" % h, align_bytes=64) for h in range(2)]
+        y_raw = [keep.tile([P, N], F32, name="y_raw%d" % t, tag="y_raw%d" % t, align_bytes=64) for t in range(PACK)]
         wt_sb = keep.tile([P, PACK], F32, name="wt_sb")
-        xm_raw = [keep.tile([P, PACK, (k1 - k0) * P], F32, name="xm_raw%d" % k0, align_bytes=64) for k0, k1 in XM_LOADS]
+        xm_raw = [keep.tile([P, PACK, (k1 - k0) * P], F32, name="xm_raw%d" % k0, tag="xm_raw%d" % k0, align_bytes=64) for k0, k1 in XM_LOADS]
         windows = [keep.tile([P, T], F32, name="window%d" % k, align_bytes=64) for k in range(WINDOWS)]
 
-        nc.vector.memset(table_scales[:].rearrange("p o t -> p (o t)").bitcast(I32), 0)
-        for window in windows:
-            nc.vector.memset(window[:], 0.0)
+        warm_in = keep.tile([P, 1], F32, name="warm_in")
+        warm_out = keep.tile([P, 1], F32, name="warm_out")
+        nc.vector.memset(warm_in[:], 0.0)
+        nc.scalar.activation(warm_out[:], warm_in[:], SIGMOID)
+        nc.gpsimd.memset(table_scales[:].rearrange("p o t -> p (o t)").bitcast(I32), 0)
+        nc.vector.memset(windows[0][:], 0.0)
+        for window in windows[1:]:
+            nc.gpsimd.memset(window[:], 0.0)
 
-        nc.sync.dma_start(offsets[:], offs)
         nc.sync.dma_start(table_words[:], w_words[0].rearrange("p t b -> p (t b)").bitcast(I32))
+        nc.sync.dma_start(offsets[:], offs)
         for q in range(4):
             nc.sync.dma_start(
                 table_scales[32 * q : 32 * q + 4, :, :].bitcast(I32),
@@ -59,8 +65,8 @@ def tile_attend_gnce_w_kernel(tc, xT, w_words, w_scales, y, wt, xm, offs, out):
             nc.sync.dma_start(x_raw[o][:], xT[0, 512 * o : 512 * (o + 1), :].rearrange("(p j) r -> p j r", j=PACK))
         nc.sync.dma_start(wt_sb[:], wt[0].rearrange("(p t) one -> p (t one)", t=PACK))
         y_rows = y[0].rearrange("(p t) i -> p t i", t=PACK)
-        for h in range(2):
-            nc.sync.dma_start(y_raw[h][:], y_rows[:, 2 * h : 2 * h + 2, :])
+        for t in range(PACK):
+            nc.sync.dma_start(y_raw[t][:], y_rows[:, t, :])
         xm_rows = xm[0].rearrange("(p j) d -> p j d", j=PACK)
         for raw, (k0, k1) in zip(xm_raw, XM_LOADS):
             nc.sync.dma_start(raw[:], xm_rows[:, :, k0 * P : k1 * P])
@@ -69,44 +75,52 @@ def tile_attend_gnce_w_kernel(tc, xT, w_words, w_scales, y, wt, xm, offs, out):
         nc.vector.tensor_copy(word_pairs[:], table_words[:].bitcast(U32).indirect(offsets[:]))
         w_plane = keep.tile([P, PASSES, N], U8, name="w_plane", align_bytes=64)
         w_codes = keep.tile([P, PASSES, 2 * N], U8, name="w_codes", align_bytes=64)
-        nc.vector.tensor_copy(w_plane[:, 0, :], table_scales[:, 0, :].indirect(offsets[:]))
+        for o in range(PASSES):
+            nc.vector.tensor_copy(w_plane[:, o, :], table_scales[:, o, :].indirect(offsets[:]))
         nc.vector.tensor_copy(
             w_codes[:].bitcast(U16), word_pairs[:].bitcast(U16).rearrange("p (n o) -> p o n", o=PASSES)
         )
-        nc.vector.tensor_copy(w_plane[:, 1, :], table_scales[:, 1, :].indirect(offsets[:]))
 
-        x_grouped = [keep.tile([P, PACK, P, PACK], BF16, name="x_grouped%d" % o, align_bytes=64) for o in range(PASSES)]
-        x_codes = [keep.tile([P, PACK, P], U32, name="x_codes%d" % o, align_bytes=64) for o in range(PASSES)]
+        x_grouped = {}
+        x_codes = {}
         x_plane = [keep.tile([P, PACK, P], U8, name="x_plane%d" % o, align_bytes=64) for o in range(PASSES)]
 
-        def round_x(copy, o, t0):
+        def round_x(copy, o, t0, tag):
+            x_grouped[o, t0 // 2] = keep.tile([P, 2, P, PACK], BF16, name=tag, tag=tag, align_bytes=64)
             copy(
-                x_grouped[o][:, t0 : t0 + 2].rearrange("p t m j -> p m j t"),
+                x_grouped[o, t0 // 2][:].rearrange("p t m j -> p m j t"),
                 x_raw[o][:].rearrange("p j (m t) -> p m j t", t=PACK)[:, :, :, t0 : t0 + 2],
             )
 
+        def codes_tile(o, pair, tag):
+            x_codes[o, pair] = keep.tile([P, 2, P], U32, name="x_codes%d%d" % (o, pair), tag=tag, align_bytes=64)
+
         def quantize_x(o, t0, t1):
             nc.vector.quantize_mx(
-                out=x_codes[o][:, t0:t1, :].rearrange("p t m -> p (t m)").bitcast(E4M3),
+                out=x_codes[o, t0 // 2][:, t0 % 2 : t0 % 2 + t1 - t0, :].rearrange("p t m -> p (t m)").bitcast(E4M3),
                 scales=x_plane[o][:, t0:t1, :].rearrange("p t m -> p (t m)"),
-                in_=x_grouped[o][:, t0:t1].rearrange("p t m j -> p (t m j)"),
+                in_=x_grouped[o, t0 // 2][:, t0 % 2 : t0 % 2 + t1 - t0].rearrange("p t m j -> p (t m j)"),
             )
 
-        round_x(nc.scalar.copy, 0, 0)
-        round_x(nc.scalar.copy, 0, 2)
+        round_x(nc.scalar.copy, 0, 0, "x_low")
+        round_x(nc.scalar.copy, 0, 2, "x_high0")
+        codes_tile(0, 0, "x_codes_low0")
         quantize_x(0, 0, 2)
-        round_x(nc.vector.tensor_copy, 1, 0)
-        round_x(nc.scalar.copy, 1, 2)
+        round_x(nc.vector.tensor_copy, 1, 0, "x_low")
+        round_x(nc.scalar.copy, 1, 2, "x_high1")
+        codes_tile(1, 0, "x_codes_low1")
         quantize_x(1, 0, 1)
         quantize_x(1, 1, 2)
+        codes_tile(0, 1, "x_low")
         quantize_x(0, 2, 4)
+        codes_tile(1, 1, "x_codes_high1")
         quantize_x(1, 2, 4)
 
         logits = [psum_a.tile([P, N], F32, name="logits%d" % t) for t in range(PACK)]
         for o, t in ((0, 0), (0, 1), (1, 0), (1, 1), (0, 2), (1, 2), (0, 3), (1, 3)):
             nc.tensor.matmul_mx(
                 out=logits[t][:],
-                lhsT=x_codes[o][:, t, :].bitcast(E4M3),
+                lhsT=x_codes[o, t // 2][:, t % 2, :].bitcast(E4M3),
                 lhsT_scale=x_plane[o][:, t, :],
                 rhs=w_codes[:, o, :].bitcast(E2M1),
                 rhs_scale=w_plane[:, o, :],
@@ -114,13 +128,15 @@ def tile_attend_gnce_w_kernel(tc, xT, w_words, w_scales, y, wt, xm, offs, out):
                 stop=(o == PASSES - 1),
             )
 
-        g_rows = keep.tile([P, PACK, N], BF16, name="g_rows", align_bytes=64)
+        wy = [keep.tile([P, N], F32, name="wy%d" % t, tag="wy%d" % t, align_bytes=64) for t in range(PACK)]
+        nc.scalar.activation(wy[0][:], y_raw[0][:], COPY, scale=wt_sb[:, 0:1])
+        for t in range(1, PACK):
+            nc.vector.tensor_scalar(wy[t][:], y_raw[t][:], wt_sb[:, t : t + 1], None, MULT)
+        g_rows = keep.tile([P, PACK, N], BF16, name="g_rows", tag="y_raw3", align_bytes=64)
+        prob = keep.tile([P, PACK, N], F32, name="prob", tag="y_raw0", align_bytes=64)
         for t in range(PACK):
-            prob = keep.tile([P, N], F32, name="prob%d" % t, tag="prob%d" % t, align_bytes=64)
-            nc.scalar.activation(prob[:], logits[t][:], SIGMOID)
-            wy = keep.tile([P, N], F32, name="wy%d" % t, align_bytes=64)
-            nc.vector.tensor_scalar(wy[:], y_raw[t // 2][:, t % 2, :], wt_sb[:, t : t + 1], None, MULT)
-            nc.vector.scalar_tensor_tensor(g_rows[:, t, :], prob[:], wt_sb[:, t : t + 1], wy[:], MULT, SUBTRACT)
+            nc.scalar.activation(prob[:, t, :], logits[t][:], SIGMOID)
+            nc.vector.scalar_tensor_tensor(g_rows[:, t, :], prob[:, t, :], wt_sb[:, t : t + 1], wy[t][:], MULT, SUBTRACT)
 
         xm_codes = keep.tile([P, D], U32, name="xm_codes", align_bytes=64)
         xm_plane = keep.tile([P, D], U8, name="xm_plane", align_bytes=64)
@@ -149,10 +165,10 @@ def tile_attend_gnce_w_kernel(tc, xT, w_words, w_scales, y, wt, xm, offs, out):
                 in_=tile[:, (k0 - base) * P : (k1 - base) * P, :].rearrange("p d j -> p (d j)"),
             )
 
-        grouped_tile(0, 1, "prob2")
+        grouped_tile(0, 1, "wy2")
         round_xm(0)
 
-        g_grouped = keep.tile([P, N, PACK], BF16, name="g_grouped", align_bytes=64)
+        g_grouped = keep.tile([P, N, PACK], BF16, name="g_grouped", tag="xm_raw0", align_bytes=64)
         dst = g_grouped[:].rearrange("p (c i) t -> p c t i", i=4)
         src = g_rows[:].rearrange("p t (c i) -> p c t i", i=4)
         cut = G_SCALAR_SHARE // 4
@@ -161,9 +177,12 @@ def tile_attend_gnce_w_kernel(tc, xT, w_words, w_scales, y, wt, xm, offs, out):
         quantize_xm(0, 1)
         g_codes = keep.tile([P, N], U32, name="g_codes", align_bytes=64)
         g_plane = keep.tile([P, N], U8, name="g_plane", align_bytes=64)
-        nc.vector.quantize_mx(
-            out=g_codes[:].bitcast(E5M2), scales=g_plane[:], in_=g_grouped[:].rearrange("p i t -> p (i t)")
-        )
+        for cols in (slice(N // 2, N), slice(0, N // 2)):
+            nc.vector.quantize_mx(
+                out=g_codes[:, cols].bitcast(E5M2),
+                scales=g_plane[:, cols],
+                in_=g_grouped[:, cols, :].rearrange("p i t -> p (i t)"),
+            )
 
         def product(k):
             dw = psum_dw.tile([P, N], F32, name="dw")
@@ -177,25 +196,31 @@ def tile_attend_gnce_w_kernel(tc, xT, w_words, w_scales, y, wt, xm, offs, out):
                 stop=True,
             )
             if k == 0:
-                dw_sb = keep.tile([P, N], F32, name="dw_first", tag="dw_first", align_bytes=64)
+                dw_sb = keep.tile([P, N], F32, name="dw_first", tag="xm_raw1", align_bytes=64)
             else:
                 dw_sb = ring.tile([P, N], F32, name="dw_sb", align_bytes=64)
-            nc.scalar.copy(dw_sb[:], dw[:])
             window = windows[k % WINDOWS]
-            nc.vector.tensor_copy(window[:].indirect(offsets[:]), dw_sb[:])
+            pieces = 2 if k == 0 else 1
+            width = N // pieces
+            for c in range(pieces):
+                cols = slice(c * width, (c + 1) * width)
+                nc.scalar.copy(dw_sb[:, cols], dw[:, cols])
+                entries = offsets[:, c * width // 16 : (c + 1) * width // 16]
+                nc.vector.tensor_copy(window[:].indirect(entries), dw_sb[:, cols])
             nc.sync.dma_start(out[k * P : (k + 1) * P, :], window[:])
 
-        grouped_tile(1, 4, "prob3")
+        grouped_tile(1, 4, "wy3")
         round_xm(1)
-        quantize_xm(1, 2)
-        product(0)
         round_xm(2)
         round_xm(3)
+        quantize_xm(1, 2)
         quantize_xm(2, 4)
-        product(1)
-        grouped_tile(4, D_TILES, "dw_first")
+        product(0)
+        for k in range(1, 4):
+            product(k)
+        grouped_tile(4, D_TILES, "xm_raw1")
         for k in range(4, D_TILES):
             round_xm(k)
         quantize_xm(4, D_TILES)
-        for k in range(2, D_TILES):
+        for k in range(4, D_TILES):
             product(k)

@@ -49,17 +49,16 @@ def tile_attend_gnce_w_kernel(tc, xT, w_words, w_scales, y, wt, xm, offs, out):
         warm_out = keep.tile([P, 1], F32, name="warm_out")
         nc.vector.memset(warm_in[:], 0.0)
         nc.scalar.activation(warm_out[:], warm_in[:], SIGMOID)
-        nc.gpsimd.memset(table_scales[:].rearrange("p o t -> p (o t)").bitcast(I32), 0)
-        nc.vector.memset(windows[0][:], 0.0)
-        for window in windows[1:]:
-            nc.gpsimd.memset(window[:], 0.0)
+        nc.vector.memset(table_scales[:].rearrange("p o t -> p (o t)").bitcast(I32), 0)
+        for window in windows:
+            nc.vector.memset(window[:], 0.0)
 
         nc.sync.dma_start(table_words[:], w_words[0].rearrange("p t b -> p (t b)").bitcast(I32))
         nc.sync.dma_start(offsets[:], offs)
-        for q in range(4):
+        for r in range(4):
             nc.sync.dma_start(
-                table_scales[32 * q : 32 * q + 4, :, :].bitcast(I32),
-                w_scales[:, 4 * q : 4 * q + 4, :].rearrange("o f t -> f o t").bitcast(I32),
+                table_scales[r:P:32, :, :].bitcast(I32),
+                w_scales[:, r:16:4, :].rearrange("o q t -> q o t").bitcast(I32),
             )
         for o in range(PASSES):
             nc.sync.dma_start(x_raw[o][:], xT[0, 512 * o : 512 * (o + 1), :].rearrange("(p j) r -> p j r", j=PACK))

@@ -25,7 +25,7 @@ PASSES = D // (P * PACK)
 D_TILES = D // P
 WINDOWS = 3
 G_SCALAR_SHARE = 160
-XM_LOADS = ((0, 1), (1, 4), (4, 8))
+XM_LOADS = ((0, 1), (1, 2), (2, 4), (4, 8))
 
 
 def tile_attend_gnce_w_kernel(tc, xT, w_words, w_scales, y, wt, xm, offs, out):
@@ -38,7 +38,7 @@ def tile_attend_gnce_w_kernel(tc, xT, w_words, w_scales, y, wt, xm, offs, out):
 
         offsets = keep.tile([P, N // 16], U16, name="offsets")
         table_words = keep.tile([P, T], I32, name="table_words", align_bytes=64)
-        table_scales = keep.tile([P, PASSES, T], U8, name="table_scales", align_bytes=64)
+        table_scales = keep.tile([P, PASSES, T], U8, name="table_scales", tag="table_scales", align_bytes=64)
         x_raw = [keep.tile([P, PACK, R], F32, name="x_raw%d" % o, align_bytes=64) for o in range(PASSES)]
         y_raw = [keep.tile([P, N], F32, name="y_raw%d" % t, tag="y_raw%d" % t, align_bytes=64) for t in range(PACK)]
         wt_sb = keep.tile([P, PACK], F32, name="wt_sb")
@@ -47,22 +47,25 @@ def tile_attend_gnce_w_kernel(tc, xT, w_words, w_scales, y, wt, xm, offs, out):
 
         warm_in = keep.tile([P, 1], F32, name="warm_in")
         warm_out = keep.tile([P, 1], F32, name="warm_out")
-        nc.vector.memset(warm_in[:], 0.0)
+        nc.gpsimd.memset(warm_in[:], 0.0)
         nc.scalar.activation(warm_out[:], warm_in[:], SIGMOID)
         nc.vector.memset(table_scales[:].rearrange("p o t -> p (o t)").bitcast(I32), 0)
         for window in windows:
             nc.vector.memset(window[:], 0.0)
 
-        nc.sync.dma_start(table_words[:], w_words[0].rearrange("p t b -> p (t b)").bitcast(I32))
+        def load_x(o):
+            nc.sync.dma_start(x_raw[o][:], xT[0, 512 * o : 512 * (o + 1), :].rearrange("(p j) r -> p j r", j=PACK))
+
+        load_x(0)
         nc.sync.dma_start(offsets[:], offs)
+        nc.sync.dma_start(wt_sb[:], wt[0].rearrange("(p t) one -> p (t one)", t=PACK))
         for r in range(4):
             nc.sync.dma_start(
                 table_scales[r:P:32, :, :].bitcast(I32),
                 w_scales[:, r:16:4, :].rearrange("o q t -> q o t").bitcast(I32),
             )
-        for o in range(PASSES):
-            nc.sync.dma_start(x_raw[o][:], xT[0, 512 * o : 512 * (o + 1), :].rearrange("(p j) r -> p j r", j=PACK))
-        nc.sync.dma_start(wt_sb[:], wt[0].rearrange("(p t) one -> p (t one)", t=PACK))
+        nc.sync.dma_start(table_words[:], w_words[0].rearrange("p t b -> p (t b)").bitcast(I32))
+        load_x(1)
         y_rows = y[0].rearrange("(p t) i -> p t i", t=PACK)
         for t in range(PACK):
             nc.sync.dma_start(y_raw[t][:], y_rows[:, t, :])
@@ -71,14 +74,14 @@ def tile_attend_gnce_w_kernel(tc, xT, w_words, w_scales, y, wt, xm, offs, out):
             nc.sync.dma_start(raw[:], xm_rows[:, :, k0 * P : k1 * P])
 
         word_pairs = keep.tile([P, N], U32, name="word_pairs", align_bytes=64)
-        nc.vector.tensor_copy(word_pairs[:], table_words[:].bitcast(U32).indirect(offsets[:]))
-        w_plane = keep.tile([P, PASSES, N], U8, name="w_plane", align_bytes=64)
-        w_codes = keep.tile([P, PASSES, 2 * N], U8, name="w_codes", align_bytes=64)
-        for o in range(PASSES):
-            nc.vector.tensor_copy(w_plane[:, o, :], table_scales[:, o, :].indirect(offsets[:]))
-        nc.vector.tensor_copy(
-            w_codes[:].bitcast(U16), word_pairs[:].bitcast(U16).rearrange("p (n o) -> p o n", o=PASSES)
-        )
+        w_plane = [keep.tile([P, N], U8, name="w_plane%d" % o, align_bytes=64) for o in range(PASSES)]
+        w_codes = [keep.tile([P, 2 * N], U8, name="w_codes%d" % o, align_bytes=64) for o in range(PASSES)]
+
+        def gather_scales(o):
+            nc.vector.tensor_copy(w_plane[o][:], table_scales[:, o, :].indirect(offsets[:]))
+
+        def part_words(o):
+            nc.vector.tensor_copy(w_codes[o][:].bitcast(U16), word_pairs[:].bitcast(U16)[:, o : 2 * N : PASSES])
 
         x_grouped = {}
         x_codes = {}
@@ -101,18 +104,23 @@ def tile_attend_gnce_w_kernel(tc, xT, w_words, w_scales, y, wt, xm, offs, out):
                 in_=x_grouped[o, t0 // 2][:, t0 % 2 : t0 % 2 + t1 - t0].rearrange("p t m j -> p (t m j)"),
             )
 
-        round_x(nc.scalar.copy, 0, 0, "x_low")
+        round_x(nc.scalar.copy, 0, 0, "x_low0")
         round_x(nc.scalar.copy, 0, 2, "x_high0")
-        codes_tile(0, 0, "x_codes_low0")
+        gather_scales(0)
+        gather_scales(1)
+        codes_tile(0, 0, "table_scales")
         quantize_x(0, 0, 2)
-        round_x(nc.vector.tensor_copy, 1, 0, "x_low")
+        nc.vector.tensor_copy(word_pairs[:], table_words[:].bitcast(U32).indirect(offsets[:]))
+        part_words(0)
+        part_words(1)
+        round_x(nc.vector.tensor_copy, 1, 0, "x_low1")
         round_x(nc.scalar.copy, 1, 2, "x_high1")
-        codes_tile(1, 0, "x_codes_low1")
+        codes_tile(1, 0, "x_codes10")
         quantize_x(1, 0, 1)
         quantize_x(1, 1, 2)
-        codes_tile(0, 1, "x_low")
+        codes_tile(0, 1, "x_low1")
         quantize_x(0, 2, 4)
-        codes_tile(1, 1, "x_codes_high1")
+        codes_tile(1, 1, "x_codes11")
         quantize_x(1, 2, 4)
 
         logits = [psum_a.tile([P, N], F32, name="logits%d" % t) for t in range(PACK)]
@@ -121,8 +129,8 @@ def tile_attend_gnce_w_kernel(tc, xT, w_words, w_scales, y, wt, xm, offs, out):
                 out=logits[t][:],
                 lhsT=x_codes[o, t // 2][:, t % 2, :].bitcast(E4M3),
                 lhsT_scale=x_plane[o][:, t, :],
-                rhs=w_codes[:, o, :].bitcast(E2M1),
-                rhs_scale=w_plane[:, o, :],
+                rhs=w_codes[o][:].bitcast(E2M1),
+                rhs_scale=w_plane[o][:],
                 start=(o == 0),
                 stop=(o == PASSES - 1),
             )
@@ -137,43 +145,41 @@ def tile_attend_gnce_w_kernel(tc, xT, w_words, w_scales, y, wt, xm, offs, out):
             nc.scalar.activation(prob[:, t, :], logits[t][:], SIGMOID)
             nc.vector.scalar_tensor_tensor(g_rows[:, t, :], prob[:, t, :], wt_sb[:, t : t + 1], wy[t][:], MULT, SUBTRACT)
 
-        xm_codes = keep.tile([P, D], U32, name="xm_codes", align_bytes=64)
-        xm_plane = keep.tile([P, D], U8, name="xm_plane", align_bytes=64)
+        xm_codes = {}
+        xm_plane = {}
         xm_grouped = {}
 
-        def grouped_tile(k0, k1, tag):
-            tile = keep.tile([P, (k1 - k0) * P, PACK], BF16, name="xm_grouped%d" % k0, tag=tag, align_bytes=64)
-            for k in range(k0, k1):
-                xm_grouped[k] = (tile, k0)
+        def round_xm(load, tag):
+            k0, k1 = XM_LOADS[load]
+            xm_grouped[load] = keep.tile([P, (k1 - k0) * P, PACK], BF16, name="xm_grouped%d" % k0, tag=tag, align_bytes=64)
+            for d0 in range(0, (k1 - k0) * P, P):
+                nc.scalar.copy(
+                    xm_grouped[load][:, d0 : d0 + P, :].rearrange("p (c i) j -> p c j i", i=4),
+                    xm_raw[load][:, :, d0 : d0 + P].rearrange("p j (c i) -> p c j i", i=4),
+                )
 
-        def round_xm(k):
-            half = max(h for h, (k0, k1) in enumerate(XM_LOADS) if k0 <= k)
-            d0 = (k - XM_LOADS[half][0]) * P
-            tile, base = xm_grouped[k]
-            nc.scalar.copy(
-                tile[:, (k - base) * P : (k - base + 1) * P, :].rearrange("p (c i) j -> p c j i", i=4),
-                xm_raw[half][:, :, d0 : d0 + P].rearrange("p j (c i) -> p c j i", i=4),
-            )
-
-        def quantize_xm(k0, k1):
-            cols = slice(k0 * P, k1 * P)
-            tile, base = xm_grouped[k0]
+        def quantize_xm(load):
+            k0, k1 = XM_LOADS[load]
+            codes = keep.tile([P, (k1 - k0) * P], U32, name="xm_codes%d" % k0, tag="xm_codes%d" % k0, align_bytes=64)
+            plane = keep.tile([P, (k1 - k0) * P], U8, name="xm_plane%d" % k0, align_bytes=64)
             nc.vector.quantize_mx(
-                out=xm_codes[:, cols].bitcast(E4M3),
-                scales=xm_plane[:, cols],
-                in_=tile[:, (k0 - base) * P : (k1 - base) * P, :].rearrange("p d j -> p (d j)"),
+                out=codes[:].bitcast(E4M3),
+                scales=plane[:],
+                in_=xm_grouped[load][:].rearrange("p d j -> p (d j)"),
             )
+            for k in range(k0, k1):
+                xm_codes[k] = codes[:, (k - k0) * P : (k - k0 + 1) * P]
+                xm_plane[k] = plane[:, (k - k0) * P : (k - k0 + 1) * P]
 
-        grouped_tile(0, 1, "wy2")
-        round_xm(0)
+        round_xm(0, "x_codes11")
 
         g_grouped = keep.tile([P, N, PACK], BF16, name="g_grouped", tag="xm_raw0", align_bytes=64)
         dst = g_grouped[:].rearrange("p (c i) t -> p c t i", i=4)
         src = g_rows[:].rearrange("p t (c i) -> p c t i", i=4)
         cut = G_SCALAR_SHARE // 4
+        quantize_xm(0)
         nc.vector.tensor_copy(dst[:, cut:], src[:, cut:])
         nc.scalar.copy(dst[:, :cut], src[:, :cut])
-        quantize_xm(0, 1)
         g_codes = keep.tile([P, N], U32, name="g_codes", align_bytes=64)
         g_plane = keep.tile([P, N], U8, name="g_plane", align_bytes=64)
         for cols in (slice(N // 2, N), slice(0, N // 2)):
@@ -183,43 +189,46 @@ def tile_attend_gnce_w_kernel(tc, xT, w_words, w_scales, y, wt, xm, offs, out):
                 in_=g_grouped[:, cols, :].rearrange("p i t -> p (i t)"),
             )
 
-        def product(k):
+        def multiply(k):
             dw = psum_dw.tile([P, N], F32, name="dw")
             nc.tensor.matmul_mx(
                 out=dw[:],
-                lhsT=xm_codes[:, k * P : (k + 1) * P].bitcast(E4M3),
-                lhsT_scale=xm_plane[:, k * P : (k + 1) * P],
+                lhsT=xm_codes[k].bitcast(E4M3),
+                lhsT_scale=xm_plane[k],
                 rhs=g_codes[:].bitcast(E5M2),
                 rhs_scale=g_plane[:],
                 start=True,
                 stop=True,
             )
-            if k == 0:
-                dw_sb = keep.tile([P, N], F32, name="dw_first", tag="xm_raw1", align_bytes=64)
-            else:
-                dw_sb = ring.tile([P, N], F32, name="dw_sb", align_bytes=64)
-            window = windows[k % WINDOWS]
-            pieces = 2 if k == 0 else 1
-            width = N // pieces
-            for c in range(pieces):
-                cols = slice(c * width, (c + 1) * width)
-                nc.scalar.copy(dw_sb[:, cols], dw[:, cols])
-                entries = offsets[:, c * width // 16 : (c + 1) * width // 16]
-                nc.vector.tensor_copy(window[:].indirect(entries), dw_sb[:, cols])
-            nc.sync.dma_start(out[k * P : (k + 1) * P, :], window[:])
+            return dw
 
-        grouped_tile(1, 4, "wy3")
-        round_xm(1)
-        round_xm(2)
-        round_xm(3)
-        quantize_xm(1, 2)
-        quantize_xm(2, 4)
-        product(0)
-        for k in range(1, 4):
-            product(k)
-        grouped_tile(4, D_TILES, "xm_raw1")
+        def place(k, dw, c0, c1, tag):
+            if tag is None:
+                dw_sb = ring.tile([P, c1 - c0], F32, name="dw_sb", align_bytes=64)
+            else:
+                dw_sb = keep.tile([P, c1 - c0], F32, name="dw_sb%d_%d" % (k, c0), tag=tag, align_bytes=64)
+            nc.scalar.copy(dw_sb[:], dw[:, c0:c1])
+            nc.vector.tensor_copy(windows[k % WINDOWS][:].indirect(offsets[:, c0 // 16 : c1 // 16]), dw_sb[:])
+
+        def store(k):
+            nc.sync.dma_start(out[k * P : (k + 1) * P, :], windows[k % WINDOWS][:])
+
+        round_xm(1, "wy3")
+        quantize_xm(1)
+        dw = multiply(0)
+        place(0, dw, 0, N // 2, "xm_raw1")
+        place(0, dw, N // 2, N, "dw_second_half")
+        store(0)
+        round_xm(2, "xm_codes0")
+        quantize_xm(2)
+        place(1, multiply(1), 0, N, "xm_raw2")
+        store(1)
+        place(2, multiply(2), 0, N, None)
+        store(2)
+        round_xm(3, "xm_raw1")
+        quantize_xm(3)
+        place(3, multiply(3), 0, N, "xm_raw4")
+        store(3)
         for k in range(4, D_TILES):
-            round_xm(k)
-        quantize_xm(4, D_TILES)
-        for k in range(4, D_TILES):
-            product(k)
+            place(k, multiply(k), 0, N, None)
+            store(k)

@@ -47,7 +47,7 @@ def tile_attend_gnce_w_kernel(tc, xT, w_words, w_scales, y, wt, xm, offs, out):
 
         warm_in = keep.tile([P, 1], F32, name="warm_in")
         warm_out = keep.tile([P, 1], F32, name="warm_out")
-        nc.gpsimd.memset(warm_in[:], 0.0)
+        nc.vector.memset(warm_in[:], 0.0)
         nc.scalar.activation(warm_out[:], warm_in[:], SIGMOID)
         nc.vector.memset(table_scales[:].rearrange("p o t -> p (o t)").bitcast(I32), 0)
         for window in windows:
@@ -56,16 +56,16 @@ def tile_attend_gnce_w_kernel(tc, xT, w_words, w_scales, y, wt, xm, offs, out):
         def load_x(o):
             nc.sync.dma_start(x_raw[o][:], xT[0, 512 * o : 512 * (o + 1), :].rearrange("(p j) r -> p j r", j=PACK))
 
-        load_x(0)
+        nc.sync.dma_start(table_words[:], w_words[0].rearrange("p t b -> p (t b)").bitcast(I32))
         nc.sync.dma_start(offsets[:], offs)
-        nc.sync.dma_start(wt_sb[:], wt[0].rearrange("(p t) one -> p (t one)", t=PACK))
         for r in range(4):
             nc.sync.dma_start(
                 table_scales[r:P:32, :, :].bitcast(I32),
                 w_scales[:, r:16:4, :].rearrange("o q t -> q o t").bitcast(I32),
             )
-        nc.sync.dma_start(table_words[:], w_words[0].rearrange("p t b -> p (t b)").bitcast(I32))
+        load_x(0)
         load_x(1)
+        nc.sync.dma_start(wt_sb[:], wt[0].rearrange("(p t) one -> p (t one)", t=PACK))
         y_rows = y[0].rearrange("(p t) i -> p t i", t=PACK)
         for t in range(PACK):
             nc.sync.dma_start(y_raw[t][:], y_rows[:, t, :])
@@ -106,13 +106,13 @@ def tile_attend_gnce_w_kernel(tc, xT, w_words, w_scales, y, wt, xm, offs, out):
 
         round_x(nc.scalar.copy, 0, 0, "x_low0")
         round_x(nc.scalar.copy, 0, 2, "x_high0")
-        gather_scales(0)
-        gather_scales(1)
-        codes_tile(0, 0, "table_scales")
-        quantize_x(0, 0, 2)
         nc.vector.tensor_copy(word_pairs[:], table_words[:].bitcast(U32).indirect(offsets[:]))
         part_words(0)
         part_words(1)
+        gather_scales(0)
+        gather_scales(1)
+        codes_tile(0, 0, "x_codes00")
+        quantize_x(0, 0, 2)
         round_x(nc.vector.tensor_copy, 1, 0, "x_low1")
         round_x(nc.scalar.copy, 1, 2, "x_high1")
         codes_tile(1, 0, "x_codes10")

@@ -24,7 +24,7 @@ PACK = 4
 PASSES = D // (P * PACK)
 D_TILES = D // P
 WINDOWS = 3
-G_SCALAR_SHARE = 160
+HALF = N // 2
 XM_LOADS = ((0, 1), (1, 2), (2, 4), (4, 8))
 
 
@@ -52,6 +52,10 @@ def tile_attend_gnce_w_kernel(tc, xT, w_words, w_scales, y, wt, xm, offs, out):
         nc.vector.memset(table_scales[:].rearrange("p o t -> p (o t)").bitcast(I32), 0)
         for window in windows:
             nc.vector.memset(window[:], 0.0)
+        g_codes = keep.tile([P, N], I32, name="g_codes", align_bytes=64)
+        g_plane = keep.tile([P, N], U8, name="g_plane", align_bytes=64)
+        nc.vector.memset(g_codes[:, HALF:], 0)
+        nc.vector.memset(g_plane[:, HALF:].bitcast(I32), 0)
 
         def load_x(o):
             nc.sync.dma_start(x_raw[o][:], xT[0, 512 * o : 512 * (o + 1), :].rearrange("(p j) r -> p j r", j=PACK))
@@ -75,7 +79,7 @@ def tile_attend_gnce_w_kernel(tc, xT, w_words, w_scales, y, wt, xm, offs, out):
 
         word_pairs = keep.tile([P, N], U32, name="word_pairs", align_bytes=64)
         w_plane = [keep.tile([P, N], U8, name="w_plane%d" % o, align_bytes=64) for o in range(PASSES)]
-        w_codes = [keep.tile([P, 2 * N], U8, name="w_codes%d" % o, align_bytes=64) for o in range(PASSES)]
+        w_codes = [keep.tile([P, 2 * N], U8, name="w_codes%d" % o, tag="w_codes%d" % o, align_bytes=64) for o in range(PASSES)]
 
         def gather_scales(o):
             nc.vector.tensor_copy(w_plane[o][:], table_scales[:, o, :].indirect(offsets[:]))
@@ -139,11 +143,36 @@ def tile_attend_gnce_w_kernel(tc, xT, w_words, w_scales, y, wt, xm, offs, out):
         nc.scalar.activation(wy[0][:], y_raw[0][:], COPY, scale=wt_sb[:, 0:1])
         for t in range(1, PACK):
             nc.vector.tensor_scalar(wy[t][:], y_raw[t][:], wt_sb[:, t : t + 1], None, MULT)
-        g_rows = keep.tile([P, PACK, N], BF16, name="g_rows", tag="y_raw3", align_bytes=64)
-        prob = keep.tile([P, PACK, N], F32, name="prob", tag="y_raw0", align_bytes=64)
-        for t in range(PACK):
-            nc.scalar.activation(prob[:, t, :], logits[t][:], SIGMOID)
-            nc.vector.scalar_tensor_tensor(g_rows[:, t, :], prob[:, t, :], wt_sb[:, t : t + 1], wy[t][:], MULT, SUBTRACT)
+        halves = (slice(0, HALF), slice(HALF, N))
+        prob = {}
+        g_rows = {}
+        g_grouped = {}
+
+        def sigmoid(h, tag):
+            prob[h] = keep.tile([P, PACK, HALF], F32, name="prob%d" % h, tag=tag, align_bytes=64)
+            for t in range(PACK):
+                nc.scalar.activation(prob[h][:, t, :], logits[t][:, halves[h]], SIGMOID)
+
+        def gradient(h):
+            g_rows[h] = keep.tile([P, PACK, HALF], BF16, name="g_rows%d" % h, tag="g_rows", align_bytes=64)
+            for t in range(PACK):
+                nc.vector.scalar_tensor_tensor(
+                    g_rows[h][:, t, :], prob[h][:, t, :], wt_sb[:, t : t + 1], wy[t][:, halves[h]], MULT, SUBTRACT
+                )
+
+        def interleave_g(copy, h):
+            g_grouped[h] = keep.tile([P, HALF, PACK], BF16, name="g_grouped%d" % h, align_bytes=64)
+            copy(
+                g_grouped[h][:].rearrange("p (c i) t -> p c t i", i=4),
+                g_rows[h][:].rearrange("p t (c i) -> p c t i", i=4),
+            )
+
+        def quantize_g(h):
+            nc.vector.quantize_mx(
+                out=g_codes[:, halves[h]].bitcast(E5M2),
+                scales=g_plane[:, halves[h]],
+                in_=g_grouped[h][:].rearrange("p i t -> p (i t)"),
+            )
 
         xm_codes = {}
         xm_plane = {}
@@ -171,24 +200,6 @@ def tile_attend_gnce_w_kernel(tc, xT, w_words, w_scales, y, wt, xm, offs, out):
                 xm_codes[k] = codes[:, (k - k0) * P : (k - k0 + 1) * P]
                 xm_plane[k] = plane[:, (k - k0) * P : (k - k0 + 1) * P]
 
-        round_xm(0, "x_codes11")
-
-        g_grouped = keep.tile([P, N, PACK], BF16, name="g_grouped", tag="xm_raw0", align_bytes=64)
-        dst = g_grouped[:].rearrange("p (c i) t -> p c t i", i=4)
-        src = g_rows[:].rearrange("p t (c i) -> p c t i", i=4)
-        cut = G_SCALAR_SHARE // 4
-        quantize_xm(0)
-        nc.vector.tensor_copy(dst[:, cut:], src[:, cut:])
-        nc.scalar.copy(dst[:, :cut], src[:, :cut])
-        g_codes = keep.tile([P, N], U32, name="g_codes", align_bytes=64)
-        g_plane = keep.tile([P, N], U8, name="g_plane", align_bytes=64)
-        for cols in (slice(N // 2, N), slice(0, N // 2)):
-            nc.vector.quantize_mx(
-                out=g_codes[:, cols].bitcast(E5M2),
-                scales=g_plane[:, cols],
-                in_=g_grouped[:, cols, :].rearrange("p i t -> p (i t)"),
-            )
-
         def multiply(k):
             dw = psum_dw.tile([P, N], F32, name="dw")
             nc.tensor.matmul_mx(
@@ -213,19 +224,31 @@ def tile_attend_gnce_w_kernel(tc, xT, w_words, w_scales, y, wt, xm, offs, out):
         def store(k):
             nc.sync.dma_start(out[k * P : (k + 1) * P, :], windows[k % WINDOWS][:])
 
-        round_xm(1, "wy3")
+        sigmoid(0, "y_raw0")
+        gradient(0)
+        round_xm(0, "w_codes1")
+        sigmoid(1, "x_codes11")
+        interleave_g(nc.vector.tensor_copy, 0)
+        quantize_xm(0)
+        quantize_g(0)
+        early0 = multiply(0)
+        gradient(1)
+        round_xm(1, "xm_raw0")
         quantize_xm(1)
-        dw = multiply(0)
-        place(0, dw, 0, N // 2, "xm_raw1")
-        place(0, dw, N // 2, N, "dw_second_half")
-        store(0)
-        round_xm(2, "xm_codes0")
+        place(0, early0, 0, HALF, "xm_raw1")
+        early1 = multiply(1)
+        interleave_g(nc.scalar.copy, 1)
+        quantize_g(1)
+        place(1, early1, 0, HALF, "dw_early1")
+        round_xm(2, "wy3")
         quantize_xm(2)
-        place(1, multiply(1), 0, N, "xm_raw2")
+        place(0, multiply(0), HALF, N, "xm_raw2")
+        store(0)
+        place(1, multiply(1), HALF, N, "dw_late1")
         store(1)
         place(2, multiply(2), 0, N, None)
         store(2)
-        round_xm(3, "xm_raw1")
+        round_xm(3, "xm_codes2")
         quantize_xm(3)
         place(3, multiply(3), 0, N, "xm_raw4")
         store(3)

@@ -213,13 +213,16 @@ def tile_attend_gnce_w_kernel(tc, xT, w_words, w_scales, y, wt, xm, offs, out):
             )
             return dw
 
-        def place(k, dw, c0, c1, tag):
-            if tag is None:
-                dw_sb = ring.tile([P, c1 - c0], F32, name="dw_sb", align_bytes=64)
-            else:
-                dw_sb = keep.tile([P, c1 - c0], F32, name="dw_sb%d_%d" % (k, c0), tag=tag, align_bytes=64)
-            nc.scalar.copy(dw_sb[:], dw[:, c0:c1])
-            nc.vector.tensor_copy(windows[k % WINDOWS][:].indirect(offsets[:, c0 // 16 : c1 // 16]), dw_sb[:])
+        def staging(name, width, tag):
+            return keep.tile([P, width], F32, name=name, tag=tag, align_bytes=64)
+
+        def place(k, dw, c0, c1, dw_sb):
+            nc.scalar.copy(dw_sb, dw[:, c0:c1])
+            nc.vector.tensor_copy(windows[k % WINDOWS][:].indirect(offsets[:, c0 // 16 : c1 // 16]), dw_sb)
+
+        def place_whole(k, dw_sb):
+            place(k, multiply(k), 0, N, dw_sb[:])
+            store(k)
 
         def store(k):
             nc.sync.dma_start(out[k * P : (k + 1) * P, :], windows[k % WINDOWS][:])
@@ -235,23 +238,20 @@ def tile_attend_gnce_w_kernel(tc, xT, w_words, w_scales, y, wt, xm, offs, out):
         gradient(1)
         round_xm(1, "xm_raw0")
         quantize_xm(1)
-        place(0, early0, 0, HALF, "xm_raw1")
+        place(0, early0, 0, HALF, staging("dw_early0", HALF, "xm_raw1")[:])
         early1 = multiply(1)
         interleave_g(nc.scalar.copy, 1)
         quantize_g(1)
-        place(1, early1, 0, HALF, "dw_early1")
+        place(1, early1, 0, HALF, staging("dw_early1", HALF, "dw_early1")[:])
         round_xm(2, "wy3")
         quantize_xm(2)
-        place(0, multiply(0), HALF, N, "xm_raw2")
-        store(0)
-        place(1, multiply(1), HALF, N, "dw_late1")
-        store(1)
-        place(2, multiply(2), 0, N, None)
-        store(2)
+        late = staging("dw_late", N, "xm_raw2")
+        for k in range(2):
+            place(k, multiply(k), HALF, N, late[:, k * HALF : (k + 1) * HALF])
+            store(k)
+        place_whole(2, ring.tile([P, N], F32, name="dw_sb", align_bytes=64))
         round_xm(3, "xm_codes2")
         quantize_xm(3)
-        place(3, multiply(3), 0, N, "xm_raw4")
-        store(3)
+        place_whole(3, staging("dw_sb3", N, "xm_raw4"))
         for k in range(4, D_TILES):
-            place(k, multiply(k), 0, N, None)
-            store(k)
+            place_whole(k, ring.tile([P, N], F32, name="dw_sb", align_bytes=64))

@@ -38,7 +38,7 @@ def tile_attend_gnce_w_kernel(tc, xT, w_words, w_scales, y, wt, xm, offs, out):
 
         offsets = keep.tile([P, N // 16], U16, name="offsets")
         table_words = keep.tile([P, T], I32, name="table_words", align_bytes=64)
-        table_scales = keep.tile([P, PASSES, T], U8, name="table_scales", tag="table_scales", align_bytes=64)
+        table_scales = keep.tile([P, T], U8, name="table_scales", align_bytes=64)
         x_raw = [keep.tile([P, PACK, R], F32, name="x_raw%d" % o, align_bytes=64) for o in range(PASSES)]
         y_raw = [keep.tile([P, N], F32, name="y_raw%d" % t, tag="y_raw%d" % t, align_bytes=64) for t in range(PACK)]
         wt_sb = keep.tile([P, PACK], F32, name="wt_sb")
@@ -49,11 +49,13 @@ def tile_attend_gnce_w_kernel(tc, xT, w_words, w_scales, y, wt, xm, offs, out):
         warm_out = keep.tile([P, 1], F32, name="warm_out")
         nc.vector.memset(warm_in[:], 0.0)
         nc.scalar.activation(warm_out[:], warm_in[:], SIGMOID)
-        nc.vector.memset(table_scales[:].rearrange("p o t -> p (o t)").bitcast(I32), 0)
+        nc.vector.memset(table_scales[:].bitcast(I32), 0)
+        w_plane = [keep.tile([P, N], U8, name="w_plane%d" % o, align_bytes=64) for o in range(PASSES)]
         for window in windows:
             nc.vector.memset(window[:], 0.0)
         g_codes = keep.tile([P, N], I32, name="g_codes", align_bytes=64)
         g_plane = keep.tile([P, N], U8, name="g_plane", align_bytes=64)
+        nc.vector.memset(w_plane[1][:].bitcast(I32), 0)
         nc.vector.memset(g_codes[:, HALF:], 0)
         nc.vector.memset(g_plane[:, HALF:].bitcast(I32), 0)
 
@@ -64,25 +66,14 @@ def tile_attend_gnce_w_kernel(tc, xT, w_words, w_scales, y, wt, xm, offs, out):
         nc.sync.dma_start(offsets[:], offs)
         for r in range(4):
             nc.sync.dma_start(
-                table_scales[r:P:32, :, :].bitcast(I32),
+                table_scales[r:P:16, :].bitcast(I32),
                 w_scales[:, r:16:4, :].rearrange("o q t -> q o t").bitcast(I32),
             )
         load_x(0)
         load_x(1)
-        nc.sync.dma_start(wt_sb[:], wt[0].rearrange("(p t) one -> p (t one)", t=PACK))
-        y_rows = y[0].rearrange("(p t) i -> p t i", t=PACK)
-        for t in range(PACK):
-            nc.sync.dma_start(y_raw[t][:], y_rows[:, t, :])
-        xm_rows = xm[0].rearrange("(p j) d -> p j d", j=PACK)
-        for raw, (k0, k1) in zip(xm_raw, XM_LOADS):
-            nc.sync.dma_start(raw[:], xm_rows[:, :, k0 * P : k1 * P])
 
         word_pairs = keep.tile([P, N], U32, name="word_pairs", align_bytes=64)
-        w_plane = [keep.tile([P, N], U8, name="w_plane%d" % o, align_bytes=64) for o in range(PASSES)]
         w_codes = [keep.tile([P, 2 * N], U8, name="w_codes%d" % o, tag="w_codes%d" % o, align_bytes=64) for o in range(PASSES)]
-
-        def gather_scales(o):
-            nc.vector.tensor_copy(w_plane[o][:], table_scales[:, o, :].indirect(offsets[:]))
 
         def part_words(o):
             nc.vector.tensor_copy(w_codes[o][:].bitcast(U16), word_pairs[:].bitcast(U16)[:, o : 2 * N : PASSES])
@@ -108,27 +99,35 @@ def tile_attend_gnce_w_kernel(tc, xT, w_words, w_scales, y, wt, xm, offs, out):
                 in_=x_grouped[o, t0 // 2][:, t0 % 2 : t0 % 2 + t1 - t0].rearrange("p t m j -> p (t m j)"),
             )
 
-        round_x(nc.scalar.copy, 0, 0, "x_low0")
         round_x(nc.scalar.copy, 0, 2, "x_high0")
         nc.vector.tensor_copy(word_pairs[:], table_words[:].bitcast(U32).indirect(offsets[:]))
+        nc.vector.tensor_copy(w_plane[0][:], table_scales[:].indirect(offsets[:]))
+        nc.sync.dma_start(w_plane[1][0 : P - 16, :].bitcast(I32), w_plane[0][16:P, :].bitcast(I32))
+        nc.sync.dma_start(wt_sb[:], wt[0].rearrange("(p t) one -> p (t one)", t=PACK))
+        y_rows = y[0].rearrange("(p t) i -> p t i", t=PACK)
+        for t in range(PACK):
+            nc.sync.dma_start(y_raw[t][:], y_rows[:, t, :])
+        xm_rows = xm[0].rearrange("(p j) d -> p j d", j=PACK)
+        for raw, (k0, k1) in zip(xm_raw, XM_LOADS):
+            nc.sync.dma_start(raw[:], xm_rows[:, :, k0 * P : k1 * P])
+
         part_words(0)
         part_words(1)
-        gather_scales(0)
-        gather_scales(1)
+        round_x(nc.vector.tensor_copy, 0, 0, "x_low0")
         codes_tile(0, 0, "x_codes00")
         quantize_x(0, 0, 2)
+        codes_tile(0, 1, "x_codes01")
+        quantize_x(0, 2, 4)
         round_x(nc.vector.tensor_copy, 1, 0, "x_low1")
         round_x(nc.scalar.copy, 1, 2, "x_high1")
         codes_tile(1, 0, "x_codes10")
         quantize_x(1, 0, 1)
         quantize_x(1, 1, 2)
-        codes_tile(0, 1, "x_low1")
-        quantize_x(0, 2, 4)
         codes_tile(1, 1, "x_codes11")
         quantize_x(1, 2, 4)
 
         logits = [psum_a.tile([P, N], F32, name="logits%d" % t) for t in range(PACK)]
-        for o, t in ((0, 0), (0, 1), (1, 0), (1, 1), (0, 2), (1, 2), (0, 3), (1, 3)):
+        for o, t in [(o, t) for o in range(PASSES) for t in range(PACK)]:
             nc.tensor.matmul_mx(
                 out=logits[t][:],
                 lhsT=x_codes[o, t // 2][:, t % 2, :].bitcast(E4M3),

@@ -37,10 +37,10 @@ def tile_attend_gnce_w_kernel(tc, xT, w_words, w_scales, y, wt, xm, offs, out):
         psum_dw = ctx.enter_context(tc.psum_pool(name="psum_dw", bufs=4))
 
         offsets = keep.tile([P, N // 16], U16, name="offsets")
-        table_words = keep.tile([P, T], I32, name="table_words", align_bytes=64)
+        table_words = keep.tile([P, T], I32, name="table_words", tag="table_words", align_bytes=64)
         table_scales = keep.tile([P, T], U8, name="table_scales", align_bytes=64)
         x_raw = [keep.tile([P, PACK, R], F32, name="x_raw%d" % o, align_bytes=64) for o in range(PASSES)]
-        y_raw = [keep.tile([P, N], F32, name="y_raw%d" % t, tag="y_raw%d" % t, align_bytes=64) for t in range(PACK)]
+        y_raw = [keep.tile([P, PACK, HALF], F32, name="y_raw%d" % h, tag="y_raw%d" % h, align_bytes=64) for h in range(2)]
         wt_sb = keep.tile([P, PACK], F32, name="wt_sb")
         xm_raw = [keep.tile([P, PACK, (k1 - k0) * P], F32, name="xm_raw%d" % k0, tag="xm_raw%d" % k0, align_bytes=64) for k0, k1 in XM_LOADS]
         windows = [keep.tile([P, T], F32, name="window%d" % k, align_bytes=64) for k in range(WINDOWS)]
@@ -50,7 +50,7 @@ def tile_attend_gnce_w_kernel(tc, xT, w_words, w_scales, y, wt, xm, offs, out):
         nc.vector.memset(warm_in[:], 0.0)
         nc.scalar.activation(warm_out[:], warm_in[:], SIGMOID)
         nc.vector.memset(table_scales[:].bitcast(I32), 0)
-        w_plane = [keep.tile([P, N], U8, name="w_plane%d" % o, align_bytes=64) for o in range(PASSES)]
+        w_plane = {1: keep.tile([P, N], U8, name="w_plane1", tag="w_plane1", align_bytes=64)}
         for window in windows:
             nc.vector.memset(window[:], 0.0)
         g_codes = keep.tile([P, N], I32, name="g_codes", align_bytes=64)
@@ -71,6 +71,9 @@ def tile_attend_gnce_w_kernel(tc, xT, w_words, w_scales, y, wt, xm, offs, out):
             )
         load_x(0)
         load_x(1)
+        nc.sync.dma_start(wt_sb[:], wt[0].rearrange("(p t) one -> p (t one)", t=PACK))
+        y_rows = y[0].rearrange("(p t) i -> p t i", t=PACK)
+        nc.sync.dma_start(y_raw[0][:], y_rows[:, :, :HALF])
 
         word_pairs = keep.tile([P, N], U32, name="word_pairs", align_bytes=64)
         w_codes = [keep.tile([P, 2 * N], U8, name="w_codes%d" % o, tag="w_codes%d" % o, align_bytes=64) for o in range(PASSES)]
@@ -101,18 +104,18 @@ def tile_attend_gnce_w_kernel(tc, xT, w_words, w_scales, y, wt, xm, offs, out):
 
         round_x(nc.scalar.copy, 0, 2, "x_high0")
         nc.vector.tensor_copy(word_pairs[:], table_words[:].bitcast(U32).indirect(offsets[:]))
-        nc.vector.tensor_copy(w_plane[0][:], table_scales[:].indirect(offsets[:]))
-        nc.sync.dma_start(w_plane[1][0 : P - 16, :].bitcast(I32), w_plane[0][16:P, :].bitcast(I32))
-        nc.sync.dma_start(wt_sb[:], wt[0].rearrange("(p t) one -> p (t one)", t=PACK))
-        y_rows = y[0].rearrange("(p t) i -> p t i", t=PACK)
-        for t in range(PACK):
-            nc.sync.dma_start(y_raw[t][:], y_rows[:, t, :])
-        xm_rows = xm[0].rearrange("(p j) d -> p j d", j=PACK)
-        for raw, (k0, k1) in zip(xm_raw, XM_LOADS):
-            nc.sync.dma_start(raw[:], xm_rows[:, :, k0 * P : k1 * P])
-
         part_words(0)
         part_words(1)
+        w_plane[0] = keep.tile([P, N], U8, name="w_plane0", tag="table_words", align_bytes=64)
+        nc.vector.tensor_copy(w_plane[0][:], table_scales[:].indirect(offsets[:]))
+        for r in range(4):
+            nc.sync.dma_start(w_plane[1][r:P:32, :].bitcast(I32), w_plane[0][16 + r : P : 32, :].bitcast(I32))
+        xm_rows = xm[0].rearrange("(p j) d -> p j d", j=PACK)
+        for load, (k0, k1) in enumerate(XM_LOADS):
+            nc.sync.dma_start(xm_raw[load][:], xm_rows[:, :, k0 * P : k1 * P])
+            if load == 0:
+                nc.sync.dma_start(y_raw[1][:], y_rows[:, :, HALF:])
+
         round_x(nc.vector.tensor_copy, 0, 0, "x_low0")
         codes_tile(0, 0, "x_codes00")
         quantize_x(0, 0, 2)
@@ -138,10 +141,17 @@ def tile_attend_gnce_w_kernel(tc, xT, w_words, w_scales, y, wt, xm, offs, out):
                 stop=(o == PASSES - 1),
             )
 
-        wy = [keep.tile([P, N], F32, name="wy%d" % t, tag="wy%d" % t, align_bytes=64) for t in range(PACK)]
-        nc.scalar.activation(wy[0][:], y_raw[0][:], COPY, scale=wt_sb[:, 0:1])
-        for t in range(1, PACK):
-            nc.vector.tensor_scalar(wy[t][:], y_raw[t][:], wt_sb[:, t : t + 1], None, MULT)
+        wy = {}
+
+        def weigh_y(h, pair, on_scalar, tag):
+            tile = keep.tile([P, 2, HALF], F32, name="wy%d%d" % (h, pair), tag=tag, align_bytes=64)
+            for t in range(2 * pair, 2 * pair + 2):
+                wy[h, t] = tile[:, t % 2, :]
+                if on_scalar:
+                    nc.scalar.activation(wy[h, t], y_raw[h][:, t, :], COPY, scale=wt_sb[:, t : t + 1])
+                else:
+                    nc.vector.tensor_scalar(wy[h, t], y_raw[h][:, t, :], wt_sb[:, t : t + 1], None, MULT)
+
         halves = (slice(0, HALF), slice(HALF, N))
         prob = {}
         g_rows = {}
@@ -156,7 +166,7 @@ def tile_attend_gnce_w_kernel(tc, xT, w_words, w_scales, y, wt, xm, offs, out):
             g_rows[h] = keep.tile([P, PACK, HALF], BF16, name="g_rows%d" % h, tag="g_rows", align_bytes=64)
             for t in range(PACK):
                 nc.vector.scalar_tensor_tensor(
-                    g_rows[h][:, t, :], prob[h][:, t, :], wt_sb[:, t : t + 1], wy[t][:, halves[h]], MULT, SUBTRACT
+                    g_rows[h][:, t, :], prob[h][:, t, :], wt_sb[:, t : t + 1], wy[h, t], MULT, SUBTRACT
                 )
 
         def interleave_g(copy, h):
@@ -226,14 +236,18 @@ def tile_attend_gnce_w_kernel(tc, xT, w_words, w_scales, y, wt, xm, offs, out):
         def store(k):
             nc.sync.dma_start(out[k * P : (k + 1) * P, :], windows[k % WINDOWS][:])
 
-        sigmoid(0, "y_raw0")
+        weigh_y(0, 0, False, "wy00")
+        weigh_y(0, 1, False, "wy01")
+        sigmoid(0, "prob0")
         gradient(0)
         round_xm(0, "w_codes1")
         sigmoid(1, "x_codes11")
+        weigh_y(1, 0, True, "w_plane1")
         interleave_g(nc.vector.tensor_copy, 0)
         quantize_xm(0)
         quantize_g(0)
         early0 = multiply(0)
+        weigh_y(1, 1, False, "prob0")
         gradient(1)
         round_xm(1, "xm_raw0")
         quantize_xm(1)
@@ -242,7 +256,7 @@ def tile_attend_gnce_w_kernel(tc, xT, w_words, w_scales, y, wt, xm, offs, out):
         interleave_g(nc.scalar.copy, 1)
         quantize_g(1)
         place(1, early1, 0, HALF, staging("dw_early1", HALF, "dw_early1")[:])
-        round_xm(2, "wy3")
+        round_xm(2, "x_codes11")
         quantize_xm(2)
         late = staging("dw_late", N, "xm_raw2")
         for k in range(2):

@@ -108,8 +108,7 @@ def tile_attend_gnce_w_kernel(tc, xT, w_words, w_scales, y, wt, xm, offs, out):
         part_words(1)
         w_plane[0] = keep.tile([P, N], U8, name="w_plane0", tag="table_words", align_bytes=64)
         nc.vector.tensor_copy(w_plane[0][:], table_scales[:].indirect(offsets[:]))
-        for r in range(4):
-            nc.sync.dma_start(w_plane[1][r:P:32, :].bitcast(I32), w_plane[0][16 + r : P : 32, :].bitcast(I32))
+        nc.sync.dma_start(w_plane[1][0 : P - 16, :].bitcast(I32), w_plane[0][16:P, :].bitcast(I32))
         xm_rows = xm[0].rearrange("(p j) d -> p j d", j=PACK)
         for load, (k0, k1) in enumerate(XM_LOADS):
             nc.sync.dma_start(xm_raw[load][:], xm_rows[:, :, k0 * P : k1 * P])

@@ -47,9 +47,9 @@ def tile_attend_gnce_w_kernel(tc, xT, w_words, w_scales, y, wt, xm, offs, out):
 
         warm_in = keep.tile([P, 1], F32, name="warm_in")
         warm_out = keep.tile([P, 1], F32, name="warm_out")
+        nc.vector.memset(table_scales[:].bitcast(I32), 0)
         nc.vector.memset(warm_in[:], 0.0)
         nc.scalar.activation(warm_out[:], warm_in[:], SIGMOID)
-        nc.vector.memset(table_scales[:].bitcast(I32), 0)
         w_plane = {1: keep.tile([P, N], U8, name="w_plane1", tag="w_plane1", align_bytes=64)}
         for window in windows:
             nc.vector.memset(window[:], 0.0)
@@ -62,17 +62,20 @@ def tile_attend_gnce_w_kernel(tc, xT, w_words, w_scales, y, wt, xm, offs, out):
         def load_x(o):
             nc.sync.dma_start(x_raw[o][:], xT[0, 512 * o : 512 * (o + 1), :].rearrange("(p j) r -> p j r", j=PACK))
 
-        nc.sync.dma_start(table_words[:], w_words[0].rearrange("p t b -> p (t b)").bitcast(I32))
         nc.sync.dma_start(offsets[:], offs)
+        nc.sync.dma_start(wt_sb[:], wt[0].rearrange("(p t) one -> p (t one)", t=PACK))
         for r in range(4):
             nc.sync.dma_start(
                 table_scales[r:P:16, :].bitcast(I32),
                 w_scales[:, r:16:4, :].rearrange("o q t -> q o t").bitcast(I32),
             )
+        nc.sync.dma_start(table_words[:], w_words[0].rearrange("p t b -> p (t b)").bitcast(I32))
         load_x(0)
         load_x(1)
-        nc.sync.dma_start(wt_sb[:], wt[0].rearrange("(p t) one -> p (t one)", t=PACK))
         y_rows = y[0].rearrange("(p t) i -> p t i", t=PACK)
+        w_plane[0] = keep.tile([P, N], U8, name="w_plane0", align_bytes=64)
+        nc.vector.tensor_copy(w_plane[0][:], table_scales[:].indirect(offsets[:]))
+        nc.sync.dma_start(w_plane[1][0 : P - 16, :].bitcast(I32), w_plane[0][16:P, :].bitcast(I32))
         nc.sync.dma_start(y_raw[0][:], y_rows[:, :, :HALF])
 
         word_pairs = keep.tile([P, N], U32, name="word_pairs", align_bytes=64)
@@ -106,9 +109,6 @@ def tile_attend_gnce_w_kernel(tc, xT, w_words, w_scales, y, wt, xm, offs, out):
         nc.vector.tensor_copy(word_pairs[:], table_words[:].bitcast(U32).indirect(offsets[:]))
         part_words(0)
         part_words(1)
-        w_plane[0] = keep.tile([P, N], U8, name="w_plane0", tag="table_words", align_bytes=64)
-        nc.vector.tensor_copy(w_plane[0][:], table_scales[:].indirect(offsets[:]))
-        nc.sync.dma_start(w_plane[1][0 : P - 16, :].bitcast(I32), w_plane[0][16:P, :].bitcast(I32))
         xm_rows = xm[0].rearrange("(p j) d -> p j d", j=PACK)
         for load, (k0, k1) in enumerate(XM_LOADS):
             nc.sync.dma_start(xm_raw[load][:], xm_rows[:, :, k0 * P : k1 * P])
@@ -195,9 +195,9 @@ def tile_attend_gnce_w_kernel(tc, xT, w_words, w_scales, y, wt, xm, offs, out):
                     xm_raw[load][:, :, d0 : d0 + P].rearrange("p j (c i) -> p c j i", i=4),
                 )
 
-        def quantize_xm(load):
+        def quantize_xm(load, tag):
             k0, k1 = XM_LOADS[load]
-            codes = keep.tile([P, (k1 - k0) * P], U32, name="xm_codes%d" % k0, tag="xm_codes%d" % k0, align_bytes=64)
+            codes = keep.tile([P, (k1 - k0) * P], U32, name="xm_codes%d" % k0, tag=tag, align_bytes=64)
             plane = keep.tile([P, (k1 - k0) * P], U8, name="xm_plane%d" % k0, align_bytes=64)
             nc.vector.quantize_mx(
                 out=codes[:].bitcast(E4M3),
@@ -243,27 +243,27 @@ def tile_attend_gnce_w_kernel(tc, xT, w_words, w_scales, y, wt, xm, offs, out):
         sigmoid(1, "x_codes11")
         weigh_y(1, 0, True, "w_plane1")
         interleave_g(nc.vector.tensor_copy, 0)
-        quantize_xm(0)
+        quantize_xm(0, "wy01")
         quantize_g(0)
         early0 = multiply(0)
         weigh_y(1, 1, False, "prob0")
         gradient(1)
         round_xm(1, "xm_raw0")
-        quantize_xm(1)
-        place(0, early0, 0, HALF, staging("dw_early0", HALF, "xm_raw1")[:])
+        quantize_xm(1, "xm_codes1")
+        place(0, early0, 0, HALF, staging("dw_early0", HALF, "dw_early0")[:])
         early1 = multiply(1)
         interleave_g(nc.scalar.copy, 1)
         quantize_g(1)
         place(1, early1, 0, HALF, staging("dw_early1", HALF, "dw_early1")[:])
         round_xm(2, "x_codes11")
-        quantize_xm(2)
+        quantize_xm(2, "xm_codes2")
         late = staging("dw_late", N, "xm_raw2")
         for k in range(2):
             place(k, multiply(k), HALF, N, late[:, k * HALF : (k + 1) * HALF])
             store(k)
         place_whole(2, ring.tile([P, N], F32, name="dw_sb", align_bytes=64))
         round_xm(3, "xm_codes2")
-        quantize_xm(3)
+        quantize_xm(3, "xm_codes4")
         place_whole(3, staging("dw_sb3", N, "xm_raw4"))
         for k in range(4, D_TILES):
             place_whole(k, ring.tile([P, N], F32, name="dw_sb", align_bytes=64))

@@ -25,6 +25,8 @@ PASSES = D // (P * PACK)
 D_TILES = D // P
 WINDOWS = 3
 HALF = N // 2
+Y_LOADS = ((0, 0, 2), (0, 2, 4), (1, 0, 4))
+SHARE = 40
 XM_LOADS = ((0, 1), (1, 2), (2, 4), (4, 8))
 
 
@@ -40,10 +42,10 @@ def tile_attend_gnce_w_kernel(tc, xT, w_words, w_scales, y, wt, xm, offs, out):
         table_words = keep.tile([P, T], I32, name="table_words", tag="table_words", align_bytes=64)
         table_scales = keep.tile([P, T], U8, name="table_scales", align_bytes=64)
         x_raw = [keep.tile([P, PACK, R], F32, name="x_raw%d" % o, align_bytes=64) for o in range(PASSES)]
-        y_raw = [keep.tile([P, PACK, HALF], F32, name="y_raw%d" % h, tag="y_raw%d" % h, align_bytes=64) for h in range(2)]
+        y_raw = {(h, t0): keep.tile([P, t1 - t0, HALF], F32, name="y_raw%d%d" % (h, t0), align_bytes=64) for h, t0, t1 in Y_LOADS}
         wt_sb = keep.tile([P, PACK], F32, name="wt_sb")
         xm_raw = [keep.tile([P, PACK, (k1 - k0) * P], F32, name="xm_raw%d" % k0, tag="xm_raw%d" % k0, align_bytes=64) for k0, k1 in XM_LOADS]
-        windows = [keep.tile([P, T], F32, name="window%d" % k, align_bytes=64) for k in range(WINDOWS)]
+        windows = [keep.tile([P, T], F32, name="window%d" % k, align_bytes=64) for k in range(WINDOWS - 1)]
 
         warm_in = keep.tile([P, 1], F32, name="warm_in")
         warm_out = keep.tile([P, 1], F32, name="warm_out")
@@ -76,7 +78,12 @@ def tile_attend_gnce_w_kernel(tc, xT, w_words, w_scales, y, wt, xm, offs, out):
         w_plane[0] = keep.tile([P, N], U8, name="w_plane0", align_bytes=64)
         nc.vector.tensor_copy(w_plane[0][:], table_scales[:].indirect(offsets[:]))
         nc.sync.dma_start(w_plane[1][0 : P - 16, :].bitcast(I32), w_plane[0][16:P, :].bitcast(I32))
-        nc.sync.dma_start(y_raw[0][:], y_rows[:, :, :HALF])
+
+        def load_y(h, t0, t1):
+            nc.sync.dma_start(y_raw[h, t0][:], y_rows[:, t0:t1, h * HALF : (h + 1) * HALF])
+
+        load_y(*Y_LOADS[0])
+        load_y(*Y_LOADS[1])
 
         word_pairs = keep.tile([P, N], U32, name="word_pairs", align_bytes=64)
         w_codes = [keep.tile([P, 2 * N], U8, name="w_codes%d" % o, tag="w_codes%d" % o, align_bytes=64) for o in range(PASSES)]
@@ -88,11 +95,12 @@ def tile_attend_gnce_w_kernel(tc, xT, w_words, w_scales, y, wt, xm, offs, out):
         x_codes = {}
         x_plane = [keep.tile([P, PACK, P], U8, name="x_plane%d" % o, align_bytes=64) for o in range(PASSES)]
 
-        def round_x(copy, o, t0, tag):
-            x_grouped[o, t0 // 2] = keep.tile([P, 2, P, PACK], BF16, name=tag, tag=tag, align_bytes=64)
+        def round_x(copy, o, t0, m0, m1):
+            if (o, t0 // 2) not in x_grouped:
+                x_grouped[o, t0 // 2] = keep.tile([P, 2, P, PACK], BF16, name="x_grouped%d%d" % (o, t0), align_bytes=64)
             copy(
-                x_grouped[o, t0 // 2][:].rearrange("p t m j -> p m j t"),
-                x_raw[o][:].rearrange("p j (m t) -> p m j t", t=PACK)[:, :, :, t0 : t0 + 2],
+                x_grouped[o, t0 // 2][:].rearrange("p t m j -> p m j t")[:, m0:m1],
+                x_raw[o][:].rearrange("p j (m t) -> p m j t", t=PACK)[:, m0:m1, :, t0 : t0 + 2],
             )
 
         def codes_tile(o, pair, tag):
@@ -105,7 +113,7 @@ def tile_attend_gnce_w_kernel(tc, xT, w_words, w_scales, y, wt, xm, offs, out):
                 in_=x_grouped[o, t0 // 2][:, t0 % 2 : t0 % 2 + t1 - t0].rearrange("p t m j -> p (t m j)"),
             )
 
-        round_x(nc.scalar.copy, 0, 2, "x_high0")
+        round_x(nc.scalar.copy, 0, 2, 0, P)
         nc.vector.tensor_copy(word_pairs[:], table_words[:].bitcast(U32).indirect(offsets[:]))
         part_words(0)
         part_words(1)
@@ -113,15 +121,16 @@ def tile_attend_gnce_w_kernel(tc, xT, w_words, w_scales, y, wt, xm, offs, out):
         for load, (k0, k1) in enumerate(XM_LOADS):
             nc.sync.dma_start(xm_raw[load][:], xm_rows[:, :, k0 * P : k1 * P])
             if load == 0:
-                nc.sync.dma_start(y_raw[1][:], y_rows[:, :, HALF:])
+                load_y(*Y_LOADS[2])
 
-        round_x(nc.vector.tensor_copy, 0, 0, "x_low0")
+        round_x(nc.vector.tensor_copy, 0, 0, 0, P)
         codes_tile(0, 0, "x_codes00")
         quantize_x(0, 0, 2)
         codes_tile(0, 1, "x_codes01")
         quantize_x(0, 2, 4)
-        round_x(nc.vector.tensor_copy, 1, 0, "x_low1")
-        round_x(nc.scalar.copy, 1, 2, "x_high1")
+        round_x(nc.vector.tensor_copy, 1, 0, 0, P)
+        round_x(nc.vector.tensor_copy, 1, 2, 0, SHARE)
+        round_x(nc.scalar.copy, 1, 2, SHARE, P)
         codes_tile(1, 0, "x_codes10")
         quantize_x(1, 0, 1)
         quantize_x(1, 1, 2)
@@ -142,14 +151,18 @@ def tile_attend_gnce_w_kernel(tc, xT, w_words, w_scales, y, wt, xm, offs, out):
 
         wy = {}
 
+        def y_part(h, t):
+            t0 = max(first for half, first, last in Y_LOADS if half == h and first <= t)
+            return y_raw[h, t0][:, t - t0, :]
+
         def weigh_y(h, pair, on_scalar, tag):
             tile = keep.tile([P, 2, HALF], F32, name="wy%d%d" % (h, pair), tag=tag, align_bytes=64)
             for t in range(2 * pair, 2 * pair + 2):
                 wy[h, t] = tile[:, t % 2, :]
                 if on_scalar:
-                    nc.scalar.activation(wy[h, t], y_raw[h][:, t, :], COPY, scale=wt_sb[:, t : t + 1])
+                    nc.scalar.activation(wy[h, t], y_part(h, t), COPY, scale=wt_sb[:, t : t + 1])
                 else:
-                    nc.vector.tensor_scalar(wy[h, t], y_raw[h][:, t, :], wt_sb[:, t : t + 1], None, MULT)
+                    nc.vector.tensor_scalar(wy[h, t], y_part(h, t), wt_sb[:, t : t + 1], None, MULT)
 
         halves = (slice(0, HALF), slice(HALF, N))
         prob = {}
@@ -235,7 +248,7 @@ def tile_attend_gnce_w_kernel(tc, xT, w_words, w_scales, y, wt, xm, offs, out):
         def store(k):
             nc.sync.dma_start(out[k * P : (k + 1) * P, :], windows[k % WINDOWS][:])
 
-        weigh_y(0, 0, False, "wy00")
+        weigh_y(0, 0, True, "wy00")
         weigh_y(0, 1, False, "wy01")
         sigmoid(0, "prob0")
         gradient(0)
@@ -255,6 +268,8 @@ def tile_attend_gnce_w_kernel(tc, xT, w_words, w_scales, y, wt, xm, offs, out):
         interleave_g(nc.scalar.copy, 1)
         quantize_g(1)
         place(1, early1, 0, HALF, staging("dw_early1", HALF, "dw_early1")[:])
+        windows.append(keep.tile([P, T], F32, name="window2", tag="dw_early1", align_bytes=64))
+        nc.gpsimd.memset(windows[2][:], 0.0)
         round_xm(2, "x_codes11")
         quantize_xm(2, "xm_codes2")
         late = staging("dw_late", N, "xm_raw2")

@@ -27,6 +27,7 @@ WINDOWS = 3
 HALF = N // 2
 Y_LOADS = ((0, 0, 2), (0, 2, 4), (1, 0, 4))
 SHARE = 40
+HEAD = 512
 XM_LOADS = ((0, 1), (1, 2), (2, 4), (4, 8))
 
 
@@ -64,25 +65,27 @@ def tile_attend_gnce_w_kernel(tc, xT, w_words, w_scales, y, wt, xm, offs, out):
         def load_x(o):
             nc.sync.dma_start(x_raw[o][:], xT[0, 512 * o : 512 * (o + 1), :].rearrange("(p j) r -> p j r", j=PACK))
 
+        words = w_words[0].rearrange("p t b -> p (t b)").bitcast(I32)
+        nc.sync.dma_start(table_words[:, :HEAD], words[:, :HEAD])
         nc.sync.dma_start(offsets[:], offs)
-        nc.sync.dma_start(wt_sb[:], wt[0].rearrange("(p t) one -> p (t one)", t=PACK))
         for r in range(4):
             nc.sync.dma_start(
                 table_scales[r:P:16, :].bitcast(I32),
                 w_scales[:, r:16:4, :].rearrange("o q t -> q o t").bitcast(I32),
             )
-        nc.sync.dma_start(table_words[:], w_words[0].rearrange("p t b -> p (t b)").bitcast(I32))
+        nc.sync.dma_start(table_words[:, HEAD:], words[:, HEAD:])
         load_x(0)
         load_x(1)
+        nc.sync.dma_start(wt_sb[:], wt[0].rearrange("(p t) one -> p (t one)", t=PACK))
         y_rows = y[0].rearrange("(p t) i -> p t i", t=PACK)
         w_plane[0] = keep.tile([P, N], U8, name="w_plane0", align_bytes=64)
         nc.vector.tensor_copy(w_plane[0][:], table_scales[:].indirect(offsets[:]))
-        nc.sync.dma_start(w_plane[1][0 : P - 16, :].bitcast(I32), w_plane[0][16:P, :].bitcast(I32))
 
         def load_y(h, t0, t1):
             nc.sync.dma_start(y_raw[h, t0][:], y_rows[:, t0:t1, h * HALF : (h + 1) * HALF])
 
         load_y(*Y_LOADS[0])
+        nc.sync.dma_start(w_plane[1][0 : P - 16, :].bitcast(I32), w_plane[0][16:P, :].bitcast(I32))
         load_y(*Y_LOADS[1])
 
         word_pairs = keep.tile([P, N], U32, name="word_pairs", align_bytes=64)

@@ -25,8 +25,8 @@ PASSES = D // (P * PACK)
 D_TILES = D // P
 WINDOWS = 3
 HALF = N // 2
-Y_LOADS = ((0, 0, 2), (0, 2, 4), (1, 0, 4))
-SHARE = 40
+Y_LOADS = ((0, 0, 2), (0, 2, 4), (1, 2, 4), (1, 0, 2))
+SHARE = 80
 HEAD = 512
 XM_LOADS = ((0, 1), (1, 2), (2, 4), (4, 8))
 
@@ -116,7 +116,6 @@ def tile_attend_gnce_w_kernel(tc, xT, w_words, w_scales, y, wt, xm, offs, out):
                 in_=x_grouped[o, t0 // 2][:, t0 % 2 : t0 % 2 + t1 - t0].rearrange("p t m j -> p (t m j)"),
             )
 
-        round_x(nc.scalar.copy, 0, 2, 0, P)
         nc.vector.tensor_copy(word_pairs[:], table_words[:].bitcast(U32).indirect(offsets[:]))
         part_words(0)
         part_words(1)
@@ -125,15 +124,18 @@ def tile_attend_gnce_w_kernel(tc, xT, w_words, w_scales, y, wt, xm, offs, out):
             nc.sync.dma_start(xm_raw[load][:], xm_rows[:, :, k0 * P : k1 * P])
             if load == 0:
                 load_y(*Y_LOADS[2])
+                load_y(*Y_LOADS[3])
 
-        round_x(nc.vector.tensor_copy, 0, 0, 0, P)
+        for t0 in (0, 2):
+            round_x(nc.vector.tensor_copy, 0, t0, 0, SHARE)
+            round_x(nc.scalar.copy, 0, t0, SHARE, P)
         codes_tile(0, 0, "x_codes00")
         quantize_x(0, 0, 2)
         codes_tile(0, 1, "x_codes01")
         quantize_x(0, 2, 4)
-        round_x(nc.vector.tensor_copy, 1, 0, 0, P)
-        round_x(nc.vector.tensor_copy, 1, 2, 0, SHARE)
-        round_x(nc.scalar.copy, 1, 2, SHARE, P)
+        for t0 in (0, 2):
+            round_x(nc.vector.tensor_copy, 1, t0, 0, SHARE)
+            round_x(nc.scalar.copy, 1, t0, SHARE, P)
         codes_tile(1, 0, "x_codes10")
         quantize_x(1, 0, 1)
         quantize_x(1, 1, 2)
@@ -158,14 +160,12 @@ def tile_attend_gnce_w_kernel(tc, xT, w_words, w_scales, y, wt, xm, offs, out):
             t0 = max(first for half, first, last in Y_LOADS if half == h and first <= t)
             return y_raw[h, t0][:, t - t0, :]
 
-        def weigh_y(h, pair, on_scalar, tag):
-            tile = keep.tile([P, 2, HALF], F32, name="wy%d%d" % (h, pair), tag=tag, align_bytes=64)
-            for t in range(2 * pair, 2 * pair + 2):
-                wy[h, t] = tile[:, t % 2, :]
-                if on_scalar:
-                    nc.scalar.activation(wy[h, t], y_part(h, t), COPY, scale=wt_sb[:, t : t + 1])
-                else:
-                    nc.vector.tensor_scalar(wy[h, t], y_part(h, t), wt_sb[:, t : t + 1], None, MULT)
+        def weigh_y(h, t, on_scalar, tag):
+            wy[h, t] = keep.tile([P, HALF], F32, name="wy%d%d" % (h, t), tag=tag, align_bytes=64)[:]
+            if on_scalar:
+                nc.scalar.activation(wy[h, t], y_part(h, t), COPY, scale=wt_sb[:, t : t + 1])
+            else:
+                nc.vector.tensor_scalar(wy[h, t], y_part(h, t), wt_sb[:, t : t + 1], None, MULT)
 
         halves = (slice(0, HALF), slice(HALF, N))
         prob = {}
@@ -177,9 +177,9 @@ def tile_attend_gnce_w_kernel(tc, xT, w_words, w_scales, y, wt, xm, offs, out):
             for t in range(PACK):
                 nc.scalar.activation(prob[h][:, t, :], logits[t][:, halves[h]], SIGMOID)
 
-        def gradient(h):
+        def gradient(h, order):
             g_rows[h] = keep.tile([P, PACK, HALF], BF16, name="g_rows%d" % h, tag="g_rows", align_bytes=64)
-            for t in range(PACK):
+            for t in order:
                 nc.vector.scalar_tensor_tensor(
                     g_rows[h][:, t, :], prob[h][:, t, :], wt_sb[:, t : t + 1], wy[h, t], MULT, SUBTRACT
                 )
@@ -251,19 +251,21 @@ def tile_attend_gnce_w_kernel(tc, xT, w_words, w_scales, y, wt, xm, offs, out):
         def store(k):
             nc.sync.dma_start(out[k * P : (k + 1) * P, :], windows[k % WINDOWS][:])
 
-        weigh_y(0, 0, True, "wy00")
-        weigh_y(0, 1, False, "wy01")
+        for t in range(PACK):
+            weigh_y(0, t, t < 2, "wy0%d" % t)
         sigmoid(0, "prob0")
-        gradient(0)
+        gradient(0, range(PACK))
         round_xm(0, "w_codes1")
         sigmoid(1, "x_codes11")
         weigh_y(1, 0, True, "w_plane1")
+        weigh_y(1, 1, True, "w_codes0")
+        weigh_y(1, 2, False, "wy02")
         interleave_g(nc.vector.tensor_copy, 0)
-        quantize_xm(0, "wy01")
+        quantize_xm(0, "wy03")
         quantize_g(0)
         early0 = multiply(0)
-        weigh_y(1, 1, False, "prob0")
-        gradient(1)
+        weigh_y(1, 3, False, "prob0")
+        gradient(1, (2, 3, 0, 1))
         round_xm(1, "xm_raw0")
         quantize_xm(1, "xm_codes1")
         place(0, early0, 0, HALF, staging("dw_early0", HALF, "dw_early0")[:])

@@ -89,7 +89,7 @@ def tile_attend_gnce_w_kernel(tc, xT, w_words, w_scales, y, wt, xm, offs, out):
         load_y(*Y_LOADS[1])
 
         word_pairs = keep.tile([P, N], U32, name="word_pairs", align_bytes=64)
-        w_codes = [keep.tile([P, 2 * N], U8, name="w_codes%d" % o, tag="w_codes%d" % o, align_bytes=64) for o in range(PASSES)]
+        w_codes = [keep.tile([P, 2 * N], U8, name="w_codes%d" % o, tag="w_codes%d" % o, align_bytes=64) for o in range(1)]
 
         def part_words(o):
             nc.vector.tensor_copy(w_codes[o][:].bitcast(U16), word_pairs[:].bitcast(U16)[:, o : 2 * N : PASSES])
@@ -100,7 +100,7 @@ def tile_attend_gnce_w_kernel(tc, xT, w_words, w_scales, y, wt, xm, offs, out):
 
         def round_x(copy, o, t0, m0, m1):
             if (o, t0 // 2) not in x_grouped:
-                x_grouped[o, t0 // 2] = keep.tile([P, 2, P, PACK], BF16, name="x_grouped%d%d" % (o, t0), align_bytes=64)
+                x_grouped[o, t0 // 2] = keep.tile([P, 2, P, PACK], BF16, name="x_grouped%d%d" % (o, t0), tag="x_grouped%d%d" % (o, t0), align_bytes=64)
             copy(
                 x_grouped[o, t0 // 2][:].rearrange("p t m j -> p m j t")[:, m0:m1],
                 x_raw[o][:].rearrange("p j (m t) -> p m j t", t=PACK)[:, m0:m1, :, t0 : t0 + 2],
@@ -118,7 +118,6 @@ def tile_attend_gnce_w_kernel(tc, xT, w_words, w_scales, y, wt, xm, offs, out):
 
         nc.vector.tensor_copy(word_pairs[:], table_words[:].bitcast(U32).indirect(offsets[:]))
         part_words(0)
-        part_words(1)
         xm_rows = xm[0].rearrange("(p j) d -> p j d", j=PACK)
         for load, (k0, k1) in enumerate(XM_LOADS):
             nc.sync.dma_start(xm_raw[load][:], xm_rows[:, :, k0 * P : k1 * P])
@@ -130,7 +129,10 @@ def tile_attend_gnce_w_kernel(tc, xT, w_words, w_scales, y, wt, xm, offs, out):
             round_x(nc.vector.tensor_copy, 0, t0, 0, SHARE)
             round_x(nc.scalar.copy, 0, t0, SHARE, P)
         codes_tile(0, 0, "x_codes00")
-        quantize_x(0, 0, 2)
+        quantize_x(0, 0, 1)
+        quantize_x(0, 1, 2)
+        w_codes.append(keep.tile([P, 2 * N], U8, name="w_codes1", tag="x_grouped00", align_bytes=64))
+        part_words(1)
         codes_tile(0, 1, "x_codes01")
         quantize_x(0, 2, 4)
         for t0 in (0, 2):
@@ -255,7 +257,7 @@ def tile_attend_gnce_w_kernel(tc, xT, w_words, w_scales, y, wt, xm, offs, out):
             weigh_y(0, t, t < 2, "wy0%d" % t)
         sigmoid(0, "prob0")
         gradient(0, range(PACK))
-        round_xm(0, "w_codes1")
+        round_xm(0, "x_grouped00")
         sigmoid(1, "x_codes11")
         weigh_y(1, 0, True, "w_plane1")
         weigh_y(1, 1, True, "w_codes0")

@@ -27,7 +27,12 @@ WINDOWS = 3
 HALF = N // 2
 Y_LOADS = ((0, 0, 2), (0, 2, 4), (1, 2, 4), (1, 0, 2))
 SHARE = 80
-HEAD = 512
+SCALE_ROW0 = 96
+AT = {
+    "window1": 0, "table_scales": 8128, "wt": 8192, "x1": 8256,
+    "prob0": 16448, "table_words": 18496, "y00": 18496, "y02": 20544, "xm0": 22592, "y12": 24640,
+    "y10": 26688, "x0": 28672, "xm1": 28736, "xm2": 30784, "xm4": 34880,
+}
 XM_LOADS = ((0, 1), (1, 2), (2, 4), (4, 8))
 
 
@@ -35,58 +40,65 @@ def tile_attend_gnce_w_kernel(tc, xT, w_words, w_scales, y, wt, xm, offs, out):
     nc = tc.nc
     with ExitStack() as ctx:
         keep = ctx.enter_context(tc.tile_pool(name="keep", bufs=1))
+        reuse = ctx.enter_context(tc.tile_pool(name="reuse", bufs=1))
         ring = ctx.enter_context(tc.tile_pool(name="ring", bufs=3))
         psum_a = ctx.enter_context(tc.psum_pool(name="psum_a", bufs=1))
         psum_dw = ctx.enter_context(tc.psum_pool(name="psum_dw", bufs=4))
 
         offsets = keep.tile([P, N // 16], U16, name="offsets")
-        table_words = keep.tile([P, T], I32, name="table_words", tag="table_words", align_bytes=64)
-        table_scales = keep.tile([P, T], U8, name="table_scales", align_bytes=64)
-        x_raw = [keep.tile([P, PACK, R], F32, name="x_raw%d" % o, align_bytes=64) for o in range(PASSES)]
-        y_raw = {(h, t0): keep.tile([P, t1 - t0, HALF], F32, name="y_raw%d%d" % (h, t0), align_bytes=64) for h, t0, t1 in Y_LOADS}
-        wt_sb = keep.tile([P, PACK], F32, name="wt_sb")
-        xm_raw = [keep.tile([P, PACK, (k1 - k0) * P], F32, name="xm_raw%d" % k0, tag="xm_raw%d" % k0, align_bytes=64) for k0, k1 in XM_LOADS]
-        windows = [keep.tile([P, T], F32, name="window%d" % k, align_bytes=64) for k in range(WINDOWS - 1)]
+
+        def tile(shape, dtype, name, tag):
+            if tag in AT:
+                return reuse.tile(shape, dtype, name=name, tag=tag, align_bytes=64, offset=AT[tag])
+            return keep.tile(shape, dtype, name=name, tag=tag, align_bytes=64)
+
+        table_words = tile([P, T], I32, "table_words", "table_words")
+        table_scales = tile([P, T], U8, "table_scales", "table_scales")
+        x_raw = [tile([P, PACK, R], F32, "x_raw%d" % o, "x%d" % o) for o in range(PASSES)]
+        y_raw = {(h, t0): tile([P, t1 - t0, HALF], F32, "y_raw%d%d" % (h, t0), "y%d%d" % (h, t0)) for h, t0, t1 in Y_LOADS}
+        wt_sb = tile([P, PACK], F32, "wt_sb", "wt")
+        xm_raw = [tile([P, PACK, (k1 - k0) * P], F32, "xm_raw%d" % k0, "xm%d" % k0) for k0, k1 in XM_LOADS]
+        windows = [tile([P, T], F32, "window%d" % k, "window%d" % k) for k in range(WINDOWS - 1)]
 
         warm_in = keep.tile([P, 1], F32, name="warm_in")
         warm_out = keep.tile([P, 1], F32, name="warm_out")
-        nc.vector.memset(table_scales[:].bitcast(I32), 0)
+        nc.vector.memset(table_scales[0:SCALE_ROW0, :].bitcast(I32), 0)
         nc.vector.memset(warm_in[:], 0.0)
         nc.scalar.activation(warm_out[:], warm_in[:], SIGMOID)
-        w_plane = {1: keep.tile([P, N], U8, name="w_plane1", tag="w_plane1", align_bytes=64)}
-        for window in windows:
-            nc.vector.memset(window[:], 0.0)
+        w_plane = [keep.tile([P, N], U8, name="w_plane%d" % o, tag="w_plane%d" % o, align_bytes=64) for o in range(PASSES)]
         g_codes = keep.tile([P, N], I32, name="g_codes", align_bytes=64)
         g_plane = keep.tile([P, N], U8, name="g_plane", align_bytes=64)
-        nc.vector.memset(w_plane[1][:].bitcast(I32), 0)
+        for plane in w_plane:
+            nc.vector.memset(plane[:].bitcast(I32), 0)
         nc.vector.memset(g_codes[:, HALF:], 0)
         nc.vector.memset(g_plane[:, HALF:].bitcast(I32), 0)
+        nc.vector.memset(windows[0][:], 0.0)
 
         def load_x(o):
             nc.sync.dma_start(x_raw[o][:], xT[0, 512 * o : 512 * (o + 1), :].rearrange("(p j) r -> p j r", j=PACK))
 
         words = w_words[0].rearrange("p t b -> p (t b)").bitcast(I32)
-        nc.sync.dma_start(table_words[:, :HEAD], words[:, :HEAD])
+        nc.sync.dma_start(table_scales[SCALE_ROW0:P, :].bitcast(I32), w_scales.rearrange("o f t -> (o f) t").bitcast(I32))
         nc.sync.dma_start(offsets[:], offs)
-        for r in range(4):
-            nc.sync.dma_start(
-                table_scales[r:P:16, :].bitcast(I32),
-                w_scales[:, r:16:4, :].rearrange("o q t -> q o t").bitcast(I32),
-            )
-        nc.sync.dma_start(table_words[:, HEAD:], words[:, HEAD:])
+        nc.sync.dma_start(table_words[:], words)
         load_x(0)
+        picked_scales = keep.tile([P, N], U8, name="picked_scales", align_bytes=64)
+        nc.vector.tensor_copy(picked_scales[:], table_scales[:].indirect(offsets[:]))
+        nc.vector.memset(windows[1][:], 0.0)
+
+        def move_scales(o):
+            for q in range(4):
+                row = SCALE_ROW0 + 16 * o + 4 * q
+                nc.sync.dma_start(w_plane[o][32 * q : 32 * q + 4, :].bitcast(I32), picked_scales[row : row + 4, :].bitcast(I32))
+
+        move_scales(0)
         load_x(1)
+        move_scales(1)
         nc.sync.dma_start(wt_sb[:], wt[0].rearrange("(p t) one -> p (t one)", t=PACK))
         y_rows = y[0].rearrange("(p t) i -> p t i", t=PACK)
-        w_plane[0] = keep.tile([P, N], U8, name="w_plane0", align_bytes=64)
-        nc.vector.tensor_copy(w_plane[0][:], table_scales[:].indirect(offsets[:]))
 
         def load_y(h, t0, t1):
             nc.sync.dma_start(y_raw[h, t0][:], y_rows[:, t0:t1, h * HALF : (h + 1) * HALF])
-
-        load_y(*Y_LOADS[0])
-        nc.sync.dma_start(w_plane[1][0 : P - 16, :].bitcast(I32), w_plane[0][16:P, :].bitcast(I32))
-        load_y(*Y_LOADS[1])
 
         word_pairs = keep.tile([P, N], U32, name="word_pairs", align_bytes=64)
         w_codes = [keep.tile([P, 2 * N], U8, name="w_codes%d" % o, tag="w_codes%d" % o, align_bytes=64) for o in range(1)]
@@ -118,16 +130,23 @@ def tile_attend_gnce_w_kernel(tc, xT, w_words, w_scales, y, wt, xm, offs, out):
 
         nc.vector.tensor_copy(word_pairs[:], table_words[:].bitcast(U32).indirect(offsets[:]))
         part_words(0)
+        load_y(*Y_LOADS[0])
+        load_y(*Y_LOADS[1])
         xm_rows = xm[0].rearrange("(p j) d -> p j d", j=PACK)
-        for load, (k0, k1) in enumerate(XM_LOADS):
+
+        def load_xm(load):
+            k0, k1 = XM_LOADS[load]
             nc.sync.dma_start(xm_raw[load][:], xm_rows[:, :, k0 * P : k1 * P])
-            if load == 0:
-                load_y(*Y_LOADS[2])
-                load_y(*Y_LOADS[3])
+
+        load_xm(0)
+        load_y(*Y_LOADS[2])
 
         for t0 in (0, 2):
             round_x(nc.vector.tensor_copy, 0, t0, 0, SHARE)
             round_x(nc.scalar.copy, 0, t0, SHARE, P)
+        load_y(*Y_LOADS[3])
+        for load in range(1, len(XM_LOADS)):
+            load_xm(load)
         codes_tile(0, 0, "x_codes00")
         quantize_x(0, 0, 1)
         quantize_x(0, 1, 2)
@@ -163,7 +182,7 @@ def tile_attend_gnce_w_kernel(tc, xT, w_words, w_scales, y, wt, xm, offs, out):
             return y_raw[h, t0][:, t - t0, :]
 
         def weigh_y(h, t, on_scalar, tag):
-            wy[h, t] = keep.tile([P, HALF], F32, name="wy%d%d" % (h, t), tag=tag, align_bytes=64)[:]
+            wy[h, t] = tile([P, HALF], F32, "wy%d%d" % (h, t), tag)[:]
             if on_scalar:
                 nc.scalar.activation(wy[h, t], y_part(h, t), COPY, scale=wt_sb[:, t : t + 1])
             else:
@@ -175,7 +194,7 @@ def tile_attend_gnce_w_kernel(tc, xT, w_words, w_scales, y, wt, xm, offs, out):
         g_grouped = {}
 
         def sigmoid(h, tag):
-            prob[h] = keep.tile([P, PACK, HALF], F32, name="prob%d" % h, tag=tag, align_bytes=64)
+            prob[h] = tile([P, PACK, HALF], F32, "prob%d" % h, tag)
             for t in range(PACK):
                 nc.scalar.activation(prob[h][:, t, :], logits[t][:, halves[h]], SIGMOID)
 
@@ -206,7 +225,7 @@ def tile_attend_gnce_w_kernel(tc, xT, w_words, w_scales, y, wt, xm, offs, out):
 
         def round_xm(load, tag):
             k0, k1 = XM_LOADS[load]
-            xm_grouped[load] = keep.tile([P, (k1 - k0) * P, PACK], BF16, name="xm_grouped%d" % k0, tag=tag, align_bytes=64)
+            xm_grouped[load] = tile([P, (k1 - k0) * P, PACK], BF16, "xm_grouped%d" % k0, tag)
             for d0 in range(0, (k1 - k0) * P, P):
                 nc.scalar.copy(
                     xm_grouped[load][:, d0 : d0 + P, :].rearrange("p (c i) j -> p c j i", i=4),
@@ -240,7 +259,7 @@ def tile_attend_gnce_w_kernel(tc, xT, w_words, w_scales, y, wt, xm, offs, out):
             return dw
 
         def staging(name, width, tag):
-            return keep.tile([P, width], F32, name=name, tag=tag, align_bytes=64)
+            return tile([P, width], F32, name, tag)
 
         def place(k, dw, c0, c1, dw_sb):
             nc.scalar.copy(dw_sb, dw[:, c0:c1])
@@ -268,7 +287,7 @@ def tile_attend_gnce_w_kernel(tc, xT, w_words, w_scales, y, wt, xm, offs, out):
         early0 = multiply(0)
         weigh_y(1, 3, False, "prob0")
         gradient(1, (2, 3, 0, 1))
-        round_xm(1, "xm_raw0")
+        round_xm(1, "xm0")
         quantize_xm(1, "xm_codes1")
         place(0, early0, 0, HALF, staging("dw_early0", HALF, "dw_early0")[:])
         early1 = multiply(1)
@@ -279,13 +298,13 @@ def tile_attend_gnce_w_kernel(tc, xT, w_words, w_scales, y, wt, xm, offs, out):
         nc.gpsimd.memset(windows[2][:], 0.0)
         round_xm(2, "x_codes11")
         quantize_xm(2, "xm_codes2")
-        late = staging("dw_late", N, "xm_raw2")
+        late = staging("dw_late", N, "xm2")
         for k in range(2):
             place(k, multiply(k), HALF, N, late[:, k * HALF : (k + 1) * HALF])
             store(k)
         place_whole(2, ring.tile([P, N], F32, name="dw_sb", align_bytes=64))
         round_xm(3, "xm_codes2")
         quantize_xm(3, "xm_codes4")
-        place_whole(3, staging("dw_sb3", N, "xm_raw4"))
+        place_whole(3, staging("dw_sb3", N, "xm4"))
         for k in range(4, D_TILES):
             place_whole(k, ring.tile([P, N], F32, name="dw_sb", align_bytes=64))

@@ -29,9 +29,9 @@ Y_LOADS = ((0, 0, 2), (0, 2, 4), (1, 2, 4), (1, 0, 2))
 SHARE = 80
 SCALE_ROW0 = 96
 AT = {
-    "window1": 0, "table_scales": 8128, "wt": 8192, "x1": 8256,
-    "prob0": 16448, "table_words": 18496, "y00": 18496, "y02": 20544, "xm0": 22592, "y12": 24640,
-    "y10": 26688, "x0": 28672, "xm1": 28736, "xm2": 30784, "xm4": 34880,
+    "window1": 0, "table_scales": 8128, "wt": 8192, "y00": 8256, "prob0": 8256, "x1": 12352,
+    "table_words": 20544, "y02": 20544, "xm0": 22592, "y12": 24640, "y10": 26688,
+    "x0": 28736, "xm1": 28736, "xm2": 30784, "xm4": 34880,
 }
 XM_LOADS = ((0, 1), (1, 2), (2, 4), (4, 8))
 
@@ -53,7 +53,7 @@ def tile_attend_gnce_w_kernel(tc, xT, w_words, w_scales, y, wt, xm, offs, out):
             return keep.tile(shape, dtype, name=name, tag=tag, align_bytes=64)
 
         table_words = tile([P, T], I32, "table_words", "table_words")
-        table_scales = tile([P, T], U8, "table_scales", "table_scales")
+        table_scales = tile([P, 4352], U8, "table_scales", "table_scales")[:, :T]
         x_raw = [tile([P, PACK, R], F32, "x_raw%d" % o, "x%d" % o) for o in range(PASSES)]
         y_raw = {(h, t0): tile([P, t1 - t0, HALF], F32, "y_raw%d%d" % (h, t0), "y%d%d" % (h, t0)) for h, t0, t1 in Y_LOADS}
         wt_sb = tile([P, PACK], F32, "wt_sb", "wt")
@@ -83,7 +83,7 @@ def tile_attend_gnce_w_kernel(tc, xT, w_words, w_scales, y, wt, xm, offs, out):
         nc.sync.dma_start(table_words[:], words)
         load_x(0)
         picked_scales = keep.tile([P, N], U8, name="picked_scales", align_bytes=64)
-        nc.vector.tensor_copy(picked_scales[:], table_scales[:].indirect(offsets[:]))
+        nc.vector.tensor_copy(picked_scales[:], table_scales.indirect(offsets[:]))
         nc.vector.memset(windows[1][:], 0.0)
 
         def move_scales(o):
@@ -93,12 +93,14 @@ def tile_attend_gnce_w_kernel(tc, xT, w_words, w_scales, y, wt, xm, offs, out):
 
         move_scales(0)
         load_x(1)
-        move_scales(1)
         nc.sync.dma_start(wt_sb[:], wt[0].rearrange("(p t) one -> p (t one)", t=PACK))
         y_rows = y[0].rearrange("(p t) i -> p t i", t=PACK)
 
         def load_y(h, t0, t1):
             nc.sync.dma_start(y_raw[h, t0][:], y_rows[:, t0:t1, h * HALF : (h + 1) * HALF])
+
+        load_y(*Y_LOADS[0])
+        move_scales(1)
 
         word_pairs = keep.tile([P, N], U32, name="word_pairs", align_bytes=64)
         w_codes = [keep.tile([P, 2 * N], U8, name="w_codes%d" % o, tag="w_codes%d" % o, align_bytes=64) for o in range(1)]
@@ -130,7 +132,6 @@ def tile_attend_gnce_w_kernel(tc, xT, w_words, w_scales, y, wt, xm, offs, out):
 
         nc.vector.tensor_copy(word_pairs[:], table_words[:].bitcast(U32).indirect(offsets[:]))
         part_words(0)
-        load_y(*Y_LOADS[0])
         load_y(*Y_LOADS[1])
         xm_rows = xm[0].rearrange("(p j) d -> p j d", j=PACK)
 
@@ -140,11 +141,11 @@ def tile_attend_gnce_w_kernel(tc, xT, w_words, w_scales, y, wt, xm, offs, out):
 
         load_xm(0)
         load_y(*Y_LOADS[2])
+        load_y(*Y_LOADS[3])
 
         for t0 in (0, 2):
             round_x(nc.vector.tensor_copy, 0, t0, 0, SHARE)
             round_x(nc.scalar.copy, 0, t0, SHARE, P)
-        load_y(*Y_LOADS[3])
         for load in range(1, len(XM_LOADS)):
             load_xm(load)
         codes_tile(0, 0, "x_codes00")

@@ -29,7 +29,7 @@ Y_LOADS = ((0, 0, 2), (0, 2, 4), (1, 2, 4), (1, 0, 2))
 SHARE = 80
 SCALE_ROW0 = 96
 AT = {
-    "window1": 0, "table_scales": 8128, "wt": 8192, "y00": 8256, "prob0": 8256, "x1": 12352,
+    "window1": 0, "table_scales": 8128, "y00": 8256, "prob0": 8256, "x1": 12352,
     "table_words": 20544, "y02": 20544, "xm0": 22592, "y12": 24640, "y10": 26688,
     "x0": 28736, "xm1": 28736, "xm2": 30784, "xm4": 34880,
 }
@@ -82,6 +82,7 @@ def tile_attend_gnce_w_kernel(tc, xT, w_words, w_scales, y, wt, xm, offs, out):
         nc.sync.dma_start(offsets[:], offs)
         nc.sync.dma_start(table_words[:], words)
         load_x(0)
+        nc.sync.dma_start(wt_sb[:], wt[0].rearrange("(p t) one -> p (t one)", t=PACK))
         picked_scales = keep.tile([P, N], U8, name="picked_scales", align_bytes=64)
         nc.vector.tensor_copy(picked_scales[:], table_scales.indirect(offsets[:]))
         nc.vector.memset(windows[1][:], 0.0)
@@ -89,11 +90,11 @@ def tile_attend_gnce_w_kernel(tc, xT, w_words, w_scales, y, wt, xm, offs, out):
         def move_scales(o):
             for q in range(4):
                 row = SCALE_ROW0 + 16 * o + 4 * q
-                nc.sync.dma_start(w_plane[o][32 * q : 32 * q + 4, :].bitcast(I32), picked_scales[row : row + 4, :].bitcast(I32))
+                queue = nc.scalar if o == 0 and q % 2 else nc.sync
+                queue.dma_start(w_plane[o][32 * q : 32 * q + 4, :].bitcast(I32), picked_scales[row : row + 4, :].bitcast(I32))
 
         move_scales(0)
         load_x(1)
-        nc.sync.dma_start(wt_sb[:], wt[0].rearrange("(p t) one -> p (t one)", t=PACK))
         y_rows = y[0].rearrange("(p t) i -> p t i", t=PACK)
 
         def load_y(h, t0, t1):

@@ -15,6 +15,7 @@ E4M3 = mybir.dt.float8_e4m3fn_x4
 E5M2 = mybir.dt.float8_e5m2_x4
 E2M1 = mybir.dt.float4_e2m1fn_x4
 MULT = mybir.AluOpType.mult
+ADD = mybir.AluOpType.add
 SUBTRACT = mybir.AluOpType.subtract
 COPY = mybir.ActivationFunctionType.Copy
 SIGMOID = mybir.ActivationFunctionType.Sigmoid
@@ -23,17 +24,18 @@ P = 128
 PACK = 4
 PASSES = D // (P * PACK)
 D_TILES = D // P
-WINDOWS = 3
+WINDOWS = 4
 HALF = N // 2
-Y_LOADS = ((0, 0, 2), (0, 2, 4), (1, 2, 4), (1, 0, 2))
+HALVES = (slice(0, HALF), slice(HALF, N))
 SHARE = 80
-SCALE_ROW0 = 96
+HEAD = 1024
+XM_LOADS = ((0, 1), (1, 2), (2, 8))
+LAST_WINDOW_CUTS = (0, 640, 1280, 1920, T)
 AT = {
-    "window1": 0, "table_scales": 8128, "y00": 8256, "prob0": 8256, "x1": 12352,
-    "table_words": 20544, "y02": 20544, "xm0": 22592, "y12": 24640, "y10": 26688,
-    "x0": 28736, "xm1": 28736, "xm2": 30784, "xm4": 34880,
+    "window3": 0, "g_grouped1": 8128, "xm_grouped2": 8192, "dw1b": 8192, "xm_grouped4": 10176, "xm_grouped6": 12160,
+    "xm_raw2": 14336, "table_words": 26560, "y_raw1": 26624, "xm_raw0": 30720, "xm_raw1": 32768,
+    "table_scales": 34816, "y_raw0": 34816,
 }
-XM_LOADS = ((0, 1), (1, 2), (2, 4), (4, 8))
 
 
 def tile_attend_gnce_w_kernel(tc, xT, w_words, w_scales, y, wt, xm, offs, out):
@@ -41,272 +43,240 @@ def tile_attend_gnce_w_kernel(tc, xT, w_words, w_scales, y, wt, xm, offs, out):
     with ExitStack() as ctx:
         keep = ctx.enter_context(tc.tile_pool(name="keep", bufs=1))
         reuse = ctx.enter_context(tc.tile_pool(name="reuse", bufs=1))
-        ring = ctx.enter_context(tc.tile_pool(name="ring", bufs=3))
-        psum_a = ctx.enter_context(tc.psum_pool(name="psum_a", bufs=1))
-        psum_dw = ctx.enter_context(tc.psum_pool(name="psum_dw", bufs=4))
+        psum = ctx.enter_context(tc.psum_pool(name="psum", bufs=1))
+
+        def tile(shape, dtype, name):
+            if name in AT:
+                return reuse.tile(shape, dtype, name=name, align_bytes=64, offset=AT[name])
+            return keep.tile(shape, dtype, name=name, align_bytes=64)
+
+        def zero_odd(view):
+            cut = view.shape[1] // 2 + 1
+            nc.vector.memset(view[:, :cut], 0)
+            nc.vector.memset(view[:, cut:], 0)
 
         offsets = keep.tile([P, N // 16], U16, name="offsets")
-
-        def tile(shape, dtype, name, tag):
-            if tag in AT:
-                return reuse.tile(shape, dtype, name=name, tag=tag, align_bytes=64, offset=AT[tag])
-            return keep.tile(shape, dtype, name=name, tag=tag, align_bytes=64)
-
-        table_words = tile([P, T], I32, "table_words", "table_words")
-        table_scales = tile([P, 4352], U8, "table_scales", "table_scales")[:, :T]
-        x_raw = [tile([P, PACK, R], F32, "x_raw%d" % o, "x%d" % o) for o in range(PASSES)]
-        y_raw = {(h, t0): tile([P, t1 - t0, HALF], F32, "y_raw%d%d" % (h, t0), "y%d%d" % (h, t0)) for h, t0, t1 in Y_LOADS}
-        wt_sb = tile([P, PACK], F32, "wt_sb", "wt")
-        xm_raw = [tile([P, PACK, (k1 - k0) * P], F32, "xm_raw%d" % k0, "xm%d" % k0) for k0, k1 in XM_LOADS]
-        windows = [tile([P, T], F32, "window%d" % k, "window%d" % k) for k in range(WINDOWS - 1)]
-
+        table_words = tile([P, T], I32, "table_words")
+        table_scales = tile([P, T], U8, "table_scales")
+        w_plane1 = tile([P, N], U8, "w_plane1")
+        windows = [tile([P, T], F32, "window%d" % k) for k in range(WINDOWS - 1)]
         warm_in = keep.tile([P, 1], F32, name="warm_in")
         warm_out = keep.tile([P, 1], F32, name="warm_out")
-        nc.vector.memset(table_scales[0:SCALE_ROW0, :].bitcast(I32), 0)
+
+        zero_odd(table_scales[:].bitcast(I32))
         nc.vector.memset(warm_in[:], 0.0)
         nc.scalar.activation(warm_out[:], warm_in[:], SIGMOID)
-        w_plane = [keep.tile([P, N], U8, name="w_plane%d" % o, tag="w_plane%d" % o, align_bytes=64) for o in range(PASSES)]
-        g_codes = keep.tile([P, N], I32, name="g_codes", align_bytes=64)
-        g_plane = keep.tile([P, N], U8, name="g_plane", align_bytes=64)
-        for plane in w_plane:
-            nc.vector.memset(plane[:].bitcast(I32), 0)
-        nc.vector.memset(g_codes[:, HALF:], 0)
-        nc.vector.memset(g_plane[:, HALF:].bitcast(I32), 0)
-        nc.vector.memset(windows[0][:], 0.0)
+        zero_odd(w_plane1[96:P, :].bitcast(I32))
+        zero_odd(windows[2][:])
+        nc.gpsimd.memset(windows[0][:], 0.0)
+        nc.gpsimd.memset(windows[1][:], 0.0)
 
-        def load_x(o):
-            nc.sync.dma_start(x_raw[o][:], xT[0, 512 * o : 512 * (o + 1), :].rearrange("(p j) r -> p j r", j=PACK))
-
+        x_raw = [tile([P, PACK, R], F32, "x_raw%d" % o) for o in range(PASSES)]
+        y_raw = {}
+        wt_sb = tile([P, PACK], F32, "wt_sb")
         words = w_words[0].rearrange("p t b -> p (t b)").bitcast(I32)
-        nc.sync.dma_start(table_scales[SCALE_ROW0:P, :].bitcast(I32), w_scales.rearrange("o f t -> (o f) t").bitcast(I32))
-        nc.sync.dma_start(offsets[:], offs)
-        nc.sync.dma_start(table_words[:], words)
-        load_x(0)
-        nc.sync.dma_start(wt_sb[:], wt[0].rearrange("(p t) one -> p (t one)", t=PACK))
-        picked_scales = keep.tile([P, N], U8, name="picked_scales", align_bytes=64)
-        nc.vector.tensor_copy(picked_scales[:], table_scales.indirect(offsets[:]))
-        nc.vector.memset(windows[1][:], 0.0)
-
-        def move_scales(o):
-            for q in range(4):
-                row = SCALE_ROW0 + 16 * o + 4 * q
-                queue = nc.scalar if o == 0 and q % 2 else nc.sync
-                queue.dma_start(w_plane[o][32 * q : 32 * q + 4, :].bitcast(I32), picked_scales[row : row + 4, :].bitcast(I32))
-
-        move_scales(0)
-        load_x(1)
+        scale_rows = w_scales.rearrange("o (q f) t -> f q o t", f=4).bitcast(I32)
         y_rows = y[0].rearrange("(p t) i -> p t i", t=PACK)
+        xm_rows = xm[0].rearrange("(p j) d -> p j d", j=PACK)
+        xm_raw = {}
 
-        def load_y(h, t0, t1):
-            nc.sync.dma_start(y_raw[h, t0][:], y_rows[:, t0:t1, h * HALF : (h + 1) * HALF])
+        def load_xm(k0, k1):
+            xm_raw[k0] = tile([P, PACK, (k1 - k0) * P], F32, "xm_raw%d" % k0)
+            nc.sync.dma_start(xm_raw[k0][:], xm_rows[:, :, k0 * P : k1 * P])
 
-        load_y(*Y_LOADS[0])
-        move_scales(1)
+        nc.sync.dma_start(offsets[:], offs)
+        nc.sync.dma_start(table_words[:, :HEAD], words[:, :HEAD])
+        for f in range(4):
+            nc.sync.dma_start(table_scales[f:P:16, :].bitcast(I32), scale_rows[f])
+        nc.sync.dma_start(table_words[:, HEAD:], words[:, HEAD:])
+        for o in range(PASSES):
+            nc.sync.dma_start(x_raw[o][:], xT[0, 512 * o : 512 * (o + 1), :].rearrange("(p j) r -> p j r", j=PACK))
+        nc.sync.dma_start(wt_sb[:], wt[0].rearrange("(p t) one -> p (t one)", t=PACK))
 
-        word_pairs = keep.tile([P, N], U32, name="word_pairs", align_bytes=64)
-        w_codes = [keep.tile([P, 2 * N], U8, name="w_codes%d" % o, tag="w_codes%d" % o, align_bytes=64) for o in range(1)]
+        def load_y(pair):
+            y_raw[pair] = tile([P, 2, N], F32, "y_raw%d" % pair)
+            nc.sync.dma_start(y_raw[pair][:], y_rows[:, 2 * pair : 2 * pair + 2, :])
 
-        def part_words(o):
+        picked_scales = tile([P, N], U8, "picked_scales")
+        nc.vector.tensor_copy(picked_scales[:], table_scales[:].indirect(offsets[:]))
+        nc.scalar.dma_start(w_plane1[0 : P - 16, :].bitcast(I32), picked_scales[16:P, :].bitcast(I32))
+        w_plane = (picked_scales, w_plane1)
+        load_y(0)
+        word_pairs = tile([P, N], U32, "word_pairs")
+        nc.vector.tensor_copy(word_pairs[:], table_words[:].bitcast(U32).indirect(offsets[:]))
+        load_y(1)
+        for k0, k1 in XM_LOADS:
+            load_xm(k0, k1)
+        w_codes = [tile([P, 2 * N], U8, "w_codes%d" % o) for o in range(PASSES)]
+        for o in range(PASSES):
             nc.vector.tensor_copy(w_codes[o][:].bitcast(U16), word_pairs[:].bitcast(U16)[:, o : 2 * N : PASSES])
 
-        x_grouped = {}
-        x_codes = {}
-        x_plane = [keep.tile([P, PACK, P], U8, name="x_plane%d" % o, align_bytes=64) for o in range(PASSES)]
+        logits = {(h, t): psum.tile([P, HALF], F32, name="logits%d%d" % (h, t), tag="bank%d" % (PACK * h + t)) for h in range(2) for t in range(PACK)}
 
-        def round_x(copy, o, t0, m0, m1):
-            if (o, t0 // 2) not in x_grouped:
-                x_grouped[o, t0 // 2] = keep.tile([P, 2, P, PACK], BF16, name="x_grouped%d%d" % (o, t0), tag="x_grouped%d%d" % (o, t0), align_bytes=64)
-            copy(
-                x_grouped[o, t0 // 2][:].rearrange("p t m j -> p m j t")[:, m0:m1],
-                x_raw[o][:].rearrange("p j (m t) -> p m j t", t=PACK)[:, m0:m1, :, t0 : t0 + 2],
-            )
+        def scores(o):
+            x_grouped = [tile([P, 2, P, PACK], BF16, "x_grouped%d%d" % (o, pair)) for pair in range(2)]
+            x_codes = [tile([P, 2, P], U32, "x_codes%d%d" % (o, pair)) for pair in range(2)]
+            x_plane = [tile([P, 2, P], U8, "x_plane%d%d" % (o, pair)) for pair in range(2)]
+            for pair in range(2):
+                for copy, m0, m1 in ((nc.vector.tensor_copy, 0, SHARE), (nc.scalar.copy, SHARE, P)):
+                    copy(
+                        x_grouped[pair][:].rearrange("p t m j -> p m j t")[:, m0:m1],
+                        x_raw[o][:].rearrange("p j (m t) -> p m j t", t=PACK)[:, m0:m1, :, 2 * pair : 2 * pair + 2],
+                    )
+            for pair, u0, u1 in ((0, 0, 1), (0, 1, 2), (1, 0, 2)):
+                nc.vector.quantize_mx(
+                    out=x_codes[pair][:, u0:u1, :].rearrange("p t m -> p (t m)").bitcast(E4M3),
+                    scales=x_plane[pair][:, u0:u1, :].rearrange("p t m -> p (t m)"),
+                    in_=x_grouped[pair][:, u0:u1].rearrange("p t m j -> p (t m j)"),
+                )
+            for h in range(2):
+                for t in range(PACK):
+                    nc.tensor.matmul_mx(
+                        out=logits[h, t][:],
+                        lhsT=x_codes[t // 2][:, t % 2, :].bitcast(E4M3),
+                        lhsT_scale=x_plane[t // 2][:, t % 2, :],
+                        rhs=w_codes[o][:, 2 * HALF * h : 2 * HALF * (h + 1)].bitcast(E2M1),
+                        rhs_scale=w_plane[o][:, HALVES[h]],
+                        start=(o == 0),
+                        stop=(o == PASSES - 1),
+                    )
 
-        def codes_tile(o, pair, tag):
-            x_codes[o, pair] = keep.tile([P, 2, P], U32, name="x_codes%d%d" % (o, pair), tag=tag, align_bytes=64)
+        for o in range(PASSES):
+            scores(o)
 
-        def quantize_x(o, t0, t1):
-            nc.vector.quantize_mx(
-                out=x_codes[o, t0 // 2][:, t0 % 2 : t0 % 2 + t1 - t0, :].rearrange("p t m -> p (t m)").bitcast(E4M3),
-                scales=x_plane[o][:, t0:t1, :].rearrange("p t m -> p (t m)"),
-                in_=x_grouped[o, t0 // 2][:, t0 % 2 : t0 % 2 + t1 - t0].rearrange("p t m j -> p (t m j)"),
-            )
+        wy = [tile([P, N], F32, "wy%d" % t) for t in range(PACK)]
+        nc.scalar.activation(wy[0][:], y_raw[0][:, 0, :], COPY, scale=wt_sb[:, 0:1])
+        for t in range(1, PACK):
+            nc.vector.tensor_scalar(wy[t][:], y_raw[t // 2][:, t % 2, :], wt_sb[:, t : t + 1], None, MULT)
 
-        nc.vector.tensor_copy(word_pairs[:], table_words[:].bitcast(U32).indirect(offsets[:]))
-        part_words(0)
-        load_y(*Y_LOADS[1])
-        xm_rows = xm[0].rearrange("(p j) d -> p j d", j=PACK)
-
-        def load_xm(load):
-            k0, k1 = XM_LOADS[load]
-            nc.sync.dma_start(xm_raw[load][:], xm_rows[:, :, k0 * P : k1 * P])
-
-        load_xm(0)
-        load_y(*Y_LOADS[2])
-        load_y(*Y_LOADS[3])
-
-        for t0 in (0, 2):
-            round_x(nc.vector.tensor_copy, 0, t0, 0, SHARE)
-            round_x(nc.scalar.copy, 0, t0, SHARE, P)
-        for load in range(1, len(XM_LOADS)):
-            load_xm(load)
-        codes_tile(0, 0, "x_codes00")
-        quantize_x(0, 0, 1)
-        quantize_x(0, 1, 2)
-        w_codes.append(keep.tile([P, 2 * N], U8, name="w_codes1", tag="x_grouped00", align_bytes=64))
-        part_words(1)
-        codes_tile(0, 1, "x_codes01")
-        quantize_x(0, 2, 4)
-        for t0 in (0, 2):
-            round_x(nc.vector.tensor_copy, 1, t0, 0, SHARE)
-            round_x(nc.scalar.copy, 1, t0, SHARE, P)
-        codes_tile(1, 0, "x_codes10")
-        quantize_x(1, 0, 1)
-        quantize_x(1, 1, 2)
-        codes_tile(1, 1, "x_codes11")
-        quantize_x(1, 2, 4)
-
-        logits = [psum_a.tile([P, N], F32, name="logits%d" % t) for t in range(PACK)]
-        for o, t in [(o, t) for o in range(PASSES) for t in range(PACK)]:
-            nc.tensor.matmul_mx(
-                out=logits[t][:],
-                lhsT=x_codes[o, t // 2][:, t % 2, :].bitcast(E4M3),
-                lhsT_scale=x_plane[o][:, t, :],
-                rhs=w_codes[o][:].bitcast(E2M1),
-                rhs_scale=w_plane[o][:],
-                start=(o == 0),
-                stop=(o == PASSES - 1),
-            )
-
-        wy = {}
-
-        def y_part(h, t):
-            t0 = max(first for half, first, last in Y_LOADS if half == h and first <= t)
-            return y_raw[h, t0][:, t - t0, :]
-
-        def weigh_y(h, t, on_scalar, tag):
-            wy[h, t] = tile([P, HALF], F32, "wy%d%d" % (h, t), tag)[:]
-            if on_scalar:
-                nc.scalar.activation(wy[h, t], y_part(h, t), COPY, scale=wt_sb[:, t : t + 1])
-            else:
-                nc.vector.tensor_scalar(wy[h, t], y_part(h, t), wt_sb[:, t : t + 1], None, MULT)
-
-        halves = (slice(0, HALF), slice(HALF, N))
+        g_codes = tile([P, N], U32, "g_codes")
+        g_plane = tile([P, N], U8, "g_plane")
         prob = {}
-        g_rows = {}
         g_grouped = {}
 
-        def sigmoid(h, tag):
-            prob[h] = tile([P, PACK, HALF], F32, "prob%d" % h, tag)
+        def sigmoid(h):
             for t in range(PACK):
-                nc.scalar.activation(prob[h][:, t, :], logits[t][:, halves[h]], SIGMOID)
+                prob[h, t] = tile([P, HALF], F32, "prob%d%d" % (h, t))
+                nc.scalar.activation(prob[h, t][:], logits[h, t][:], SIGMOID)
 
-        def gradient(h, order):
-            g_rows[h] = keep.tile([P, PACK, HALF], BF16, name="g_rows%d" % h, tag="g_rows", align_bytes=64)
-            for t in order:
+        def gradient(h):
+            g_rows = tile([P, PACK, HALF], BF16, "g_rows%d" % h)
+            for t in range(PACK):
                 nc.vector.scalar_tensor_tensor(
-                    g_rows[h][:, t, :], prob[h][:, t, :], wt_sb[:, t : t + 1], wy[h, t], MULT, SUBTRACT
+                    g_rows[:, t, :], prob[h, t][:], wt_sb[:, t : t + 1], wy[t][:, HALVES[h]], MULT, SUBTRACT
                 )
-
-        def interleave_g(copy, h):
-            g_grouped[h] = keep.tile([P, HALF, PACK], BF16, name="g_grouped%d" % h, align_bytes=64)
-            copy(
+            g_grouped[h] = tile([P, HALF, PACK], BF16, "g_grouped%d" % h)
+            nc.vector.tensor_copy(
                 g_grouped[h][:].rearrange("p (c i) t -> p c t i", i=4),
-                g_rows[h][:].rearrange("p t (c i) -> p c t i", i=4),
+                g_rows[:].rearrange("p t (c i) -> p c t i", i=4),
             )
 
         def quantize_g(h):
             nc.vector.quantize_mx(
-                out=g_codes[:, halves[h]].bitcast(E5M2),
-                scales=g_plane[:, halves[h]],
+                out=g_codes[:, HALVES[h]].bitcast(E5M2),
+                scales=g_plane[:, HALVES[h]],
                 in_=g_grouped[h][:].rearrange("p i t -> p (i t)"),
             )
 
+        xm_grouped = {}
         xm_codes = {}
         xm_plane = {}
-        xm_grouped = {}
 
-        def round_xm(load, tag):
-            k0, k1 = XM_LOADS[load]
-            xm_grouped[load] = tile([P, (k1 - k0) * P, PACK], BF16, "xm_grouped%d" % k0, tag)
-            for d0 in range(0, (k1 - k0) * P, P):
-                nc.scalar.copy(
-                    xm_grouped[load][:, d0 : d0 + P, :].rearrange("p (c i) j -> p c j i", i=4),
-                    xm_raw[load][:, :, d0 : d0 + P].rearrange("p j (c i) -> p c j i", i=4),
+        def gpsimd_round(dst, src):
+            nc.gpsimd.tensor_scalar(dst.rearrange("p c j i -> p c i j"), src.rearrange("p c j i -> p c i j"), 1.0, 0.0, MULT, ADD)
+
+        def round_xm(copy, k0, k1):
+            xm_grouped[k0] = tile([P, (k1 - k0) * P, PACK], BF16, "xm_grouped%d" % k0)
+            for k in range(k0, k1):
+                first = max(a for a, b in XM_LOADS if a <= k)
+                copy(
+                    xm_grouped[k0][:, (k - k0) * P : (k - k0 + 1) * P, :].rearrange("p (c i) j -> p c j i", i=4),
+                    xm_raw[first][:, :, (k - first) * P : (k - first + 1) * P].rearrange("p j (c i) -> p c j i", i=4),
                 )
 
-        def quantize_xm(load, tag):
-            k0, k1 = XM_LOADS[load]
-            codes = keep.tile([P, (k1 - k0) * P], U32, name="xm_codes%d" % k0, tag=tag, align_bytes=64)
-            plane = keep.tile([P, (k1 - k0) * P], U8, name="xm_plane%d" % k0, align_bytes=64)
+        def quantize_xm(k0, k1):
+            codes = tile([P, (k1 - k0) * P], U32, "xm_codes%d" % k0)
+            plane = tile([P, (k1 - k0) * P], U8, "xm_plane%d" % k0)
             nc.vector.quantize_mx(
-                out=codes[:].bitcast(E4M3),
-                scales=plane[:],
-                in_=xm_grouped[load][:].rearrange("p d j -> p (d j)"),
+                out=codes[:].bitcast(E4M3), scales=plane[:], in_=xm_grouped[k0][:].rearrange("p d j -> p (d j)")
             )
             for k in range(k0, k1):
                 xm_codes[k] = codes[:, (k - k0) * P : (k - k0 + 1) * P]
                 xm_plane[k] = plane[:, (k - k0) * P : (k - k0 + 1) * P]
 
-        def multiply(k):
-            dw = psum_dw.tile([P, N], F32, name="dw")
+        dw = {}
+
+        def multiply(k, cols):
+            if k not in dw:
+                dw[k] = psum.tile([P, N], F32, name="dw%d" % k, tag="bank%d" % k)
             nc.tensor.matmul_mx(
-                out=dw[:],
+                out=dw[k][:, cols],
                 lhsT=xm_codes[k].bitcast(E4M3),
                 lhsT_scale=xm_plane[k],
-                rhs=g_codes[:].bitcast(E5M2),
-                rhs_scale=g_plane[:],
+                rhs=g_codes[:, cols].bitcast(E5M2),
+                rhs_scale=g_plane[:, cols],
                 start=True,
                 stop=True,
             )
-            return dw
 
-        def staging(name, width, tag):
-            return tile([P, width], F32, name, tag)
-
-        def place(k, dw, c0, c1, dw_sb):
-            nc.scalar.copy(dw_sb, dw[:, c0:c1])
-            nc.vector.tensor_copy(windows[k % WINDOWS][:].indirect(offsets[:, c0 // 16 : c1 // 16]), dw_sb)
-
-        def place_whole(k, dw_sb):
-            place(k, multiply(k), 0, N, dw_sb[:])
-            store(k)
+        def place(k, cols, name):
+            staged = tile([P, cols.stop - cols.start], F32, name)
+            window = windows[k % WINDOWS]
+            if k % 2:
+                nc.vector.tensor_copy(staged[:], dw[k][:, cols])
+                nc.vector.tensor_copy(window[:].indirect(offsets[:, cols.start // 16 : cols.stop // 16]), staged[:])
+            else:
+                nc.scalar.copy(staged[:], dw[k][:, cols])
+                for c in range(cols.start, cols.stop, HALF):
+                    nc.scalar.activation(
+                        window[:].indirect(offsets[:, c // 16 : (c + HALF) // 16]),
+                        staged[:, c - cols.start : c - cols.start + HALF],
+                        COPY,
+                    )
 
         def store(k):
             nc.sync.dma_start(out[k * P : (k + 1) * P, :], windows[k % WINDOWS][:])
 
-        for t in range(PACK):
-            weigh_y(0, t, t < 2, "wy0%d" % t)
-        sigmoid(0, "prob0")
-        gradient(0, range(PACK))
-        round_xm(0, "x_grouped00")
-        sigmoid(1, "x_codes11")
-        weigh_y(1, 0, True, "w_plane1")
-        weigh_y(1, 1, True, "w_codes0")
-        weigh_y(1, 2, False, "wy02")
-        interleave_g(nc.vector.tensor_copy, 0)
-        quantize_xm(0, "wy03")
-        quantize_g(0)
-        early0 = multiply(0)
-        weigh_y(1, 3, False, "prob0")
-        gradient(1, (2, 3, 0, 1))
-        round_xm(1, "xm0")
-        quantize_xm(1, "xm_codes1")
-        place(0, early0, 0, HALF, staging("dw_early0", HALF, "dw_early0")[:])
-        early1 = multiply(1)
-        interleave_g(nc.scalar.copy, 1)
-        quantize_g(1)
-        place(1, early1, 0, HALF, staging("dw_early1", HALF, "dw_early1")[:])
-        windows.append(keep.tile([P, T], F32, name="window2", tag="dw_early1", align_bytes=64))
-        nc.gpsimd.memset(windows[2][:], 0.0)
-        round_xm(2, "x_codes11")
-        quantize_xm(2, "xm_codes2")
-        late = staging("dw_late", N, "xm2")
-        for k in range(2):
-            place(k, multiply(k), HALF, N, late[:, k * HALF : (k + 1) * HALF])
+        def whole_tile(k):
+            multiply(k, slice(0, N))
+            place(k, slice(0, N), "dw_sb%d" % k)
             store(k)
-        place_whole(2, ring.tile([P, N], F32, name="dw_sb", align_bytes=64))
-        round_xm(3, "xm_codes2")
-        quantize_xm(3, "xm_codes4")
-        place_whole(3, staging("dw_sb3", N, "xm4"))
-        for k in range(4, D_TILES):
-            place_whole(k, ring.tile([P, N], F32, name="dw_sb", align_bytes=64))
+
+        def zero_last_window(piece):
+            nc.gpsimd.memset(windows[3][:, LAST_WINDOW_CUTS[piece] : LAST_WINDOW_CUTS[piece + 1]], 0.0)
+
+        sigmoid(0)
+        round_xm(nc.scalar.copy, 0, 1)
+        sigmoid(1)
+        round_xm(nc.scalar.copy, 1, 2)
+        gradient(0)
+        quantize_xm(0, 1)
+        quantize_g(0)
+        multiply(0, HALVES[0])
+        place(0, HALVES[0], "dw0a")
+        gradient(1)
+        quantize_xm(1, 2)
+        multiply(1, HALVES[0])
+        quantize_g(1)
+        multiply(0, HALVES[1])
+        place(0, HALVES[1], "dw0b")
+        store(0)
+        multiply(1, HALVES[1])
+        round_xm(gpsimd_round, 2, 4)
+        windows.append(tile([P, T], F32, "window3"))
+        for piece in range(3):
+            zero_last_window(piece)
+        place(1, HALVES[0], "dw1a")
+        quantize_xm(2, 4)
+        place(1, HALVES[1], "dw1b")
+        store(1)
+        round_xm(gpsimd_round, 4, 6)
+        zero_last_window(3)
+        whole_tile(2)
+        quantize_xm(4, 6)
+        whole_tile(3)
+        round_xm(gpsimd_round, 6, 8)
+        whole_tile(4)
+        quantize_xm(6, 8)
+        for k in range(5, D_TILES):
+            whole_tile(k)

@@ -29,12 +29,17 @@ HALF = N // 2
 HALVES = (slice(0, HALF), slice(HALF, N))
 SHARE = 80
 HEAD = 1024
-XM_LOADS = ((0, 1), (1, 2), (2, 8))
-LAST_WINDOW_CUTS = (0, 640, 1280, 1920, T)
+XM_LOADS = ((0, 1), (1, 3), (3, 8))
+EARLY_CUT = 1536
 AT = {
-    "window3": 0, "g_grouped1": 8128, "xm_grouped2": 8192, "dw1b": 8192, "xm_grouped4": 10176, "xm_grouped6": 12160,
-    "xm_raw2": 14336, "table_words": 26560, "y_raw1": 26624, "xm_raw0": 30720, "xm_raw1": 32768,
-    "table_scales": 34816, "y_raw0": 34816,
+    "g_rows1": 0, "g_rows0": 1984, "xm_grouped1": 2048,
+    "g_grouped1": 4096, "xm_grouped3": 4096, "xm_grouped5": 4096,
+    "dw_sb4": 8192, "dw_sb6": 8192, "dw_sb70": 10240, "dw_sb51": 11200, "dw_sb71": 12160,
+    "table_words": 14336, "y_raw1": 14336,
+    "table_scales": 22528, "y_raw0": 22528,
+    "word_pairs": 26624, "xm_raw0": 26624, "prob1": 26624,
+    "x_raw0": 30720, "xm_raw1": 30720,
+    "x_grouped00": 38912, "xm_raw3": 38912,
 }
 
 
@@ -59,7 +64,7 @@ def tile_attend_gnce_w_kernel(tc, xT, w_words, w_scales, y, wt, xm, offs, out):
         table_words = tile([P, T], I32, "table_words")
         table_scales = tile([P, T], U8, "table_scales")
         w_plane1 = tile([P, N], U8, "w_plane1")
-        windows = [tile([P, T], F32, "window%d" % k) for k in range(WINDOWS - 1)]
+        windows = [tile([P, T], F32, "window%d" % k) for k in range(WINDOWS)]
         warm_in = keep.tile([P, 1], F32, name="warm_in")
         warm_out = keep.tile([P, 1], F32, name="warm_out")
 
@@ -68,8 +73,10 @@ def tile_attend_gnce_w_kernel(tc, xT, w_words, w_scales, y, wt, xm, offs, out):
         nc.scalar.activation(warm_out[:], warm_in[:], SIGMOID)
         zero_odd(w_plane1[96:P, :].bitcast(I32))
         zero_odd(windows[2][:])
+        zero_odd(windows[3][:, EARLY_CUT:])
         nc.gpsimd.memset(windows[0][:], 0.0)
         nc.gpsimd.memset(windows[1][:], 0.0)
+        nc.gpsimd.memset(windows[3][:, :EARLY_CUT], 0.0)
 
         x_raw = [tile([P, PACK, R], F32, "x_raw%d" % o) for o in range(PASSES)]
         y_raw = {}
@@ -105,8 +112,6 @@ def tile_attend_gnce_w_kernel(tc, xT, w_words, w_scales, y, wt, xm, offs, out):
         word_pairs = tile([P, N], U32, "word_pairs")
         nc.vector.tensor_copy(word_pairs[:], table_words[:].bitcast(U32).indirect(offsets[:]))
         load_y(1)
-        for k0, k1 in XM_LOADS:
-            load_xm(k0, k1)
         w_codes = [tile([P, 2 * N], U8, "w_codes%d" % o) for o in range(PASSES)]
         for o in range(PASSES):
             nc.vector.tensor_copy(w_codes[o][:].bitcast(U16), word_pairs[:].bitcast(U16)[:, o : 2 * N : PASSES])
@@ -141,8 +146,11 @@ def tile_attend_gnce_w_kernel(tc, xT, w_words, w_scales, y, wt, xm, offs, out):
                         stop=(o == PASSES - 1),
                     )
 
-        for o in range(PASSES):
-            scores(o)
+        load_xm(*XM_LOADS[0])
+        scores(0)
+        for k0, k1 in XM_LOADS[1:]:
+            load_xm(k0, k1)
+        scores(1)
 
         wy = [tile([P, N], F32, "wy%d" % t) for t in range(PACK)]
         nc.scalar.activation(wy[0][:], y_raw[0][:, 0, :], COPY, scale=wt_sb[:, 0:1])
@@ -155,15 +163,15 @@ def tile_attend_gnce_w_kernel(tc, xT, w_words, w_scales, y, wt, xm, offs, out):
         g_grouped = {}
 
         def sigmoid(h):
+            prob[h] = tile([P, PACK, HALF], F32, "prob%d" % h)
             for t in range(PACK):
-                prob[h, t] = tile([P, HALF], F32, "prob%d%d" % (h, t))
-                nc.scalar.activation(prob[h, t][:], logits[h, t][:], SIGMOID)
+                nc.scalar.activation(prob[h][:, t, :], logits[h, t][:], SIGMOID)
 
         def gradient(h):
             g_rows = tile([P, PACK, HALF], BF16, "g_rows%d" % h)
             for t in range(PACK):
                 nc.vector.scalar_tensor_tensor(
-                    g_rows[:, t, :], prob[h, t][:], wt_sb[:, t : t + 1], wy[t][:, HALVES[h]], MULT, SUBTRACT
+                    g_rows[:, t, :], prob[h][:, t, :], wt_sb[:, t : t + 1], wy[t][:, HALVES[h]], MULT, SUBTRACT
                 )
             g_grouped[h] = tile([P, HALF, PACK], BF16, "g_grouped%d" % h)
             nc.vector.tensor_copy(
@@ -186,11 +194,14 @@ def tile_attend_gnce_w_kernel(tc, xT, w_words, w_scales, y, wt, xm, offs, out):
             nc.gpsimd.tensor_scalar(dst.rearrange("p c j i -> p c i j"), src.rearrange("p c j i -> p c i j"), 1.0, 0.0, MULT, ADD)
 
         def round_xm(copy, k0, k1):
-            xm_grouped[k0] = tile([P, (k1 - k0) * P, PACK], BF16, "xm_grouped%d" % k0)
+            grouped = tile([P, (k1 - k0) * P, PACK], BF16, "xm_grouped%d" % k0)
+            for a in range(k0, k1, 2):
+                b = min(a + 2, k1)
+                xm_grouped[a, b] = grouped[:, (a - k0) * P : (b - k0) * P, :].rearrange("p d j -> p (d j)")
             for k in range(k0, k1):
                 first = max(a for a, b in XM_LOADS if a <= k)
                 copy(
-                    xm_grouped[k0][:, (k - k0) * P : (k - k0 + 1) * P, :].rearrange("p (c i) j -> p c j i", i=4),
+                    grouped[:, (k - k0) * P : (k - k0 + 1) * P, :].rearrange("p (c i) j -> p c j i", i=4),
                     xm_raw[first][:, :, (k - first) * P : (k - first + 1) * P].rearrange("p j (c i) -> p c j i", i=4),
                 )
 
@@ -198,7 +209,7 @@ def tile_attend_gnce_w_kernel(tc, xT, w_words, w_scales, y, wt, xm, offs, out):
             codes = tile([P, (k1 - k0) * P], U32, "xm_codes%d" % k0)
             plane = tile([P, (k1 - k0) * P], U8, "xm_plane%d" % k0)
             nc.vector.quantize_mx(
-                out=codes[:].bitcast(E4M3), scales=plane[:], in_=xm_grouped[k0][:].rearrange("p d j -> p (d j)")
+                out=codes[:].bitcast(E4M3), scales=plane[:], in_=xm_grouped[k0, k1]
             )
             for k in range(k0, k1):
                 xm_codes[k] = codes[:, (k - k0) * P : (k - k0 + 1) * P]
@@ -219,64 +230,58 @@ def tile_attend_gnce_w_kernel(tc, xT, w_words, w_scales, y, wt, xm, offs, out):
                 stop=True,
             )
 
-        def place(k, cols, name):
+        def place_vector(k, cols, name, between):
             staged = tile([P, cols.stop - cols.start], F32, name)
-            window = windows[k % WINDOWS]
-            if k % 2:
-                nc.vector.tensor_copy(staged[:], dw[k][:, cols])
-                nc.vector.tensor_copy(window[:].indirect(offsets[:, cols.start // 16 : cols.stop // 16]), staged[:])
-            else:
-                nc.scalar.copy(staged[:], dw[k][:, cols])
-                for c in range(cols.start, cols.stop, HALF):
-                    nc.scalar.activation(
-                        window[:].indirect(offsets[:, c // 16 : (c + HALF) // 16]),
-                        staged[:, c - cols.start : c - cols.start + HALF],
-                        COPY,
-                    )
+            nc.vector.tensor_copy(staged[:], dw[k][:, cols])
+            for k0, k1 in between:
+                quantize_xm(k0, k1)
+            nc.vector.tensor_copy(windows[k % WINDOWS][:].indirect(offsets[:, cols.start // 16 : cols.stop // 16]), staged[:])
+
+        def place_scalar(k, halves):
+            staged = {h: tile([P, HALF], F32, "dw_sb%d%d" % (k, h)) for h in halves}
+            for h in halves:
+                nc.scalar.copy(staged[h][:], dw[k][:, HALVES[h]])
+            for h in halves:
+                nc.scalar.activation(windows[k % WINDOWS][:].indirect(offsets[:, 16 * h : 16 * (h + 1)]), staged[h][:], COPY)
 
         def store(k):
             nc.sync.dma_start(out[k * P : (k + 1) * P, :], windows[k % WINDOWS][:])
 
-        def whole_tile(k):
-            multiply(k, slice(0, N))
-            place(k, slice(0, N), "dw_sb%d" % k)
-            store(k)
-
-        def zero_last_window(piece):
-            nc.gpsimd.memset(windows[3][:, LAST_WINDOW_CUTS[piece] : LAST_WINDOW_CUTS[piece + 1]], 0.0)
+        def whole(j0, j1):
+            for j in range(j0, j1):
+                multiply(j, slice(0, N))
 
         sigmoid(0)
         round_xm(nc.scalar.copy, 0, 1)
         sigmoid(1)
-        round_xm(nc.scalar.copy, 1, 2)
         gradient(0)
+        round_xm(nc.scalar.copy, 1, 3)
         quantize_xm(0, 1)
         quantize_g(0)
         multiply(0, HALVES[0])
-        place(0, HALVES[0], "dw0a")
+        place_scalar(0, (0,))
         gradient(1)
-        quantize_xm(1, 2)
-        multiply(1, HALVES[0])
+        quantize_xm(1, 3)
         quantize_g(1)
         multiply(0, HALVES[1])
-        place(0, HALVES[1], "dw0b")
+        whole(1, 3)
+        round_xm(gpsimd_round, 3, 5)
+        place_vector(0, HALVES[1], "dw0b", ())
         store(0)
-        multiply(1, HALVES[1])
-        round_xm(gpsimd_round, 2, 4)
-        windows.append(tile([P, T], F32, "window3"))
-        for piece in range(3):
-            zero_last_window(piece)
-        place(1, HALVES[0], "dw1a")
-        quantize_xm(2, 4)
-        place(1, HALVES[1], "dw1b")
+        place_scalar(1, (0, 1))
         store(1)
-        round_xm(gpsimd_round, 4, 6)
-        zero_last_window(3)
-        whole_tile(2)
-        quantize_xm(4, 6)
-        whole_tile(3)
-        round_xm(gpsimd_round, 6, 8)
-        whole_tile(4)
-        quantize_xm(6, 8)
-        for k in range(5, D_TILES):
-            whole_tile(k)
+        place_vector(2, slice(0, N), "dw_sb2", ((3, 5),))
+        store(2)
+        whole(3, 5)
+        round_xm(gpsimd_round, 5, 8)
+        place_scalar(3, (0, 1))
+        store(3)
+        place_vector(4, slice(0, N), "dw_sb4", ((5, 7), (7, 8)))
+        store(4)
+        whole(5, 8)
+        place_scalar(5, (0, 1))
+        store(5)
+        place_vector(6, slice(0, N), "dw_sb6", ())
+        store(6)
+        place_scalar(7, (0, 1))
+        store(7)

@@ -31,15 +31,19 @@ SHARE = 80
 HEAD = 1024
 XM_LOADS = ((0, 1), (1, 3), (3, 8))
 EARLY_CUT = 1536
+BANK_OF_TILE = (0, 1, 1, 3, 4, 5, 6, 7)
 AT = {
-    "g_rows1": 0, "g_rows0": 1984, "xm_grouped1": 2048,
-    "g_grouped1": 4096, "xm_grouped3": 4096, "xm_grouped5": 4096,
+    "g_rows1": 0, "g_rows0": 1984, "wy10": 2048, "wy11": 3072,
+    "g_grouped1": 4096, "xm_grouped2": 4096, "xm_grouped3": 4096, "xm_grouped5": 4096,
     "dw_sb4": 8192, "dw_sb6": 8192, "dw_sb70": 10240, "dw_sb51": 11200, "dw_sb71": 12160,
-    "table_words": 14336, "y_raw1": 14336,
-    "table_scales": 22528, "y_raw0": 22528,
-    "word_pairs": 26624, "xm_raw0": 26624, "prob1": 26624,
-    "x_raw0": 30720, "xm_raw1": 30720,
-    "x_grouped00": 38912, "xm_raw3": 38912,
+    "table_words": 13312, "y_raw0": 21440, "table_scales": 25472,
+    "x_raw0": 27520, "xm_raw0": 27520, "prob1": 27520,
+    "x_grouped00": 35712, "y_raw1": 35712,
+    "x_grouped01": 39808, "xm_raw1": 39808,
+    "x_codes00": 43904, "xm_raw3": 43904,
+    "x_grouped11": 54144, "w_codes11": 54144,
+    "wy01": 56192, "xm_grouped0": 56192,
+    "wy12": 57216, "wy02": 58176, "wy13": 59136, "xm_grouped1": 59136,
 }
 
 
@@ -100,21 +104,28 @@ def tile_attend_gnce_w_kernel(tc, xT, w_words, w_scales, y, wt, xm, offs, out):
             nc.sync.dma_start(x_raw[o][:], xT[0, 512 * o : 512 * (o + 1), :].rearrange("(p j) r -> p j r", j=PACK))
         nc.sync.dma_start(wt_sb[:], wt[0].rearrange("(p t) one -> p (t one)", t=PACK))
 
-        def load_y(pair):
-            y_raw[pair] = tile([P, 2, N], F32, "y_raw%d" % pair)
-            nc.sync.dma_start(y_raw[pair][:], y_rows[:, 2 * pair : 2 * pair + 2, :])
+        def load_y(h):
+            y_raw[h] = tile([P, PACK, HALF], F32, "y_raw%d" % h)
+            nc.sync.dma_start(y_raw[h][:], y_rows[:, :, HALVES[h]])
 
         picked_scales = tile([P, N], U8, "picked_scales")
         nc.vector.tensor_copy(picked_scales[:], table_scales[:].indirect(offsets[:]))
         nc.scalar.dma_start(w_plane1[0 : P - 16, :].bitcast(I32), picked_scales[16:P, :].bitcast(I32))
         w_plane = (picked_scales, w_plane1)
-        load_y(0)
         word_pairs = tile([P, N], U32, "word_pairs")
         nc.vector.tensor_copy(word_pairs[:], table_words[:].bitcast(U32).indirect(offsets[:]))
-        load_y(1)
-        w_codes = [tile([P, 2 * N], U8, "w_codes%d" % o) for o in range(PASSES)]
-        for o in range(PASSES):
-            nc.vector.tensor_copy(w_codes[o][:].bitcast(U16), word_pairs[:].bitcast(U16)[:, o : 2 * N : PASSES])
+        load_y(0)
+        w_codes = {}
+
+        def part_words(o, halves):
+            codes = tile([P, 2 * HALF * len(halves)], U8, "w_codes%d%d" % (o, halves[0]))
+            c0 = PASSES * HALF * halves[0]
+            nc.vector.tensor_copy(codes[:].bitcast(U16), word_pairs[:].bitcast(U16)[:, c0 + o : c0 + PASSES * HALF * len(halves) : PASSES])
+            for n, h in enumerate(halves):
+                w_codes[o, h] = codes[:, 2 * HALF * n : 2 * HALF * (n + 1)]
+
+        part_words(0, (0, 1))
+        part_words(1, (0,))
 
         logits = {(h, t): psum.tile([P, HALF], F32, name="logits%d%d" % (h, t), tag="bank%d" % (PACK * h + t)) for h in range(2) for t in range(PACK)}
 
@@ -135,27 +146,34 @@ def tile_attend_gnce_w_kernel(tc, xT, w_words, w_scales, y, wt, xm, offs, out):
                     in_=x_grouped[pair][:, u0:u1].rearrange("p t m j -> p (t m j)"),
                 )
             for h in range(2):
+                if (o, h) not in w_codes:
+                    part_words(o, (h,))
                 for t in range(PACK):
                     nc.tensor.matmul_mx(
                         out=logits[h, t][:],
                         lhsT=x_codes[t // 2][:, t % 2, :].bitcast(E4M3),
                         lhsT_scale=x_plane[t // 2][:, t % 2, :],
-                        rhs=w_codes[o][:, 2 * HALF * h : 2 * HALF * (h + 1)].bitcast(E2M1),
+                        rhs=w_codes[o, h].bitcast(E2M1),
                         rhs_scale=w_plane[o][:, HALVES[h]],
                         start=(o == 0),
                         stop=(o == PASSES - 1),
                     )
 
-        load_xm(*XM_LOADS[0])
         scores(0)
+        load_xm(*XM_LOADS[0])
+        load_y(1)
         for k0, k1 in XM_LOADS[1:]:
             load_xm(k0, k1)
         scores(1)
 
-        wy = [tile([P, N], F32, "wy%d" % t) for t in range(PACK)]
-        nc.scalar.activation(wy[0][:], y_raw[0][:, 0, :], COPY, scale=wt_sb[:, 0:1])
-        for t in range(1, PACK):
-            nc.vector.tensor_scalar(wy[t][:], y_raw[t // 2][:, t % 2, :], wt_sb[:, t : t + 1], None, MULT)
+        wy = {}
+
+        def weigh_y(h, t, on_scalar):
+            wy[h, t] = tile([P, HALF], F32, "wy%d%d" % (h, t))
+            if on_scalar:
+                nc.scalar.activation(wy[h, t][:], y_raw[h][:, t, :], COPY, scale=wt_sb[:, t : t + 1])
+            else:
+                nc.vector.tensor_scalar(wy[h, t][:], y_raw[h][:, t, :], wt_sb[:, t : t + 1], None, MULT)
 
         g_codes = tile([P, N], U32, "g_codes")
         g_plane = tile([P, N], U8, "g_plane")
@@ -171,7 +189,7 @@ def tile_attend_gnce_w_kernel(tc, xT, w_words, w_scales, y, wt, xm, offs, out):
             g_rows = tile([P, PACK, HALF], BF16, "g_rows%d" % h)
             for t in range(PACK):
                 nc.vector.scalar_tensor_tensor(
-                    g_rows[:, t, :], prob[h][:, t, :], wt_sb[:, t : t + 1], wy[t][:, HALVES[h]], MULT, SUBTRACT
+                    g_rows[:, t, :], prob[h][:, t, :], wt_sb[:, t : t + 1], wy[h, t][:], MULT, SUBTRACT
                 )
             g_grouped[h] = tile([P, HALF, PACK], BF16, "g_grouped%d" % h)
             nc.vector.tensor_copy(
@@ -219,7 +237,7 @@ def tile_attend_gnce_w_kernel(tc, xT, w_words, w_scales, y, wt, xm, offs, out):
 
         def multiply(k, cols):
             if k not in dw:
-                dw[k] = psum.tile([P, N], F32, name="dw%d" % k, tag="bank%d" % k)
+                dw[k] = psum.tile([P, N], F32, name="dw%d" % k, tag="bank%d" % BANK_OF_TILE[k])
             nc.tensor.matmul_mx(
                 out=dw[k][:, cols],
                 lhsT=xm_codes[k].bitcast(E4M3),
@@ -251,23 +269,29 @@ def tile_attend_gnce_w_kernel(tc, xT, w_words, w_scales, y, wt, xm, offs, out):
             for j in range(j0, j1):
                 multiply(j, slice(0, N))
 
+        for t in range(PACK):
+            weigh_y(0, t, t < 2)
         sigmoid(0)
+        gradient(0)
         round_xm(nc.scalar.copy, 0, 1)
         sigmoid(1)
-        gradient(0)
-        round_xm(nc.scalar.copy, 1, 3)
+        for t in range(PACK):
+            weigh_y(1, t, t < 2)
         quantize_xm(0, 1)
         quantize_g(0)
         multiply(0, HALVES[0])
-        place_scalar(0, (0,))
         gradient(1)
-        quantize_xm(1, 3)
+        round_xm(nc.scalar.copy, 1, 2)
+        place_scalar(0, (0,))
+        quantize_xm(1, 2)
         quantize_g(1)
         multiply(0, HALVES[1])
-        whole(1, 3)
-        round_xm(gpsimd_round, 3, 5)
-        place_vector(0, HALVES[1], "dw0b", ())
+        whole(1, 2)
+        round_xm(nc.vector.tensor_copy, 2, 3)
+        place_vector(0, HALVES[1], "dw0b", ((2, 3),))
         store(0)
+        whole(2, 3)
+        round_xm(gpsimd_round, 3, 5)
         place_scalar(1, (0, 1))
         store(1)
         place_vector(2, slice(0, N), "dw_sb2", ((3, 5),))

@@ -35,7 +35,7 @@ BANK_OF_TILE = (0, 1, 1, 3, 4, 5, 6, 7)
 AT = {
     "g_rows1": 0, "g_rows0": 1984, "wy10": 2048, "wy11": 3072,
     "g_grouped1": 4096, "xm_grouped2": 4096, "xm_grouped3": 4096, "xm_grouped5": 4096,
-    "dw_sb4": 8192, "dw_sb6": 8192, "dw_sb70": 10240, "dw_sb51": 11200, "dw_sb71": 12160,
+    "dw_sb6": 6208, "dw_sb4": 8192, "dw_sb7": 10176,
     "table_words": 13312, "y_raw0": 21440, "table_scales": 25472,
     "x_raw0": 27520, "xm_raw0": 27520, "prob1": 27520,
     "x_grouped00": 35712, "y_raw1": 35712,
@@ -305,7 +305,11 @@ def tile_attend_gnce_w_kernel(tc, xT, w_words, w_scales, y, wt, xm, offs, out):
         whole(5, 8)
         place_scalar(5, (0, 1))
         store(5)
-        place_vector(6, slice(0, N), "dw_sb6", ())
+        staged = {k: tile([P, N], F32, "dw_sb%d" % k) for k in (6, 7)}
+        for k in (6, 7):
+            nc.vector.tensor_copy(staged[k][:], dw[k][:])
+        nc.vector.tensor_copy(windows[6 % WINDOWS][:].indirect(offsets[:]), staged[6][:])
         store(6)
-        place_scalar(7, (0, 1))
+        for h in range(2):
+            nc.scalar.activation(windows[7 % WINDOWS][:].indirect(offsets[:, 16 * h : 16 * (h + 1)]), staged[7][:, HALVES[h]], COPY)
         store(7)

@@ -74,6 +74,8 @@ def tile_attend_gnce_w_kernel(tc, xT, w_words, w_scales, y, wt, xm, offs, out):
 
         zero_odd(table_scales[:].bitcast(I32))
         nc.vector.memset(warm_in[:], 0.0)
+        unit = keep.tile([P, 1], F32, name="unit")
+        nc.vector.memset(unit[:], 1.0)
         nc.scalar.activation(warm_out[:], warm_in[:], SIGMOID)
         zero_odd(w_plane1[96:P, :].bitcast(I32))
         zero_odd(windows[2][:])
@@ -262,6 +264,11 @@ def tile_attend_gnce_w_kernel(tc, xT, w_words, w_scales, y, wt, xm, offs, out):
             for h in halves:
                 nc.scalar.activation(windows[k % WINDOWS][:].indirect(offsets[:, 16 * h : 16 * (h + 1)]), staged[h][:], COPY)
 
+        def place_scalar_whole(k):
+            staged = tile([P, N], F32, "dw_whole%d" % k)
+            nc.scalar.copy(staged[:], dw[k][:])
+            nc.scalar.activation(windows[k % WINDOWS][:].indirect(offsets[:]), staged[:], COPY, scale=unit[:])
+
         def store(k):
             nc.sync.dma_start(out[k * P : (k + 1) * P, :], windows[k % WINDOWS][:])
 
@@ -292,24 +299,23 @@ def tile_attend_gnce_w_kernel(tc, xT, w_words, w_scales, y, wt, xm, offs, out):
         store(0)
         whole(2, 3)
         round_xm(gpsimd_round, 3, 5)
-        place_scalar(1, (0, 1))
+        place_scalar_whole(1)
         store(1)
         place_vector(2, slice(0, N), "dw_sb2", ((3, 5),))
         store(2)
         whole(3, 5)
         round_xm(gpsimd_round, 5, 8)
-        place_scalar(3, (0, 1))
+        place_scalar_whole(3)
         store(3)
         place_vector(4, slice(0, N), "dw_sb4", ((5, 7), (7, 8)))
         store(4)
         whole(5, 8)
-        place_scalar(5, (0, 1))
+        place_scalar_whole(5)
         store(5)
         staged = {k: tile([P, N], F32, "dw_sb%d" % k) for k in (6, 7)}
         for k in (6, 7):
             nc.vector.tensor_copy(staged[k][:], dw[k][:])
         nc.vector.tensor_copy(windows[6 % WINDOWS][:].indirect(offsets[:]), staged[6][:])
         store(6)
-        for h in range(2):
-            nc.scalar.activation(windows[7 % WINDOWS][:].indirect(offsets[:, 16 * h : 16 * (h + 1)]), staged[7][:, HALVES[h]], COPY)
+        nc.scalar.activation(windows[7 % WINDOWS][:].indirect(offsets[:]), staged[7][:], COPY, scale=unit[:])
         store(7)

@@ -23,27 +23,27 @@ SIGMOID = mybir.ActivationFunctionType.Sigmoid
 P = 128
 PACK = 4
 PASSES = D // (P * PACK)
-D_TILES = D // P
 WINDOWS = 4
 HALF = N // 2
 HALVES = (slice(0, HALF), slice(HALF, N))
-SHARE = 80
+WHOLE = slice(0, N)
+QUARTER = N // 4
+LAST_QUARTERS = (slice(HALF, HALF + QUARTER), slice(HALF + QUARTER, N))
+VECTOR_CASTS = (80, 48)
 HEAD = 1024
+GPSIMD_ZEROES = 1536
 XM_LOADS = ((0, 1), (1, 3), (3, 8))
-EARLY_CUT = 1536
-BANK_OF_TILE = (0, 1, 1, 3, 4, 5, 6, 7)
-AT = {
-    "g_rows1": 0, "g_rows0": 1984, "wy10": 2048, "wy11": 3072,
-    "g_grouped1": 4096, "xm_grouped2": 4096, "xm_grouped3": 4096, "xm_grouped5": 4096,
-    "dw_sb6": 6208, "dw_sb4": 8192, "dw_sb7": 10176,
-    "table_words": 13312, "y_raw0": 21440, "table_scales": 25472,
-    "x_raw0": 27520, "xm_raw0": 27520, "prob1": 27520,
-    "x_grouped00": 35712, "y_raw1": 35712,
-    "x_grouped01": 39808, "xm_raw1": 39808,
-    "x_codes00": 43904, "xm_raw3": 43904,
-    "x_grouped11": 54144, "w_codes11": 54144,
-    "wy01": 56192, "xm_grouped0": 56192,
-    "wy12": 57216, "wy02": 58176, "wy13": 59136, "xm_grouped1": 59136,
+BANK_OF = {(0, 0): 0, (0, 256): 2, (0, 384): 3, (1, 0): 1, (2, 0): 1, (3, 0): 4, (4, 0): 5, (5, 0): 6, (6, 0): 7, (7, 0): 0}
+KIB = 1024
+SHARED = {
+    "table_words": 0, "y_raw00": 0, "y_raw01": 2 * KIB,
+    "x_raw0": 8 * KIB, "xm_raw0": 8 * KIB,
+    "x_grouped00": 16 * KIB, "y_raw10": 16 * KIB,
+    "x_grouped01": 20 * KIB, "xm_raw1": 20 * KIB,
+    "x_codes00": 24 * KIB, "xm_raw3": 24 * KIB,
+    "w_codes1": 34 * KIB, "xm_grouped0": 34 * KIB,
+    "g_grouped384": 37 * KIB, "xm_grouped2": 38 * KIB, "xm_grouped3": 37 * KIB, "xm_grouped5": 37 * KIB,
+    "staged4": 40 * KIB, "staged6": 40 * KIB, "staged5": 42 * KIB, "staged7": 42 * KIB,
 }
 
 
@@ -51,12 +51,12 @@ def tile_attend_gnce_w_kernel(tc, xT, w_words, w_scales, y, wt, xm, offs, out):
     nc = tc.nc
     with ExitStack() as ctx:
         keep = ctx.enter_context(tc.tile_pool(name="keep", bufs=1))
-        reuse = ctx.enter_context(tc.tile_pool(name="reuse", bufs=1))
+        shared = ctx.enter_context(tc.tile_pool(name="shared", bufs=1))
         psum = ctx.enter_context(tc.psum_pool(name="psum", bufs=1))
 
         def tile(shape, dtype, name):
-            if name in AT:
-                return reuse.tile(shape, dtype, name=name, align_bytes=64, offset=AT[name])
+            if name in SHARED:
+                return shared.tile(shape, dtype, name=name, align_bytes=64, offset=SHARED[name])
             return keep.tile(shape, dtype, name=name, align_bytes=64)
 
         def zero_odd(view):
@@ -71,31 +71,39 @@ def tile_attend_gnce_w_kernel(tc, xT, w_words, w_scales, y, wt, xm, offs, out):
         windows = [tile([P, T], F32, "window%d" % k) for k in range(WINDOWS)]
         warm_in = keep.tile([P, 1], F32, name="warm_in")
         warm_out = keep.tile([P, 1], F32, name="warm_out")
+        unit = keep.tile([P, 1], F32, name="unit")
+        wt_sb = tile([P, PACK], F32, "wt_sb")
 
         zero_odd(table_scales[:].bitcast(I32))
         nc.vector.memset(warm_in[:], 0.0)
-        unit = keep.tile([P, 1], F32, name="unit")
         nc.vector.memset(unit[:], 1.0)
         nc.scalar.activation(warm_out[:], warm_in[:], SIGMOID)
         zero_odd(w_plane1[96:P, :].bitcast(I32))
         zero_odd(windows[2][:])
-        zero_odd(windows[3][:, EARLY_CUT:])
+        zero_odd(windows[3][:, GPSIMD_ZEROES:])
         nc.gpsimd.memset(windows[0][:], 0.0)
         nc.gpsimd.memset(windows[1][:], 0.0)
-        nc.gpsimd.memset(windows[3][:, :EARLY_CUT], 0.0)
+        nc.gpsimd.memset(windows[3][:, :GPSIMD_ZEROES], 0.0)
 
-        x_raw = [tile([P, PACK, R], F32, "x_raw%d" % o) for o in range(PASSES)]
-        y_raw = {}
-        wt_sb = tile([P, PACK], F32, "wt_sb")
         words = w_words[0].rearrange("p t b -> p (t b)").bitcast(I32)
         scale_rows = w_scales.rearrange("o (q f) t -> f q o t", f=4).bitcast(I32)
         y_rows = y[0].rearrange("(p t) i -> p t i", t=PACK)
         xm_rows = xm[0].rearrange("(p j) d -> p j d", j=PACK)
+        x_raw = [tile([P, PACK, R], F32, "x_raw%d" % o) for o in range(PASSES)]
+        y_raw = {}
         xm_raw = {}
 
+        def load_y(h, t0, t1):
+            piece = tile([P, t1 - t0, HALF], F32, "y_raw%d%d" % (h, t0 // 2))
+            nc.sync.dma_start(piece[:], y_rows[:, t0:t1, HALVES[h]])
+            for t in range(t0, t1):
+                y_raw[h, t] = piece[:, t - t0, :]
+
         def load_xm(k0, k1):
-            xm_raw[k0] = tile([P, PACK, (k1 - k0) * P], F32, "xm_raw%d" % k0)
-            nc.sync.dma_start(xm_raw[k0][:], xm_rows[:, :, k0 * P : k1 * P])
+            piece = tile([P, PACK, (k1 - k0) * P], F32, "xm_raw%d" % k0)
+            nc.sync.dma_start(piece[:], xm_rows[:, :, k0 * P : k1 * P])
+            for k in range(k0, k1):
+                xm_raw[k] = piece[:, :, (k - k0) * P : (k - k0 + 1) * P]
 
         nc.sync.dma_start(offsets[:], offs)
         nc.sync.dma_start(table_words[:, :HEAD], words[:, :HEAD])
@@ -104,11 +112,8 @@ def tile_attend_gnce_w_kernel(tc, xT, w_words, w_scales, y, wt, xm, offs, out):
         nc.sync.dma_start(table_words[:, HEAD:], words[:, HEAD:])
         for o in range(PASSES):
             nc.sync.dma_start(x_raw[o][:], xT[0, 512 * o : 512 * (o + 1), :].rearrange("(p j) r -> p j r", j=PACK))
-        nc.sync.dma_start(wt_sb[:], wt[0].rearrange("(p t) one -> p (t one)", t=PACK))
 
-        def load_y(h):
-            y_raw[h] = tile([P, PACK, HALF], F32, "y_raw%d" % h)
-            nc.sync.dma_start(y_raw[h][:], y_rows[:, :, HALVES[h]])
+        nc.sync.dma_start(wt_sb[:], wt[0].rearrange("(p t) one -> p (t one)", t=PACK))
 
         picked_scales = tile([P, N], U8, "picked_scales")
         nc.vector.tensor_copy(picked_scales[:], table_scales[:].indirect(offsets[:]))
@@ -116,18 +121,11 @@ def tile_attend_gnce_w_kernel(tc, xT, w_words, w_scales, y, wt, xm, offs, out):
         w_plane = (picked_scales, w_plane1)
         word_pairs = tile([P, N], U32, "word_pairs")
         nc.vector.tensor_copy(word_pairs[:], table_words[:].bitcast(U32).indirect(offsets[:]))
-        load_y(0)
-        w_codes = {}
-
-        def part_words(o, halves):
-            codes = tile([P, 2 * HALF * len(halves)], U8, "w_codes%d%d" % (o, halves[0]))
-            c0 = PASSES * HALF * halves[0]
-            nc.vector.tensor_copy(codes[:].bitcast(U16), word_pairs[:].bitcast(U16)[:, c0 + o : c0 + PASSES * HALF * len(halves) : PASSES])
-            for n, h in enumerate(halves):
-                w_codes[o, h] = codes[:, 2 * HALF * n : 2 * HALF * (n + 1)]
-
-        part_words(0, (0, 1))
-        part_words(1, (0,))
+        load_y(0, 0, 2)
+        load_y(0, 2, 4)
+        w_codes = [tile([P, 2 * N], U8, "w_codes%d" % o) for o in range(PASSES)]
+        for o in range(PASSES):
+            nc.vector.tensor_copy(w_codes[o][:].bitcast(U16), word_pairs[:].bitcast(U16)[:, o : PASSES * N : PASSES])
 
         logits = {(h, t): psum.tile([P, HALF], F32, name="logits%d%d" % (h, t), tag="bank%d" % (PACK * h + t)) for h in range(2) for t in range(PACK)}
 
@@ -136,7 +134,7 @@ def tile_attend_gnce_w_kernel(tc, xT, w_words, w_scales, y, wt, xm, offs, out):
             x_codes = [tile([P, 2, P], U32, "x_codes%d%d" % (o, pair)) for pair in range(2)]
             x_plane = [tile([P, 2, P], U8, "x_plane%d%d" % (o, pair)) for pair in range(2)]
             for pair in range(2):
-                for copy, m0, m1 in ((nc.vector.tensor_copy, 0, SHARE), (nc.scalar.copy, SHARE, P)):
+                for copy, m0, m1 in ((nc.vector.tensor_copy, 0, VECTOR_CASTS[pair]), (nc.scalar.copy, VECTOR_CASTS[pair], P)):
                     copy(
                         x_grouped[pair][:].rearrange("p t m j -> p m j t")[:, m0:m1],
                         x_raw[o][:].rearrange("p j (m t) -> p m j t", t=PACK)[:, m0:m1, :, 2 * pair : 2 * pair + 2],
@@ -148,14 +146,12 @@ def tile_attend_gnce_w_kernel(tc, xT, w_words, w_scales, y, wt, xm, offs, out):
                     in_=x_grouped[pair][:, u0:u1].rearrange("p t m j -> p (t m j)"),
                 )
             for h in range(2):
-                if (o, h) not in w_codes:
-                    part_words(o, (h,))
                 for t in range(PACK):
                     nc.tensor.matmul_mx(
                         out=logits[h, t][:],
                         lhsT=x_codes[t // 2][:, t % 2, :].bitcast(E4M3),
                         lhsT_scale=x_plane[t // 2][:, t % 2, :],
-                        rhs=w_codes[o, h].bitcast(E2M1),
+                        rhs=w_codes[o][:, 2 * HALF * h : 2 * HALF * (h + 1)].bitcast(E2M1),
                         rhs_scale=w_plane[o][:, HALVES[h]],
                         start=(o == 0),
                         stop=(o == PASSES - 1),
@@ -163,24 +159,25 @@ def tile_attend_gnce_w_kernel(tc, xT, w_words, w_scales, y, wt, xm, offs, out):
 
         scores(0)
         load_xm(*XM_LOADS[0])
-        load_y(1)
+        load_y(1, 0, 4)
         for k0, k1 in XM_LOADS[1:]:
             load_xm(k0, k1)
         scores(1)
 
         wy = {}
-
-        def weigh_y(h, t, on_scalar):
-            wy[h, t] = tile([P, HALF], F32, "wy%d%d" % (h, t))
-            if on_scalar:
-                nc.scalar.activation(wy[h, t][:], y_raw[h][:, t, :], COPY, scale=wt_sb[:, t : t + 1])
-            else:
-                nc.vector.tensor_scalar(wy[h, t][:], y_raw[h][:, t, :], wt_sb[:, t : t + 1], None, MULT)
-
+        prob = {}
+        g_rows = {}
+        g_grouped = {}
         g_codes = tile([P, N], U32, "g_codes")
         g_plane = tile([P, N], U8, "g_plane")
-        prob = {}
-        g_grouped = {}
+
+        def weigh_y(h, on_scalar):
+            for t in range(PACK):
+                wy[h, t] = tile([P, HALF], F32, "wy%d%d" % (h, t))
+                if on_scalar:
+                    nc.scalar.activation(wy[h, t][:], y_raw[h, t], COPY, scale=wt_sb[:, t : t + 1])
+                else:
+                    nc.vector.tensor_scalar(wy[h, t][:], y_raw[h, t], wt_sb[:, t : t + 1], None, MULT)
 
         def sigmoid(h):
             prob[h] = tile([P, PACK, HALF], F32, "prob%d" % h)
@@ -188,22 +185,26 @@ def tile_attend_gnce_w_kernel(tc, xT, w_words, w_scales, y, wt, xm, offs, out):
                 nc.scalar.activation(prob[h][:, t, :], logits[h, t][:], SIGMOID)
 
         def gradient(h):
-            g_rows = tile([P, PACK, HALF], BF16, "g_rows%d" % h)
+            g_rows[h] = tile([P, PACK, HALF], BF16, "g_rows%d" % h)
             for t in range(PACK):
                 nc.vector.scalar_tensor_tensor(
-                    g_rows[:, t, :], prob[h][:, t, :], wt_sb[:, t : t + 1], wy[h, t][:], MULT, SUBTRACT
+                    g_rows[h][:, t, :], prob[h][:, t, :], wt_sb[:, t : t + 1], wy[h, t][:], MULT, SUBTRACT
                 )
-            g_grouped[h] = tile([P, HALF, PACK], BF16, "g_grouped%d" % h)
+
+        def group_g(cols):
+            h, c0 = divmod(cols.start, HALF)
+            width = cols.stop - cols.start
+            g_grouped[cols.start] = tile([P, width, PACK], BF16, "g_grouped%d" % cols.start)
             nc.vector.tensor_copy(
-                g_grouped[h][:].rearrange("p (c i) t -> p c t i", i=4),
-                g_rows[:].rearrange("p t (c i) -> p c t i", i=4),
+                g_grouped[cols.start][:].rearrange("p (c i) t -> p c t i", i=4),
+                g_rows[h][:, :, c0 : c0 + width].rearrange("p t (c i) -> p c t i", i=4),
             )
 
-        def quantize_g(h):
+        def quantize_g(cols):
             nc.vector.quantize_mx(
-                out=g_codes[:, HALVES[h]].bitcast(E5M2),
-                scales=g_plane[:, HALVES[h]],
-                in_=g_grouped[h][:].rearrange("p i t -> p (i t)"),
+                out=g_codes[:, cols].bitcast(E5M2),
+                scales=g_plane[:, cols],
+                in_=g_grouped[cols.start][:].rearrange("p i t -> p (i t)"),
             )
 
         xm_grouped = {}
@@ -215,33 +216,30 @@ def tile_attend_gnce_w_kernel(tc, xT, w_words, w_scales, y, wt, xm, offs, out):
 
         def round_xm(copy, k0, k1):
             grouped = tile([P, (k1 - k0) * P, PACK], BF16, "xm_grouped%d" % k0)
-            for a in range(k0, k1, 2):
-                b = min(a + 2, k1)
-                xm_grouped[a, b] = grouped[:, (a - k0) * P : (b - k0) * P, :].rearrange("p d j -> p (d j)")
+            xm_grouped[k0, k1] = grouped[:].rearrange("p d j -> p (d j)")
             for k in range(k0, k1):
-                first = max(a for a, b in XM_LOADS if a <= k)
                 copy(
                     grouped[:, (k - k0) * P : (k - k0 + 1) * P, :].rearrange("p (c i) j -> p c j i", i=4),
-                    xm_raw[first][:, :, (k - first) * P : (k - first + 1) * P].rearrange("p j (c i) -> p c j i", i=4),
+                    xm_raw[k].rearrange("p j (c i) -> p c j i", i=4),
                 )
 
         def quantize_xm(k0, k1):
             codes = tile([P, (k1 - k0) * P], U32, "xm_codes%d" % k0)
             plane = tile([P, (k1 - k0) * P], U8, "xm_plane%d" % k0)
-            nc.vector.quantize_mx(
-                out=codes[:].bitcast(E4M3), scales=plane[:], in_=xm_grouped[k0, k1]
-            )
+            nc.vector.quantize_mx(out=codes[:].bitcast(E4M3), scales=plane[:], in_=xm_grouped[k0, k1])
             for k in range(k0, k1):
                 xm_codes[k] = codes[:, (k - k0) * P : (k - k0 + 1) * P]
                 xm_plane[k] = plane[:, (k - k0) * P : (k - k0 + 1) * P]
 
         dw = {}
+        staged = {}
 
         def multiply(k, cols):
-            if k not in dw:
-                dw[k] = psum.tile([P, N], F32, name="dw%d" % k, tag="bank%d" % BANK_OF_TILE[k])
+            if (k, cols.start) in BANK_OF:
+                width = cols.stop - cols.start if k == 0 else N
+                dw[k, cols.start] = psum.tile([P, width], F32, name="dw%d_%d" % (k, cols.start), tag="bank%d" % BANK_OF[k, cols.start])
             nc.tensor.matmul_mx(
-                out=dw[k][:, cols],
+                out=dw[k, cols.start][:] if k == 0 else dw[k, 0][:, cols],
                 lhsT=xm_codes[k].bitcast(E4M3),
                 lhsT_scale=xm_plane[k],
                 rhs=g_codes[:, cols].bitcast(E5M2),
@@ -250,72 +248,80 @@ def tile_attend_gnce_w_kernel(tc, xT, w_words, w_scales, y, wt, xm, offs, out):
                 stop=True,
             )
 
-        def place_vector(k, cols, name, between):
-            staged = tile([P, cols.stop - cols.start], F32, name)
-            nc.vector.tensor_copy(staged[:], dw[k][:, cols])
-            for k0, k1 in between:
-                quantize_xm(k0, k1)
-            nc.vector.tensor_copy(windows[k % WINDOWS][:].indirect(offsets[:, cols.start // 16 : cols.stop // 16]), staged[:])
+        def stage(copy, k, cols):
+            name = "staged%d" % k if cols == WHOLE else "staged%d_%d" % (k, cols.start)
+            staged[k, cols.start] = tile([P, cols.stop - cols.start], F32, name)
+            copy(staged[k, cols.start][:], dw[k, cols.start][:])
 
-        def place_scalar(k, halves):
-            staged = {h: tile([P, HALF], F32, "dw_sb%d%d" % (k, h)) for h in halves}
-            for h in halves:
-                nc.scalar.copy(staged[h][:], dw[k][:, HALVES[h]])
-            for h in halves:
-                nc.scalar.activation(windows[k % WINDOWS][:].indirect(offsets[:, 16 * h : 16 * (h + 1)]), staged[h][:], COPY)
+        def listed(k, cols):
+            return windows[k % WINDOWS][:].indirect(offsets[:, cols.start // 16 : cols.stop // 16])
 
-        def place_scalar_whole(k):
-            staged = tile([P, N], F32, "dw_whole%d" % k)
-            nc.scalar.copy(staged[:], dw[k][:])
-            nc.scalar.activation(windows[k % WINDOWS][:].indirect(offsets[:]), staged[:], COPY, scale=unit[:])
+        def place_vector(k, cols):
+            nc.vector.tensor_copy(listed(k, cols), staged[k, cols.start][:])
+
+        def place_scalar(k, cols):
+            nc.scalar.activation(listed(k, cols), staged[k, cols.start][:], COPY, scale=unit[:])
 
         def store(k):
             nc.sync.dma_start(out[k * P : (k + 1) * P, :], windows[k % WINDOWS][:])
 
-        def whole(j0, j1):
-            for j in range(j0, j1):
-                multiply(j, slice(0, N))
-
-        for t in range(PACK):
-            weigh_y(0, t, t < 2)
+        weigh_y(0, False)
         sigmoid(0)
-        gradient(0)
-        round_xm(nc.scalar.copy, 0, 1)
         sigmoid(1)
-        for t in range(PACK):
-            weigh_y(1, t, t < 2)
-        quantize_xm(0, 1)
-        quantize_g(0)
-        multiply(0, HALVES[0])
-        gradient(1)
+        weigh_y(1, True)
         round_xm(nc.scalar.copy, 1, 2)
-        place_scalar(0, (0,))
+        gradient(0)
+        group_g(HALVES[0])
+        round_xm(nc.vector.tensor_copy, 0, 1)
+        quantize_g(HALVES[0])
+        quantize_xm(0, 1)
+        multiply(0, HALVES[0])
+        stage(nc.scalar.copy, 0, HALVES[0])
+        place_scalar(0, HALVES[0])
+        gradient(1)
         quantize_xm(1, 2)
-        quantize_g(1)
-        multiply(0, HALVES[1])
-        whole(1, 2)
-        round_xm(nc.vector.tensor_copy, 2, 3)
-        place_vector(0, HALVES[1], "dw0b", ((2, 3),))
+        multiply(1, HALVES[0])
+        for cols in LAST_QUARTERS:
+            group_g(cols)
+        for cols in LAST_QUARTERS:
+            quantize_g(cols)
+        for cols in LAST_QUARTERS:
+            multiply(0, cols)
+            multiply(1, cols)
+        staged[0, HALF] = tile([P, HALF], F32, "staged0_256")
+        for cols in LAST_QUARTERS:
+            nc.vector.tensor_copy(staged[0, HALF][:, cols.start - HALF : cols.stop - HALF], dw[0, cols.start][:])
+        place_vector(0, HALVES[1])
         store(0)
-        whole(2, 3)
+        round_xm(nc.vector.tensor_copy, 2, 3)
+        quantize_xm(2, 3)
+        multiply(2, WHOLE)
         round_xm(gpsimd_round, 3, 5)
-        place_scalar_whole(1)
+        stage(nc.scalar.copy, 1, WHOLE)
+        place_scalar(1, WHOLE)
         store(1)
-        place_vector(2, slice(0, N), "dw_sb2", ((3, 5),))
+        stage(nc.vector.tensor_copy, 2, WHOLE)
+        quantize_xm(3, 5)
+        place_vector(2, WHOLE)
         store(2)
-        whole(3, 5)
+        multiply(3, WHOLE)
+        multiply(4, WHOLE)
         round_xm(gpsimd_round, 5, 8)
-        place_scalar_whole(3)
+        stage(nc.scalar.copy, 3, WHOLE)
+        place_scalar(3, WHOLE)
         store(3)
-        place_vector(4, slice(0, N), "dw_sb4", ((5, 7), (7, 8)))
+        stage(nc.vector.tensor_copy, 4, WHOLE)
+        quantize_xm(5, 8)
+        place_vector(4, WHOLE)
         store(4)
-        whole(5, 8)
-        place_scalar_whole(5)
+        for k in range(5, 8):
+            multiply(k, WHOLE)
+        stage(nc.scalar.copy, 5, WHOLE)
+        place_scalar(5, WHOLE)
         store(5)
-        staged = {k: tile([P, N], F32, "dw_sb%d" % k) for k in (6, 7)}
-        for k in (6, 7):
-            nc.vector.tensor_copy(staged[k][:], dw[k][:])
-        nc.vector.tensor_copy(windows[6 % WINDOWS][:].indirect(offsets[:]), staged[6][:])
+        stage(nc.vector.tensor_copy, 6, WHOLE)
+        place_vector(6, WHOLE)
         store(6)
-        nc.scalar.activation(windows[7 % WINDOWS][:].indirect(offsets[:]), staged[7][:], COPY, scale=unit[:])
+        stage(nc.scalar.copy, 7, WHOLE)
+        place_scalar(7, WHOLE)
         store(7)

@@ -29,21 +29,24 @@ HALVES = (slice(0, HALF), slice(HALF, N))
 WHOLE = slice(0, N)
 QUARTER = N // 4
 LAST_QUARTERS = (slice(HALF, HALF + QUARTER), slice(HALF + QUARTER, N))
-VECTOR_CASTS = (80, 48)
+X_LOADS = ((0, 0, 4), (1, 0, 4))
+VECTOR_CASTS = {(0, 0): (80, 48), (1, 0): (80, 48)}
+LATE_PASS0 = ((1, 2), (1, 3))
 HEAD = 1024
 GPSIMD_ZEROES = 1536
-XM_LOADS = ((0, 1), (1, 3), (3, 8))
-BANK_OF = {(0, 0): 0, (0, 256): 2, (0, 384): 3, (1, 0): 1, (2, 0): 1, (3, 0): 4, (4, 0): 5, (5, 0): 6, (6, 0): 7, (7, 0): 0}
+XM_LOADS = ((0, 1), (1, 2), (2, 3), (3, 5), (5, 8))
+BANK_OF = {(0, 0): 0, (0, 256): 2, (0, 384): 3, (1, 0): 1, (2, 0): 0, (3, 0): 4, (4, 0): 5, (5, 0): 6, (6, 0): 7, (7, 0): 2}
 KIB = 1024
 SHARED = {
     "table_words": 0, "y_raw00": 0, "y_raw01": 2 * KIB,
-    "x_raw0": 8 * KIB, "xm_raw0": 8 * KIB,
-    "x_grouped00": 16 * KIB, "y_raw10": 16 * KIB,
-    "x_grouped01": 20 * KIB, "xm_raw1": 20 * KIB,
-    "x_codes00": 24 * KIB, "xm_raw3": 24 * KIB,
+    "x_raw00": 8 * KIB, "xm_raw0": 8 * KIB,
+    "x_grouped00": 17 * KIB, "y_raw10": 16 * KIB, "y_raw11": 18 * KIB,
+    "x_grouped01": 21 * KIB, "xm_raw1": 20 * KIB, "xm_raw2": 22 * KIB,
+    "x_codes00": 24 * KIB, "xm_raw3": 24 * KIB, "staged2": 24 * KIB,
+    "x_codes01": 28 * KIB, "xm_raw5": 28 * KIB, "staged4": 28 * KIB, "staged6": 28 * KIB,
     "w_codes1": 34 * KIB, "xm_grouped0": 34 * KIB,
     "g_grouped384": 37 * KIB, "xm_grouped2": 38 * KIB, "xm_grouped3": 37 * KIB, "xm_grouped5": 37 * KIB,
-    "staged4": 40 * KIB, "staged6": 40 * KIB, "staged5": 42 * KIB, "staged7": 42 * KIB,
+    "staged5": 42 * KIB, "staged7": 42 * KIB,
 }
 
 
@@ -89,7 +92,7 @@ def tile_attend_gnce_w_kernel(tc, xT, w_words, w_scales, y, wt, xm, offs, out):
         scale_rows = w_scales.rearrange("o (q f) t -> f q o t", f=4).bitcast(I32)
         y_rows = y[0].rearrange("(p t) i -> p t i", t=PACK)
         xm_rows = xm[0].rearrange("(p j) d -> p j d", j=PACK)
-        x_raw = [tile([P, PACK, R], F32, "x_raw%d" % o) for o in range(PASSES)]
+        x_raw = {}
         y_raw = {}
         xm_raw = {}
 
@@ -110,8 +113,9 @@ def tile_attend_gnce_w_kernel(tc, xT, w_words, w_scales, y, wt, xm, offs, out):
         for f in range(4):
             nc.sync.dma_start(table_scales[f:P:16, :].bitcast(I32), scale_rows[f])
         nc.sync.dma_start(table_words[:, HEAD:], words[:, HEAD:])
-        for o in range(PASSES):
-            nc.sync.dma_start(x_raw[o][:], xT[0, 512 * o : 512 * (o + 1), :].rearrange("(p j) r -> p j r", j=PACK))
+        for o, j0, j1 in X_LOADS:
+            x_raw[o, j0] = tile([P, j1 - j0, R], F32, "x_raw%d%d" % (o, j0))
+            nc.sync.dma_start(x_raw[o, j0][:], xT[0, 512 * o : 512 * (o + 1), :].rearrange("(p j) r -> p j r", j=PACK)[:, j0:j1, :])
 
         nc.sync.dma_start(wt_sb[:], wt[0].rearrange("(p t) one -> p (t one)", t=PACK))
 
@@ -129,37 +133,52 @@ def tile_attend_gnce_w_kernel(tc, xT, w_words, w_scales, y, wt, xm, offs, out):
 
         logits = {(h, t): psum.tile([P, HALF], F32, name="logits%d%d" % (h, t), tag="bank%d" % (PACK * h + t)) for h in range(2) for t in range(PACK)}
 
+        x_operand = {}
+
+        def score_pass(o, h, t, first):
+            nc.tensor.matmul_mx(
+                out=logits[h, t][:],
+                lhsT=x_operand[o, t][0].bitcast(E4M3),
+                lhsT_scale=x_operand[o, t][1],
+                rhs=w_codes[o][:, 2 * HALF * h : 2 * HALF * (h + 1)].bitcast(E2M1),
+                rhs_scale=w_plane[o][:, HALVES[h]],
+                start=first,
+                stop=not first,
+            )
+
         def scores(o):
             x_grouped = [tile([P, 2, P, PACK], BF16, "x_grouped%d%d" % (o, pair)) for pair in range(2)]
             x_codes = [tile([P, 2, P], U32, "x_codes%d%d" % (o, pair)) for pair in range(2)]
             x_plane = [tile([P, 2, P], U8, "x_plane%d%d" % (o, pair)) for pair in range(2)]
-            for pair in range(2):
-                for copy, m0, m1 in ((nc.vector.tensor_copy, 0, VECTOR_CASTS[pair]), (nc.scalar.copy, VECTOR_CASTS[pair], P)):
-                    copy(
-                        x_grouped[pair][:].rearrange("p t m j -> p m j t")[:, m0:m1],
-                        x_raw[o][:].rearrange("p j (m t) -> p m j t", t=PACK)[:, m0:m1, :, 2 * pair : 2 * pair + 2],
-                    )
+            for j0, j1 in [(j0, j1) for pass_of, j0, j1 in X_LOADS if pass_of == o]:
+                for pair in range(2):
+                    share = VECTOR_CASTS[o, j0][pair]
+                    for copy, m0, m1 in ((nc.vector.tensor_copy, 0, share), (nc.scalar.copy, share, P)):
+                        if m0 < m1:
+                            copy(
+                                x_grouped[pair][:].rearrange("p t m j -> p m j t")[:, m0:m1, j0:j1],
+                                x_raw[o, j0][:].rearrange("p j (m t) -> p m j t", t=PACK)[:, m0:m1, :, 2 * pair : 2 * pair + 2],
+                            )
             for pair, u0, u1 in ((0, 0, 1), (0, 1, 2), (1, 0, 2)):
                 nc.vector.quantize_mx(
                     out=x_codes[pair][:, u0:u1, :].rearrange("p t m -> p (t m)").bitcast(E4M3),
                     scales=x_plane[pair][:, u0:u1, :].rearrange("p t m -> p (t m)"),
                     in_=x_grouped[pair][:, u0:u1].rearrange("p t m j -> p (t m j)"),
                 )
+            for t in range(PACK):
+                x_operand[o, t] = (x_codes[t // 2][:, t % 2, :], x_plane[t // 2][:, t % 2, :])
             for h in range(2):
                 for t in range(PACK):
-                    nc.tensor.matmul_mx(
-                        out=logits[h, t][:],
-                        lhsT=x_codes[t // 2][:, t % 2, :].bitcast(E4M3),
-                        lhsT_scale=x_plane[t // 2][:, t % 2, :],
-                        rhs=w_codes[o][:, 2 * HALF * h : 2 * HALF * (h + 1)].bitcast(E2M1),
-                        rhs_scale=w_plane[o][:, HALVES[h]],
-                        start=(o == 0),
-                        stop=(o == PASSES - 1),
-                    )
+                    if (h, t) not in LATE_PASS0:
+                        score_pass(o, h, t, o == 0)
+                    elif o == 1:
+                        score_pass(1, h, t, True)
+                        score_pass(0, h, t, False)
 
         scores(0)
         load_xm(*XM_LOADS[0])
-        load_y(1, 0, 4)
+        load_y(1, 0, 2)
+        load_y(1, 2, 4)
         for k0, k1 in XM_LOADS[1:]:
             load_xm(k0, k1)
         scores(1)

@@ -29,8 +29,8 @@ HALVES = (slice(0, HALF), slice(HALF, N))
 WHOLE = slice(0, N)
 QUARTER = N // 4
 LAST_QUARTERS = (slice(HALF, HALF + QUARTER), slice(HALF + QUARTER, N))
-X_LOADS = ((0, 0, 4), (1, 0, 4))
-VECTOR_CASTS = {(0, 0): (80, 48), (1, 0): (80, 48)}
+X_LOADS = ((0, 0, 4), (1, 0, 2), (1, 2, 4))
+VECTOR_CASTS = {(0, 0): (80, 48), (1, 0): (80, 80), (1, 2): (88, 64)}
 LATE_PASS0 = ((1, 2), (1, 3))
 HEAD = 1024
 GPSIMD_ZEROES = 1536
@@ -41,11 +41,11 @@ SHARED = {
     "table_words": 0, "y_raw00": 0, "y_raw01": 2 * KIB,
     "x_raw00": 8 * KIB, "xm_raw0": 8 * KIB,
     "x_grouped00": 17 * KIB, "y_raw10": 16 * KIB, "y_raw11": 18 * KIB,
-    "x_grouped01": 21 * KIB, "xm_raw1": 20 * KIB, "xm_raw2": 22 * KIB,
+    "x_grouped01": 21 * KIB, "xm_raw1": 20 * KIB, "staged0_0": 20 * KIB, "xm_raw2": 22 * KIB,
     "x_codes00": 24 * KIB, "xm_raw3": 24 * KIB, "staged2": 24 * KIB,
     "x_codes01": 28 * KIB, "xm_raw5": 28 * KIB, "staged4": 28 * KIB, "staged6": 28 * KIB,
     "w_codes1": 34 * KIB, "xm_grouped0": 34 * KIB,
-    "g_grouped384": 37 * KIB, "xm_grouped2": 38 * KIB, "xm_grouped3": 37 * KIB, "xm_grouped5": 37 * KIB,
+    "g_grouped256": 37 * KIB, "xm_grouped2": 37 * KIB, "xm_grouped3": 37 * KIB, "xm_grouped5": 37 * KIB,
     "staged5": 42 * KIB, "staged7": 42 * KIB,
 }
 
@@ -190,8 +190,8 @@ def tile_attend_gnce_w_kernel(tc, xT, w_words, w_scales, y, wt, xm, offs, out):
         g_codes = tile([P, N], U32, "g_codes")
         g_plane = tile([P, N], U8, "g_plane")
 
-        def weigh_y(h, on_scalar):
-            for t in range(PACK):
+        def weigh_y(h, on_scalar, places):
+            for t in places:
                 wy[h, t] = tile([P, HALF], F32, "wy%d%d" % (h, t))
                 if on_scalar:
                     nc.scalar.activation(wy[h, t][:], y_raw[h, t], COPY, scale=wt_sb[:, t : t + 1])
@@ -284,10 +284,10 @@ def tile_attend_gnce_w_kernel(tc, xT, w_words, w_scales, y, wt, xm, offs, out):
         def store(k):
             nc.sync.dma_start(out[k * P : (k + 1) * P, :], windows[k % WINDOWS][:])
 
-        weigh_y(0, False)
+        weigh_y(0, False, range(PACK))
         sigmoid(0)
         sigmoid(1)
-        weigh_y(1, True)
+        weigh_y(1, True, range(PACK))
         round_xm(nc.scalar.copy, 1, 2)
         gradient(0)
         group_g(HALVES[0])
@@ -310,10 +310,10 @@ def tile_attend_gnce_w_kernel(tc, xT, w_words, w_scales, y, wt, xm, offs, out):
         staged[0, HALF] = tile([P, HALF], F32, "staged0_256")
         for cols in LAST_QUARTERS:
             nc.vector.tensor_copy(staged[0, HALF][:, cols.start - HALF : cols.stop - HALF], dw[0, cols.start][:])
-        place_vector(0, HALVES[1])
-        store(0)
         round_xm(nc.vector.tensor_copy, 2, 3)
         quantize_xm(2, 3)
+        place_vector(0, HALVES[1])
+        store(0)
         multiply(2, WHOLE)
         round_xm(gpsimd_round, 3, 5)
         stage(nc.scalar.copy, 1, WHOLE)

@@ -35,18 +35,18 @@ LATE_PASS0 = ((1, 2), (1, 3))
 HEAD = 1024
 GPSIMD_ZEROES = 1536
 XM_LOADS = ((0, 1), (1, 2), (2, 3), (3, 5), (5, 8))
-BANK_OF = {(0, 0): 0, (0, 256): 2, (0, 384): 3, (1, 0): 1, (2, 0): 0, (3, 0): 4, (4, 0): 5, (5, 0): 6, (6, 0): 7, (7, 0): 2}
+BANK_OF = {(0, 0): 0, (0, 256): 2, (0, 384): 3, (1, 0): 1, (2, 0): 1, (3, 0): 4, (4, 0): 5, (5, 0): 6, (6, 0): 7, (7, 0): 2}
 KIB = 1024
 SHARED = {
     "table_words": 0, "y_raw00": 0, "y_raw01": 2 * KIB,
     "x_raw00": 8 * KIB, "xm_raw0": 8 * KIB,
     "x_grouped00": 17 * KIB, "y_raw10": 16 * KIB, "y_raw11": 18 * KIB,
     "x_grouped01": 21 * KIB, "xm_raw1": 20 * KIB, "staged0_0": 20 * KIB, "xm_raw2": 22 * KIB,
-    "x_codes00": 24 * KIB, "xm_raw3": 24 * KIB, "staged2": 24 * KIB,
-    "x_codes01": 28 * KIB, "xm_raw5": 28 * KIB, "staged4": 28 * KIB, "staged6": 28 * KIB,
+    "x_codes00": 24 * KIB, "xm_raw3": 24 * KIB,
+    "x_codes01": 28 * KIB, "xm_raw5": 28 * KIB, "staged4": 44 * KIB, "staged6": 43 * KIB, "xm_codes7": 45 * KIB,
     "w_codes1": 34 * KIB, "xm_grouped0": 34 * KIB,
-    "g_grouped256": 37 * KIB, "xm_grouped2": 37 * KIB, "xm_grouped3": 37 * KIB, "xm_grouped5": 37 * KIB,
-    "staged5": 42 * KIB, "staged7": 42 * KIB,
+    "g_grouped256": 37 * KIB, "xm_grouped2": 37 * KIB, "xm_grouped3": 37 * KIB, "xm_grouped5": 37 * KIB, "xm_grouped7": 37 * KIB,
+    "staged5": 48 * KIB, "staged7": 48 * KIB,
 }
 
 
@@ -325,20 +325,23 @@ def tile_attend_gnce_w_kernel(tc, xT, w_words, w_scales, y, wt, xm, offs, out):
         store(2)
         multiply(3, WHOLE)
         multiply(4, WHOLE)
-        round_xm(gpsimd_round, 5, 8)
+        round_xm(gpsimd_round, 5, 7)
         stage(nc.scalar.copy, 3, WHOLE)
         place_scalar(3, WHOLE)
         store(3)
         stage(nc.vector.tensor_copy, 4, WHOLE)
-        quantize_xm(5, 8)
+        quantize_xm(5, 7)
+        round_xm(gpsimd_round, 7, 8)
         place_vector(4, WHOLE)
         store(4)
-        for k in range(5, 8):
+        for k in range(5, 7):
             multiply(k, WHOLE)
         stage(nc.scalar.copy, 5, WHOLE)
         place_scalar(5, WHOLE)
         store(5)
         stage(nc.vector.tensor_copy, 6, WHOLE)
+        quantize_xm(7, 8)
+        multiply(7, WHOLE)
         place_vector(6, WHOLE)
         store(6)
         stage(nc.scalar.copy, 7, WHOLE)

@@ -30,7 +30,7 @@ WHOLE = slice(0, N)
 QUARTER = N // 4
 LAST_QUARTERS = (slice(HALF, HALF + QUARTER), slice(HALF + QUARTER, N))
 X_LOADS = ((0, 0, 4), (1, 0, 2), (1, 2, 4))
-VECTOR_CASTS = {(0, 0): (80, 48), (1, 0): (80, 80), (1, 2): (88, 64)}
+VECTOR_CASTS = {(0, 0): (72, 40), (1, 0): (64, 56), (1, 2): (88, 64)}
 LATE_PASS0 = ((1, 2), (1, 3))
 HEAD = 1024
 GPSIMD_ZEROES = 1536

@@ -33,7 +33,7 @@ X_LOADS = ((0, 0, 4), (1, 0, 2), (1, 2, 4))
 VECTOR_CASTS = {(0, 0): (72, 40), (1, 0): (64, 56), (1, 2): (88, 64)}
 LATE_PASS0 = ((1, 2), (1, 3))
 HEAD = 1024
-GPSIMD_ZEROES = 1536
+GPSIMD_ZEROES = 1280
 XM_LOADS = ((0, 1), (1, 2), (2, 3), (3, 5), (5, 8))
 BANK_OF = {(0, 0): 0, (0, 256): 2, (0, 384): 3, (1, 0): 1, (2, 0): 1, (3, 0): 4, (4, 0): 5, (5, 0): 6, (6, 0): 7, (7, 0): 2}
 KIB = 1024
@@ -77,7 +77,7 @@ def tile_attend_gnce_w_kernel(tc, xT, w_words, w_scales, y, wt, xm, offs, out):
         unit = keep.tile([P, 1], F32, name="unit")
         wt_sb = tile([P, PACK], F32, "wt_sb")
 
-        zero_odd(table_scales[:].bitcast(I32))
+        nc.gpsimd.memset(table_scales[:].bitcast(I32), 0)
         nc.vector.memset(warm_in[:], 0.0)
         nc.vector.memset(unit[:], 1.0)
         nc.scalar.activation(warm_out[:], warm_in[:], SIGMOID)
@@ -108,8 +108,8 @@ def tile_attend_gnce_w_kernel(tc, xT, w_words, w_scales, y, wt, xm, offs, out):
             for k in range(k0, k1):
                 xm_raw[k] = piece[:, :, (k - k0) * P : (k - k0 + 1) * P]
 
-        nc.sync.dma_start(offsets[:], offs)
         nc.sync.dma_start(table_words[:, :HEAD], words[:, :HEAD])
+        nc.sync.dma_start(offsets[:], offs)
         for f in range(4):
             nc.sync.dma_start(table_scales[f:P:16, :].bitcast(I32), scale_rows[f])
         nc.sync.dma_start(table_words[:, HEAD:], words[:, HEAD:])

@@ -23,6 +23,7 @@ SIGMOID = mybir.ActivationFunctionType.Sigmoid
 P = 128
 PACK = 4
 PASSES = D // (P * PACK)
+QUADRANT = 32
 WINDOWS = 4
 HALF = N // 2
 HALVES = (slice(0, HALF), slice(HALF, N))
@@ -32,13 +33,13 @@ LAST_QUARTERS = (slice(HALF, HALF + QUARTER), slice(HALF + QUARTER, N))
 X_LOADS = ((0, 0, 4), (1, 0, 2), (1, 2, 4))
 VECTOR_CASTS = {(0, 0): (72, 40), (1, 0): (64, 56), (1, 2): (88, 64)}
 LATE_PASS0 = ((1, 2), (1, 3))
-HEAD = 1024
-GPSIMD_ZEROES = 1280
+HEAD = 640
+VECTOR_ZEROES = {1: 704, 2: T}
 XM_LOADS = ((0, 1), (1, 2), (2, 3), (3, 5), (5, 8))
 BANK_OF = {(0, 0): 0, (0, 256): 2, (0, 384): 3, (1, 0): 1, (2, 0): 1, (3, 0): 4, (4, 0): 5, (5, 0): 6, (6, 0): 7, (7, 0): 2}
 KIB = 1024
 SHARED = {
-    "table_words": 0, "y_raw00": 0, "y_raw01": 2 * KIB,
+    "table_words": 64 * KIB, "y_raw00": 62 * KIB + 512, "wt_sb": 64 * KIB + 512, "y_raw01": 69 * KIB,
     "x_raw00": 8 * KIB, "xm_raw0": 8 * KIB,
     "x_grouped00": 17 * KIB, "y_raw10": 16 * KIB, "y_raw11": 18 * KIB,
     "x_grouped01": 21 * KIB, "xm_raw1": 20 * KIB, "staged0_0": 20 * KIB, "xm_raw2": 22 * KIB,
@@ -46,7 +47,8 @@ SHARED = {
     "x_codes01": 28 * KIB, "xm_raw5": 28 * KIB, "staged4": 44 * KIB, "staged6": 43 * KIB, "xm_codes7": 45 * KIB,
     "w_codes1": 34 * KIB, "xm_grouped0": 34 * KIB,
     "g_grouped256": 37 * KIB, "xm_grouped2": 37 * KIB, "xm_grouped3": 37 * KIB, "xm_grouped5": 37 * KIB, "xm_grouped7": 37 * KIB,
-    "staged5": 48 * KIB, "staged7": 48 * KIB,
+    "staged5": 46 * KIB, "staged7": 46 * KIB,
+    "x_raw10": 48 * KIB + 512, "table_scales": 52 * KIB, "w_planes": 52 * KIB + 512, "x_raw12": 53 * KIB + 512,
 }
 
 
@@ -67,34 +69,40 @@ def tile_attend_gnce_w_kernel(tc, xT, w_words, w_scales, y, wt, xm, offs, out):
             nc.vector.memset(view[:, :cut], 0)
             nc.vector.memset(view[:, cut:], 0)
 
+        windows = {}
+
+        def zero_window(k):
+            windows[k] = tile([P, T], F32, "window%d" % k)
+            share = VECTOR_ZEROES.get(k, 0)
+            if share > 0:
+                zero_odd(windows[k][:, :share])
+            if share < T:
+                nc.gpsimd.memset(windows[k][:, share:], 0.0)
+
         offsets = keep.tile([P, N // 16], U16, name="offsets")
         table_words = tile([P, T], I32, "table_words")
         table_scales = tile([P, T], U8, "table_scales")
-        w_plane1 = tile([P, N], U8, "w_plane1")
-        windows = [tile([P, T], F32, "window%d" % k) for k in range(WINDOWS)]
         warm_in = keep.tile([P, 1], F32, name="warm_in")
         warm_out = keep.tile([P, 1], F32, name="warm_out")
         unit = keep.tile([P, 1], F32, name="unit")
-        wt_sb = tile([P, PACK], F32, "wt_sb")
 
         nc.gpsimd.memset(table_scales[:].bitcast(I32), 0)
         nc.vector.memset(warm_in[:], 0.0)
         nc.vector.memset(unit[:], 1.0)
         nc.scalar.activation(warm_out[:], warm_in[:], SIGMOID)
-        zero_odd(w_plane1[96:P, :].bitcast(I32))
-        zero_odd(windows[2][:])
-        zero_odd(windows[3][:, GPSIMD_ZEROES:])
-        nc.gpsimd.memset(windows[0][:], 0.0)
-        nc.gpsimd.memset(windows[1][:], 0.0)
-        nc.gpsimd.memset(windows[3][:, :GPSIMD_ZEROES], 0.0)
+        for k in range(WINDOWS - 1):
+            zero_window(k)
 
         words = w_words[0].rearrange("p t b -> p (t b)").bitcast(I32)
-        scale_rows = w_scales.rearrange("o (q f) t -> f q o t", f=4).bitcast(I32)
         y_rows = y[0].rearrange("(p t) i -> p t i", t=PACK)
         xm_rows = xm[0].rearrange("(p j) d -> p j d", j=PACK)
         x_raw = {}
         y_raw = {}
         xm_raw = {}
+
+        def load_x(o, j0, j1):
+            x_raw[o, j0] = tile([P, j1 - j0, R], F32, "x_raw%d%d" % (o, j0))
+            nc.sync.dma_start(x_raw[o, j0][:], xT[0, 512 * o : 512 * (o + 1), :].rearrange("(p j) r -> p j r", j=PACK)[:, j0:j1, :])
 
         def load_y(h, t0, t1):
             piece = tile([P, t1 - t0, HALF], F32, "y_raw%d%d" % (h, t0 // 2))
@@ -110,21 +118,23 @@ def tile_attend_gnce_w_kernel(tc, xT, w_words, w_scales, y, wt, xm, offs, out):
 
         nc.sync.dma_start(table_words[:, :HEAD], words[:, :HEAD])
         nc.sync.dma_start(offsets[:], offs)
-        for f in range(4):
-            nc.sync.dma_start(table_scales[f:P:16, :].bitcast(I32), scale_rows[f])
+        for o in range(PASSES):
+            nc.sync.dma_start(table_scales[4 * o : P : 8, :].bitcast(I32), w_scales[o].bitcast(I32))
         nc.sync.dma_start(table_words[:, HEAD:], words[:, HEAD:])
-        for o, j0, j1 in X_LOADS:
-            x_raw[o, j0] = tile([P, j1 - j0, R], F32, "x_raw%d%d" % (o, j0))
-            nc.sync.dma_start(x_raw[o, j0][:], xT[0, 512 * o : 512 * (o + 1), :].rearrange("(p j) r -> p j r", j=PACK)[:, j0:j1, :])
-
-        nc.sync.dma_start(wt_sb[:], wt[0].rearrange("(p t) one -> p (t one)", t=PACK))
+        load_x(*X_LOADS[0])
 
         picked_scales = tile([P, N], U8, "picked_scales")
         nc.vector.tensor_copy(picked_scales[:], table_scales[:].indirect(offsets[:]))
-        nc.scalar.dma_start(w_plane1[0 : P - 16, :].bitcast(I32), picked_scales[16:P, :].bitcast(I32))
-        w_plane = (picked_scales, w_plane1)
+        w_planes = tile([P, PASSES * N], U8, "w_planes")
+        for q in range(0, P, QUADRANT):
+            nc.sync.dma_start(w_planes[q : q + 4, :].bitcast(I32), picked_scales[q : q + QUADRANT : 4, :].bitcast(I32))
+        load_x(*X_LOADS[1])
+        load_x(*X_LOADS[2])
+        zero_window(WINDOWS - 1)
         word_pairs = tile([P, N], U32, "word_pairs")
         nc.vector.tensor_copy(word_pairs[:], table_words[:].bitcast(U32).indirect(offsets[:]))
+        wt_sb = tile([P, PACK], F32, "wt_sb")
+        nc.sync.dma_start(wt_sb[:], wt[0].rearrange("(p t) one -> p (t one)", t=PACK))
         load_y(0, 0, 2)
         load_y(0, 2, 4)
         w_codes = [tile([P, 2 * N], U8, "w_codes%d" % o) for o in range(PASSES)]
@@ -141,7 +151,7 @@ def tile_attend_gnce_w_kernel(tc, xT, w_words, w_scales, y, wt, xm, offs, out):
                 lhsT=x_operand[o, t][0].bitcast(E4M3),
                 lhsT_scale=x_operand[o, t][1],
                 rhs=w_codes[o][:, 2 * HALF * h : 2 * HALF * (h + 1)].bitcast(E2M1),
-                rhs_scale=w_plane[o][:, HALVES[h]],
+                rhs_scale=w_planes[:, o * N + h * HALF : o * N + (h + 1) * HALF],
                 start=first,
                 stop=not first,
             )

@@ -32,9 +32,9 @@ QUARTER = N // 4
 LAST_QUARTERS = (slice(HALF, HALF + QUARTER), slice(HALF + QUARTER, N))
 X_LOADS = ((0, 0, 4), (1, 0, 2), (1, 2, 4))
 VECTOR_CASTS = {(0, 0): (72, 40), (1, 0): (64, 56), (1, 2): (88, 64)}
-LATE_PASS0 = ((1, 2), (1, 3))
+LATE_PASS0 = ((1, 1), (1, 2), (1, 3))
 HEAD = 640
-VECTOR_ZEROES = {1: 704, 2: T}
+VECTOR_ZEROES = {1: 1200, 2: T}
 XM_LOADS = ((0, 1), (1, 2), (2, 3), (3, 5), (5, 8))
 BANK_OF = {(0, 0): 0, (0, 256): 2, (0, 384): 3, (1, 0): 1, (2, 0): 1, (3, 0): 4, (4, 0): 5, (5, 0): 6, (6, 0): 7, (7, 0): 2}
 KIB = 1024
@@ -48,7 +48,7 @@ SHARED = {
     "w_codes1": 34 * KIB, "xm_grouped0": 34 * KIB,
     "g_grouped256": 37 * KIB, "xm_grouped2": 37 * KIB, "xm_grouped3": 37 * KIB, "xm_grouped5": 37 * KIB, "xm_grouped7": 37 * KIB,
     "staged5": 46 * KIB, "staged7": 46 * KIB,
-    "x_raw10": 48 * KIB + 512, "table_scales": 52 * KIB, "w_planes": 52 * KIB + 512, "x_raw12": 53 * KIB + 512,
+    "table_scales": 52 * KIB, "w_planes": 52 * KIB + 512, "x_raw12": 53 * KIB + 512,
 }
 
 
@@ -122,13 +122,13 @@ def tile_attend_gnce_w_kernel(tc, xT, w_words, w_scales, y, wt, xm, offs, out):
             nc.sync.dma_start(table_scales[4 * o : P : 8, :].bitcast(I32), w_scales[o].bitcast(I32))
         nc.sync.dma_start(table_words[:, HEAD:], words[:, HEAD:])
         load_x(*X_LOADS[0])
+        load_x(*X_LOADS[1])
 
         picked_scales = tile([P, N], U8, "picked_scales")
         nc.vector.tensor_copy(picked_scales[:], table_scales[:].indirect(offsets[:]))
         w_planes = tile([P, PASSES * N], U8, "w_planes")
         for q in range(0, P, QUADRANT):
             nc.sync.dma_start(w_planes[q : q + 4, :].bitcast(I32), picked_scales[q : q + QUADRANT : 4, :].bitcast(I32))
-        load_x(*X_LOADS[1])
         load_x(*X_LOADS[2])
         zero_window(WINDOWS - 1)
         word_pairs = tile([P, N], U32, "word_pairs")

@@ -29,14 +29,15 @@ HALF = N // 2
 HALVES = (slice(0, HALF), slice(HALF, N))
 WHOLE = slice(0, N)
 QUARTER = N // 4
+FIRST_QUARTERS = (slice(0, QUARTER), slice(QUARTER, HALF))
 LAST_QUARTERS = (slice(HALF, HALF + QUARTER), slice(HALF + QUARTER, N))
 X_LOADS = ((0, 0, 4), (1, 0, 2), (1, 2, 4))
 VECTOR_CASTS = {(0, 0): (72, 40), (1, 0): (64, 56), (1, 2): (88, 64)}
 LATE_PASS0 = ((1, 1), (1, 2), (1, 3))
-HEAD = 640
+HEAD = 1024
 VECTOR_ZEROES = {1: 1200, 2: T}
 XM_LOADS = ((0, 1), (1, 2), (2, 3), (3, 5), (5, 8))
-BANK_OF = {(0, 0): 0, (0, 256): 2, (0, 384): 3, (1, 0): 1, (2, 0): 1, (3, 0): 4, (4, 0): 5, (5, 0): 6, (6, 0): 7, (7, 0): 2}
+BANK_OF = {(0, 0): 0, (0, 256): 2, (0, 384): 3, (1, 0): 1, (1, 256): 6, (2, 0): 6, (3, 0): 4, (4, 0): 5, (5, 0): 1, (6, 0): 7, (7, 0): 2}
 KIB = 1024
 SHARED = {
     "table_words": 64 * KIB, "y_raw00": 62 * KIB + 512, "wt_sb": 64 * KIB + 512, "y_raw01": 69 * KIB,
@@ -264,11 +265,9 @@ def tile_attend_gnce_w_kernel(tc, xT, w_words, w_scales, y, wt, xm, offs, out):
         staged = {}
 
         def multiply(k, cols):
-            if (k, cols.start) in BANK_OF:
-                width = cols.stop - cols.start if k == 0 else N
-                dw[k, cols.start] = psum.tile([P, width], F32, name="dw%d_%d" % (k, cols.start), tag="bank%d" % BANK_OF[k, cols.start])
+            dw[k, cols.start] = psum.tile([P, cols.stop - cols.start], F32, name="dw%d_%d" % (k, cols.start), tag="bank%d" % BANK_OF[k, cols.start])
             nc.tensor.matmul_mx(
-                out=dw[k, cols.start][:] if k == 0 else dw[k, 0][:, cols],
+                out=dw[k, cols.start][:],
                 lhsT=xm_codes[k].bitcast(E4M3),
                 lhsT_scale=xm_plane[k],
                 rhs=g_codes[:, cols].bitcast(E5M2),
@@ -277,10 +276,11 @@ def tile_attend_gnce_w_kernel(tc, xT, w_words, w_scales, y, wt, xm, offs, out):
                 stop=True,
             )
 
-        def stage(copy, k, cols):
+        def stage(copy, k, cols, pieces=None):
             name = "staged%d" % k if cols == WHOLE else "staged%d_%d" % (k, cols.start)
             staged[k, cols.start] = tile([P, cols.stop - cols.start], F32, name)
-            copy(staged[k, cols.start][:], dw[k, cols.start][:])
+            for piece in pieces or (cols,):
+                copy(staged[k, cols.start][:, piece.start - cols.start : piece.stop - cols.start], dw[k, piece.start][:])
 
         def listed(k, cols):
             return windows[k % WINDOWS][:].indirect(offsets[:, cols.start // 16 : cols.stop // 16])
@@ -300,10 +300,12 @@ def tile_attend_gnce_w_kernel(tc, xT, w_words, w_scales, y, wt, xm, offs, out):
         weigh_y(1, True, range(PACK))
         round_xm(nc.scalar.copy, 1, 2)
         gradient(0)
-        group_g(HALVES[0])
         round_xm(nc.vector.tensor_copy, 0, 1)
-        quantize_g(HALVES[0])
+        for cols in FIRST_QUARTERS:
+            group_g(cols)
         quantize_xm(0, 1)
+        for cols in FIRST_QUARTERS:
+            quantize_g(cols)
         multiply(0, HALVES[0])
         stage(nc.scalar.copy, 0, HALVES[0])
         place_scalar(0, HALVES[0])
@@ -316,17 +318,15 @@ def tile_attend_gnce_w_kernel(tc, xT, w_words, w_scales, y, wt, xm, offs, out):
             quantize_g(cols)
         for cols in LAST_QUARTERS:
             multiply(0, cols)
-            multiply(1, cols)
-        staged[0, HALF] = tile([P, HALF], F32, "staged0_256")
-        for cols in LAST_QUARTERS:
-            nc.vector.tensor_copy(staged[0, HALF][:, cols.start - HALF : cols.stop - HALF], dw[0, cols.start][:])
+        multiply(1, HALVES[1])
+        stage(nc.vector.tensor_copy, 0, HALVES[1], LAST_QUARTERS)
         round_xm(nc.vector.tensor_copy, 2, 3)
         quantize_xm(2, 3)
         place_vector(0, HALVES[1])
         store(0)
         multiply(2, WHOLE)
         round_xm(gpsimd_round, 3, 5)
-        stage(nc.scalar.copy, 1, WHOLE)
+        stage(nc.scalar.copy, 1, WHOLE, HALVES)
         place_scalar(1, WHOLE)
         store(1)
         stage(nc.vector.tensor_copy, 2, WHOLE)

@@ -40,7 +40,7 @@ XM_LOADS = ((0, 1), (1, 2), (2, 3), (3, 5), (5, 8))
 BANK_OF = {(0, 0): 0, (0, 256): 2, (0, 384): 3, (1, 0): 1, (1, 256): 6, (2, 0): 6, (3, 0): 4, (4, 0): 5, (5, 0): 1, (6, 0): 7, (7, 0): 2}
 KIB = 1024
 SHARED = {
-    "table_words": 64 * KIB, "y_raw00": 62 * KIB + 512, "wt_sb": 64 * KIB + 512, "y_raw01": 69 * KIB,
+    "table_words": 64 * KIB, "y_raw00": 61 * KIB + 512, "wt_sb": 64 * KIB + 512, "y_raw01": 69 * KIB,
     "x_raw00": 8 * KIB, "xm_raw0": 8 * KIB,
     "x_grouped00": 17 * KIB, "y_raw10": 16 * KIB, "y_raw11": 18 * KIB,
     "x_grouped01": 21 * KIB, "xm_raw1": 20 * KIB, "staged0_0": 20 * KIB, "xm_raw2": 22 * KIB,
@@ -136,8 +136,8 @@ def tile_attend_gnce_w_kernel(tc, xT, w_words, w_scales, y, wt, xm, offs, out):
         nc.vector.tensor_copy(word_pairs[:], table_words[:].bitcast(U32).indirect(offsets[:]))
         wt_sb = tile([P, PACK], F32, "wt_sb")
         nc.sync.dma_start(wt_sb[:], wt[0].rearrange("(p t) one -> p (t one)", t=PACK))
-        load_y(0, 0, 2)
-        load_y(0, 2, 4)
+        load_y(0, 0, 3)
+        load_y(0, 3, 4)
         w_codes = [tile([P, 2 * N], U8, "w_codes%d" % o) for o in range(PASSES)]
         for o in range(PASSES):
             nc.vector.tensor_copy(w_codes[o][:].bitcast(U16), word_pairs[:].bitcast(U16)[:, o : PASSES * N : PASSES])

@@ -32,10 +32,10 @@ QUARTER = N // 4
 FIRST_QUARTERS = (slice(0, QUARTER), slice(QUARTER, HALF))
 LAST_QUARTERS = (slice(HALF, HALF + QUARTER), slice(HALF + QUARTER, N))
 X_LOADS = ((0, 0, 4), (1, 0, 2), (1, 2, 4))
-VECTOR_CASTS = {(0, 0): (72, 40), (1, 0): (64, 56), (1, 2): (88, 64)}
+VECTOR_CASTS = {(0, 0): (104, 72), (1, 0): (88, 72), (1, 2): (88, 64)}
 LATE_PASS0 = ((1, 1), (1, 2), (1, 3))
 HEAD = 1024
-VECTOR_ZEROES = {1: 1200, 2: T}
+VECTOR_ZEROES = {1: 752, 2: T}
 XM_LOADS = ((0, 1), (1, 2), (2, 3), (3, 5), (5, 8))
 BANK_OF = {(0, 0): 0, (0, 256): 2, (0, 384): 3, (1, 0): 1, (1, 256): 6, (2, 0): 6, (3, 0): 4, (4, 0): 5, (5, 0): 1, (6, 0): 7, (7, 0): 2}
 KIB = 1024
@@ -216,9 +216,12 @@ def tile_attend_gnce_w_kernel(tc, xT, w_words, w_scales, y, wt, xm, offs, out):
 
         def gradient(h):
             g_rows[h] = tile([P, PACK, HALF], BF16, "g_rows%d" % h)
-            for t in range(PACK):
+            steps = [(t, slice(0, HALF)) for t in range(PACK)]
+            if h == 1:
+                steps[PACK - 1 :] = [(PACK - 1, cols) for cols in FIRST_QUARTERS]
+            for t, cols in steps:
                 nc.vector.scalar_tensor_tensor(
-                    g_rows[h][:, t, :], prob[h][:, t, :], wt_sb[:, t : t + 1], wy[h, t][:], MULT, SUBTRACT
+                    g_rows[h][:, t, cols], prob[h][:, t, cols], wt_sb[:, t : t + 1], wy[h, t][:, cols], MULT, SUBTRACT
                 )
 
         def group_g(cols):

from contextlib import ExitStack

import concourse.mybir as mybir

N, T, D, R = 512, 2048, 1024, 512
FLOPS = 2 * 2 * N * D * R

F32 = mybir.dt.float32
BF16 = mybir.dt.bfloat16
I32 = mybir.dt.int32
U32 = mybir.dt.uint32
U16 = mybir.dt.uint16
U8 = mybir.dt.uint8
E4M3 = mybir.dt.float8_e4m3fn_x4
E5M2 = mybir.dt.float8_e5m2_x4
E2M1 = mybir.dt.float4_e2m1fn_x4
MULT = mybir.AluOpType.mult
ADD = mybir.AluOpType.add
SUBTRACT = mybir.AluOpType.subtract
COPY = mybir.ActivationFunctionType.Copy
SIGMOID = mybir.ActivationFunctionType.Sigmoid

P = 128
PACK = 4
PASSES = D // (P * PACK)
QUADRANT = 32
WINDOWS = 4
HALF = N // 2
HALVES = (slice(0, HALF), slice(HALF, N))
WHOLE = slice(0, N)
QUARTER = N // 4
FIRST_QUARTERS = (slice(0, QUARTER), slice(QUARTER, HALF))
LAST_QUARTERS = (slice(HALF, HALF + QUARTER), slice(HALF + QUARTER, N))
X_LOADS = ((0, 0, 4), (1, 0, 2), (1, 2, 4))
VECTOR_CASTS = {(0, 0): (104, 72), (1, 0): (88, 72), (1, 2): (88, 64)}
LATE_PASS0 = ((1, 1), (1, 2), (1, 3))
HEAD = 1024
VECTOR_ZEROES = {1: 752, 2: T}
XM_LOADS = ((0, 1), (1, 2), (2, 3), (3, 5), (5, 8))
BANK_OF = {(0, 0): 0, (0, 256): 2, (0, 384): 3, (1, 0): 1, (1, 256): 6, (2, 0): 6, (3, 0): 4, (4, 0): 5, (5, 0): 1, (6, 0): 7, (7, 0): 2}
KIB = 1024
SHARED = {
    "table_words": 64 * KIB, "y_raw00": 61 * KIB + 512, "wt_sb": 64 * KIB + 512, "y_raw01": 69 * KIB,
    "x_raw00": 8 * KIB, "xm_raw0": 8 * KIB,
    "x_grouped00": 17 * KIB, "y_raw10": 16 * KIB, "y_raw11": 18 * KIB,
    "x_grouped01": 21 * KIB, "xm_raw1": 20 * KIB, "staged0_0": 20 * KIB, "xm_raw2": 22 * KIB,
    "x_codes00": 24 * KIB, "xm_raw3": 24 * KIB,
    "x_codes01": 28 * KIB, "xm_raw5": 28 * KIB, "staged4": 44 * KIB, "staged6": 43 * KIB, "xm_codes7": 45 * KIB,
    "w_codes1": 34 * KIB, "xm_grouped0": 34 * KIB,
    "g_grouped256": 37 * KIB, "xm_grouped2": 37 * KIB, "xm_grouped3": 37 * KIB, "xm_grouped5": 37 * KIB, "xm_grouped7": 37 * KIB,
    "staged5": 46 * KIB, "staged7": 46 * KIB,
    "table_scales": 52 * KIB, "w_planes": 52 * KIB + 512, "x_raw12": 53 * KIB + 512,
}


def tile_attend_gnce_w_kernel(tc, xT, w_words, w_scales, y, wt, xm, offs, out):
    nc = tc.nc
    with ExitStack() as ctx:
        keep = ctx.enter_context(tc.tile_pool(name="keep", bufs=1))
        shared = ctx.enter_context(tc.tile_pool(name="shared", bufs=1))
        psum = ctx.enter_context(tc.psum_pool(name="psum", bufs=1))

        def tile(shape, dtype, name):
            if name in SHARED:
                return shared.tile(shape, dtype, name=name, align_bytes=64, offset=SHARED[name])
            return keep.tile(shape, dtype, name=name, align_bytes=64)

        def zero_odd(view):
            cut = view.shape[1] // 2 + 1
            nc.vector.memset(view[:, :cut], 0)
            nc.vector.memset(view[:, cut:], 0)

        windows = {}

        def zero_window(k):
            windows[k] = tile([P, T], F32, "window%d" % k)
            share = VECTOR_ZEROES.get(k, 0)
            if share > 0:
                zero_odd(windows[k][:, :share])
            if share < T:
                nc.gpsimd.memset(windows[k][:, share:], 0.0)

        offsets = keep.tile([P, N // 16], U16, name="offsets")
        table_words = tile([P, T], I32, "table_words")
        table_scales = tile([P, T], U8, "table_scales")
        warm_in = keep.tile([P, 1], F32, name="warm_in")
        warm_out = keep.tile([P, 1], F32, name="warm_out")
        unit = keep.tile([P, 1], F32, name="unit")

        nc.gpsimd.memset(table_scales[:].bitcast(I32), 0)
        nc.vector.memset(warm_in[:], 0.0)
        nc.vector.memset(unit[:], 1.0)
        nc.scalar.activation(warm_out[:], warm_in[:], SIGMOID)
        for k in range(WINDOWS - 1):
            zero_window(k)

        words = w_words[0].rearrange("p t b -> p (t b)").bitcast(I32)
        y_rows = y[0].rearrange("(p t) i -> p t i", t=PACK)
        xm_rows = xm[0].rearrange("(p j) d -> p j d", j=PACK)
        x_raw = {}
        y_raw = {}
        xm_raw = {}

        def load_x(o, j0, j1):
            x_raw[o, j0] = tile([P, j1 - j0, R], F32, "x_raw%d%d" % (o, j0))
            nc.sync.dma_start(x_raw[o, j0][:], xT[0, 512 * o : 512 * (o + 1), :].rearrange("(p j) r -> p j r", j=PACK)[:, j0:j1, :])

        def load_y(h, t0, t1):
            piece = tile([P, t1 - t0, HALF], F32, "y_raw%d%d" % (h, t0 // 2))
            nc.sync.dma_start(piece[:], y_rows[:, t0:t1, HALVES[h]])
            for t in range(t0, t1):
                y_raw[h, t] = piece[:, t - t0, :]

        def load_xm(k0, k1):
            piece = tile([P, PACK, (k1 - k0) * P], F32, "xm_raw%d" % k0)
            nc.sync.dma_start(piece[:], xm_rows[:, :, k0 * P : k1 * P])
            for k in range(k0, k1):
                xm_raw[k] = piece[:, :, (k - k0) * P : (k - k0 + 1) * P]

        nc.sync.dma_start(table_words[:, :HEAD], words[:, :HEAD])
        nc.sync.dma_start(offsets[:], offs)
        for o in range(PASSES):
            nc.sync.dma_start(table_scales[4 * o : P : 8, :].bitcast(I32), w_scales[o].bitcast(I32))
        nc.sync.dma_start(table_words[:, HEAD:], words[:, HEAD:])
        load_x(*X_LOADS[0])
        load_x(*X_LOADS[1])

        picked_scales = tile([P, N], U8, "picked_scales")
        nc.vector.tensor_copy(picked_scales[:], table_scales[:].indirect(offsets[:]))
        w_planes = tile([P, PASSES * N], U8, "w_planes")
        for q in range(0, P, QUADRANT):
            nc.sync.dma_start(w_planes[q : q + 4, :].bitcast(I32), picked_scales[q : q + QUADRANT : 4, :].bitcast(I32))
        load_x(*X_LOADS[2])
        zero_window(WINDOWS - 1)
        word_pairs = tile([P, N], U32, "word_pairs")
        nc.vector.tensor_copy(word_pairs[:], table_words[:].bitcast(U32).indirect(offsets[:]))
        wt_sb = tile([P, PACK], F32, "wt_sb")
        nc.sync.dma_start(wt_sb[:], wt[0].rearrange("(p t) one -> p (t one)", t=PACK))
        load_y(0, 0, 3)
        load_y(0, 3, 4)
        w_codes = [tile([P, 2 * N], U8, "w_codes%d" % o) for o in range(PASSES)]
        for o in range(PASSES):
            nc.vector.tensor_copy(w_codes[o][:].bitcast(U16), word_pairs[:].bitcast(U16)[:, o : PASSES * N : PASSES])

        logits = {(h, t): psum.tile([P, HALF], F32, name="logits%d%d" % (h, t), tag="bank%d" % (PACK * h + t)) for h in range(2) for t in range(PACK)}

        x_operand = {}

        def score_pass(o, h, t, first):
            nc.tensor.matmul_mx(
                out=logits[h, t][:],
                lhsT=x_operand[o, t][0].bitcast(E4M3),
                lhsT_scale=x_operand[o, t][1],
                rhs=w_codes[o][:, 2 * HALF * h : 2 * HALF * (h + 1)].bitcast(E2M1),
                rhs_scale=w_planes[:, o * N + h * HALF : o * N + (h + 1) * HALF],
                start=first,
                stop=not first,
            )

        def scores(o):
            x_grouped = [tile([P, 2, P, PACK], BF16, "x_grouped%d%d" % (o, pair)) for pair in range(2)]
            x_codes = [tile([P, 2, P], U32, "x_codes%d%d" % (o, pair)) for pair in range(2)]
            x_plane = [tile([P, 2, P], U8, "x_plane%d%d" % (o, pair)) for pair in range(2)]
            for j0, j1 in [(j0, j1) for pass_of, j0, j1 in X_LOADS if pass_of == o]:
                for pair in range(2):
                    share = VECTOR_CASTS[o, j0][pair]
                    for copy, m0, m1 in ((nc.vector.tensor_copy, 0, share), (nc.scalar.copy, share, P)):
                        if m0 < m1:
                            copy(
                                x_grouped[pair][:].rearrange("p t m j -> p m j t")[:, m0:m1, j0:j1],
                                x_raw[o, j0][:].rearrange("p j (m t) -> p m j t", t=PACK)[:, m0:m1, :, 2 * pair : 2 * pair + 2],
                            )
            for pair, u0, u1 in ((0, 0, 1), (0, 1, 2), (1, 0, 2)):
                nc.vector.quantize_mx(
                    out=x_codes[pair][:, u0:u1, :].rearrange("p t m -> p (t m)").bitcast(E4M3),
                    scales=x_plane[pair][:, u0:u1, :].rearrange("p t m -> p (t m)"),
                    in_=x_grouped[pair][:, u0:u1].rearrange("p t m j -> p (t m j)"),
                )
            for t in range(PACK):
                x_operand[o, t] = (x_codes[t // 2][:, t % 2, :], x_plane[t // 2][:, t % 2, :])
            for h in range(2):
                for t in range(PACK):
                    if (h, t) not in LATE_PASS0:
                        score_pass(o, h, t, o == 0)
                    elif o == 1:
                        score_pass(1, h, t, True)
                        score_pass(0, h, t, False)

        scores(0)
        load_xm(*XM_LOADS[0])
        load_y(1, 0, 2)
        load_y(1, 2, 4)
        for k0, k1 in XM_LOADS[1:]:
            load_xm(k0, k1)
        scores(1)

        wy = {}
        prob = {}
        g_rows = {}
        g_grouped = {}
        g_codes = tile([P, N], U32, "g_codes")
        g_plane = tile([P, N], U8, "g_plane")

        def weigh_y(h, on_scalar, places):
            for t in places:
                wy[h, t] = tile([P, HALF], F32, "wy%d%d" % (h, t))
                if on_scalar:
                    nc.scalar.activation(wy[h, t][:], y_raw[h, t], COPY, scale=wt_sb[:, t : t + 1])
                else:
                    nc.vector.tensor_scalar(wy[h, t][:], y_raw[h, t], wt_sb[:, t : t + 1], None, MULT)

        def sigmoid(h):
            prob[h] = tile([P, PACK, HALF], F32, "prob%d" % h)
            for t in range(PACK):
                nc.scalar.activation(prob[h][:, t, :], logits[h, t][:], SIGMOID)

        def gradient(h):
            g_rows[h] = tile([P, PACK, HALF], BF16, "g_rows%d" % h)
            steps = [(t, slice(0, HALF)) for t in range(PACK)]
            if h == 1:
                steps[PACK - 1 :] = [(PACK - 1, cols) for cols in FIRST_QUARTERS]
            for t, cols in steps:
                nc.vector.scalar_tensor_tensor(
                    g_rows[h][:, t, cols], prob[h][:, t, cols], wt_sb[:, t : t + 1], wy[h, t][:, cols], MULT, SUBTRACT
                )

        def group_g(cols):
            h, c0 = divmod(cols.start, HALF)
            width = cols.stop - cols.start
            g_grouped[cols.start] = tile([P, width, PACK], BF16, "g_grouped%d" % cols.start)
            nc.vector.tensor_copy(
                g_grouped[cols.start][:].rearrange("p (c i) t -> p c t i", i=4),
                g_rows[h][:, :, c0 : c0 + width].rearrange("p t (c i) -> p c t i", i=4),
            )

        def quantize_g(cols):
            nc.vector.quantize_mx(
                out=g_codes[:, cols].bitcast(E5M2),
                scales=g_plane[:, cols],
                in_=g_grouped[cols.start][:].rearrange("p i t -> p (i t)"),
            )

        xm_grouped = {}
        xm_codes = {}
        xm_plane = {}

        def gpsimd_round(dst, src):
            nc.gpsimd.tensor_scalar(dst.rearrange("p c j i -> p c i j"), src.rearrange("p c j i -> p c i j"), 1.0, 0.0, MULT, ADD)

        def round_xm(copy, k0, k1):
            grouped = tile([P, (k1 - k0) * P, PACK], BF16, "xm_grouped%d" % k0)
            xm_grouped[k0, k1] = grouped[:].rearrange("p d j -> p (d j)")
            for k in range(k0, k1):
                copy(
                    grouped[:, (k - k0) * P : (k - k0 + 1) * P, :].rearrange("p (c i) j -> p c j i", i=4),
                    xm_raw[k].rearrange("p j (c i) -> p c j i", i=4),
                )

        def quantize_xm(k0, k1):
            codes = tile([P, (k1 - k0) * P], U32, "xm_codes%d" % k0)
            plane = tile([P, (k1 - k0) * P], U8, "xm_plane%d" % k0)
            nc.vector.quantize_mx(out=codes[:].bitcast(E4M3), scales=plane[:], in_=xm_grouped[k0, k1])
            for k in range(k0, k1):
                xm_codes[k] = codes[:, (k - k0) * P : (k - k0 + 1) * P]
                xm_plane[k] = plane[:, (k - k0) * P : (k - k0 + 1) * P]

        dw = {}
        staged = {}

        def multiply(k, cols):
            dw[k, cols.start] = psum.tile([P, cols.stop - cols.start], F32, name="dw%d_%d" % (k, cols.start), tag="bank%d" % BANK_OF[k, cols.start])
            nc.tensor.matmul_mx(
                out=dw[k, cols.start][:],
                lhsT=xm_codes[k].bitcast(E4M3),
                lhsT_scale=xm_plane[k],
                rhs=g_codes[:, cols].bitcast(E5M2),
                rhs_scale=g_plane[:, cols],
                start=True,
                stop=True,
            )

        def stage(copy, k, cols, pieces=None):
            name = "staged%d" % k if cols == WHOLE else "staged%d_%d" % (k, cols.start)
            staged[k, cols.start] = tile([P, cols.stop - cols.start], F32, name)
            for piece in pieces or (cols,):
                copy(staged[k, cols.start][:, piece.start - cols.start : piece.stop - cols.start], dw[k, piece.start][:])

        def listed(k, cols):
            return windows[k % WINDOWS][:].indirect(offsets[:, cols.start // 16 : cols.stop // 16])

        def place_vector(k, cols):
            nc.vector.tensor_copy(listed(k, cols), staged[k, cols.start][:])

        def place_scalar(k, cols):
            nc.scalar.activation(listed(k, cols), staged[k, cols.start][:], COPY, scale=unit[:])

        def store(k):
            nc.sync.dma_start(out[k * P : (k + 1) * P, :], windows[k % WINDOWS][:])

        weigh_y(0, False, range(PACK))
        sigmoid(0)
        sigmoid(1)
        weigh_y(1, True, range(PACK))
        round_xm(nc.scalar.copy, 1, 2)
        gradient(0)
        round_xm(nc.vector.tensor_copy, 0, 1)
        for cols in FIRST_QUARTERS:
            group_g(cols)
        quantize_xm(0, 1)
        for cols in FIRST_QUARTERS:
            quantize_g(cols)
        multiply(0, HALVES[0])
        stage(nc.scalar.copy, 0, HALVES[0])
        place_scalar(0, HALVES[0])
        gradient(1)
        quantize_xm(1, 2)
        multiply(1, HALVES[0])
        for cols in LAST_QUARTERS:
            group_g(cols)
        for cols in LAST_QUARTERS:
            quantize_g(cols)
        for cols in LAST_QUARTERS:
            multiply(0, cols)
        multiply(1, HALVES[1])
        stage(nc.vector.tensor_copy, 0, HALVES[1], LAST_QUARTERS)
        round_xm(nc.vector.tensor_copy, 2, 3)
        quantize_xm(2, 3)
        place_vector(0, HALVES[1])
        store(0)
        multiply(2, WHOLE)
        round_xm(gpsimd_round, 3, 5)
        stage(nc.scalar.copy, 1, WHOLE, HALVES)
        place_scalar(1, WHOLE)
        store(1)
        stage(nc.vector.tensor_copy, 2, WHOLE)
        quantize_xm(3, 5)
        place_vector(2, WHOLE)
        store(2)
        multiply(3, WHOLE)
        multiply(4, WHOLE)
        round_xm(gpsimd_round, 5, 7)
        stage(nc.scalar.copy, 3, WHOLE)
        place_scalar(3, WHOLE)
        store(3)
        stage(nc.vector.tensor_copy, 4, WHOLE)
        quantize_xm(5, 7)
        round_xm(gpsimd_round, 7, 8)
        place_vector(4, WHOLE)
        store(4)
        for k in range(5, 7):
            multiply(k, WHOLE)
        stage(nc.scalar.copy, 5, WHOLE)
        place_scalar(5, WHOLE)
        store(5)
        stage(nc.vector.tensor_copy, 6, WHOLE)
        quantize_xm(7, 8)
        multiply(7, WHOLE)
        place_vector(6, WHOLE)
        store(6)
        stage(nc.scalar.copy, 7, WHOLE)
        place_scalar(7, WHOLE)
        store(7)
